import numpy as np
import ml_dtypes


def mxq(x, axis, fmt="e4m3"):
    dtype, down = {"e4m3": (ml_dtypes.float8_e4m3fn, 7), "e5m2": (ml_dtypes.float8_e5m2, 14)}[fmt]
    v = np.moveaxis(np.asarray(x, np.float32).astype(ml_dtypes.bfloat16).astype(np.float64), axis, -1)
    blocks = v.reshape(v.shape[:-1] + (-1, 32))
    amax = np.abs(blocks).max(-1, keepdims=True)
    byte = np.maximum(np.where(amax > 0, np.frexp(amax)[1] - 1 + 127, 0) - down, 1)
    scale = np.exp2(byte - 127.0)
    codes = (blocks / scale).astype(np.float32).astype(dtype).astype(np.float64)
    return np.moveaxis((codes * scale).reshape(v.shape), -1, axis)


WIDE = False


def mx_kscale(k):
    if not WIDE:
        return np.ones(k)
    levels = np.array([24, -24, 12, -12, 0])
    if k % 512:
        return np.exp2(np.random.permutation(np.resize(levels, k // 32))).repeat(32)
    a = np.empty((k // 512, 16))
    for p in range(k // 512):
        a[p, :8] = np.random.permutation(np.resize(levels, 8))
        for g in range(8):
            far = levels[np.abs(levels - a[p, g]) >= 10]
            a[p, g + 8] = far[np.random.randint(len(far))]
    return np.exp2(a.ravel()).repeat(32)


def f64(x):
    return np.asarray(x).astype(np.float64)


def striped(idx):
    return np.tile(idx.reshape(-1, 16).T, (8, 1)).astype(np.uint16)


def unstriped(offs):
    return offs[:16].T.reshape(-1).astype(np.int64)


E2M1 = np.array([0.0, 0.5, 1.0, 1.5, 2.0, 3.0, 4.0, 6.0, -0.0, -0.5, -1.0, -1.5, -2.0, -3.0, -4.0, -6.0])


def pack_weight(w, fmt):
    k, n = w.shape
    w = f64(np.asarray(w, np.float32).astype(ml_dtypes.bfloat16)).reshape(k // 32, 32, n)
    amax = np.abs(w).max(1)
    if fmt == "e4m3":
        byte = np.frexp(amax)[1] - 1 + 127 - 7
    else:
        mant, ex = np.frexp(amax / 6.0)
        byte = np.where(mant > 0.5, ex, ex - 1) + 127
    byte = np.clip(np.where(amax > 0, byte, 1), 1, 254)
    scaled = (w * np.exp2(127.0 - byte)[:, None, :]).reshape(k, n).astype(np.float32)
    by_word = np.ascontiguousarray(scaled.reshape(k // 512, 128, 4, n).transpose(0, 1, 3, 2))
    if fmt == "e4m3":
        words = by_word.astype(ml_dtypes.float8_e4m3fn).view(np.uint8)
    else:
        c = by_word.astype(ml_dtypes.float4_e2m1fn).view(np.uint8) & 0xF
        words = (c[..., 0::2] | (c[..., 1::2] << 4)).reshape(k // 512, 128, 2 * n)
    return np.ascontiguousarray(words), np.ascontiguousarray(byte.astype(np.uint8).reshape(k // 512, 16, n))


def unpack_weight(words, scales, fmt):
    g, _, n = scales.shape
    words = np.ascontiguousarray(words).reshape(g, 128, n, -1)
    if fmt == "e4m3":
        vals = words.view(ml_dtypes.float8_e4m3fn).astype(np.float64)
    else:
        nib = np.empty((g, 128, n, 4), np.uint8)
        nib[..., 0::2] = words & 0xF
        nib[..., 1::2] = words >> 4
        vals = E2M1[nib]
    vals = vals * np.repeat(np.exp2(scales.astype(np.float64) - 127.0), 8, axis=1)[..., None]
    return vals.transpose(0, 1, 3, 2).reshape(g * 512, n)


def pack_table4(v):
    words, scales = pack_weight(v, "e2m1")
    g, t = words.shape[0] // 2, v.shape[1]
    return np.ascontiguousarray(words.reshape(g, 2, 128, t, 2).transpose(0, 2, 3, 1, 4).reshape(g, 128, t, 4)), scales


def unpack_table4(words, scales):
    g, _, t, _ = words.shape
    return unpack_weight(words.reshape(g, 128, t, 2, 2).transpose(0, 3, 1, 2, 4).reshape(2 * g, 128, 2 * t), scales, "e2m1")


K, R, M, N, T, J = 1024, 1024, 256, 512, 4096, 2048


def setup_inputs():
    n = np.random.standard_normal
    s = mx_kscale(K)[:, None]
    s2 = mx_kscale(K)[:, None]
    u = mx_kscale(R)[:, None]
    wv = n((K, N)) / np.sqrt(K) / s2
    p_tab = pack_table4(n((K, T)) * s2)
    p_wq = pack_weight(n((K, R)) / np.sqrt(K) / s / u.T, "e2m1")
    p_wk = pack_weight(n((K, R)) / np.sqrt(K) / s2 * u.T, "e2m1")
    p_wv4 = pack_weight(wv[512:], "e2m1")
    return {
        "tab_words": p_tab[0],
        "tab_scales": p_tab[1],
        "x": (n((K, M)) * s).astype(np.float32),
        "wq_words": p_wq[0],
        "wq_scales": p_wq[1],
        "wk_words": p_wk[0],
        "wk_scales": p_wk[1],
        "wv8": (wv[:512]).astype(np.float32),
        "wv4_words": p_wv4[0],
        "wv4_scales": p_wv4[1],
        "offs": striped(np.random.permutation(T)[:J]),
    }


def reference(tab_words, tab_scales, x, wq_words, wq_scales, wk_words, wk_scales, wv8, wv4_words, wv4_scales, offs):
    idx = unstriped(offs)
    tab_ = unpack_table4(tab_words, tab_scales)[:, idx]
    x_ = mxq(f64(x), 0, "e4m3")
    wq_ = unpack_weight(wq_words, wq_scales, "e2m1")
    wk_ = unpack_weight(wk_words, wk_scales, "e2m1")
    qr = wq_.T @ x_
    kr = wk_.T @ tab_
    qr_ = mxq(qr, 0, "e4m3")
    kr_ = mxq(kr, 0, "e4m3")
    sc = qr_.T @ kr_
    wv8_ = mxq(f64(wv8), 0, "e4m3")
    wv4_ = unpack_weight(wv4_words, wv4_scales, "e2m1")
    vv = wv8_.T @ tab_[:512] + wv4_.T @ tab_[512:]
    return np.exp(sc * 0.015625), vv

@@ -1,0 +1,244 @@
+from contextlib import ExitStack
+
+import concourse.mybir as mybir
+
+K, R, M, N, T, J = 1024, 1024, 256, 512, 4096, 2048
+FLOPS = 2 * (K * R * M + K * R * J + R * M * J + K * N * J)
+
+F32 = mybir.dt.float32
+BF16 = mybir.dt.bfloat16
+I32 = mybir.dt.int32
+U32 = mybir.dt.uint32
+U16 = mybir.dt.uint16
+U8 = mybir.dt.uint8
+FP8X4 = mybir.dt.float8_e4m3fn_x4
+FP4X4 = mybir.dt.float4_e2m1fn_x4
+EXP = mybir.ActivationFunctionType.Exp
+
+P = 128
+CH = 512
+NCH = J // CH
+SUB = CH // P
+SCORE_SCALE = 0.015625
+
+
+def tile_list_kvt_qf_exp_kernel(
+    tc, tab_words, tab_scales, x, wq_words, wq_scales, wk_words, wk_scales, wv8, wv4_words, wv4_scales, offs, out_0, out_1
+):
+    nc = tc.nc
+    with ExitStack() as ctx:
+        keep = ctx.enter_context(tc.tile_pool(name="keep", bufs=1))
+        ring = ctx.enter_context(tc.tile_pool(name="ring", bufs=2))
+        outs = ctx.enter_context(tc.tile_pool(name="outs", bufs=6))
+        psum = ctx.enter_context(tc.psum_pool(name="psum", bufs=8))
+
+        offsets = keep.tile([P, J // 16], U16, name="offsets")
+        nc.sync.dma_start(offsets[:], offs)
+        tscale = keep.tile([P, T], U8, name="tscale", align_bytes=64)
+        nc.sync.dma_start(out=tscale[96:128, :].bitcast(I32), in_=tab_scales.rearrange("a q t -> q a t").bitcast(I32))
+        table = keep.tile([P, T], U32, name="table", align_bytes=64)
+        nc.sync.dma_start(out=table[:].bitcast(I32), in_=tab_words[0].rearrange("p t b -> p (t b)").bitcast(I32))
+
+        def load_weight_words(words, name):
+            raw = keep.tile([P, 1024], I32, name=name, tag="raw_words", align_bytes=64)
+            nc.sync.dma_start(out=raw[:].rearrange("p (a n) -> p a n", a=2), in_=words.rearrange("a p n -> p a n").bitcast(I32))
+            return raw
+
+        def deal(raw, name, per_run):
+            dealt = keep.tile([P, 256 * per_run], I32, name=name, align_bytes=64)
+            nc.vector.tensor_copy(
+                out=dealt[:].rearrange("p (h t g w) -> p h t g w", h=4, t=4, g=16),
+                in_=raw.rearrange("p (h g t w) -> p h t g w", h=4, t=4, g=16),
+            )
+            return dealt
+
+        rows = slice(96, 128)
+
+        def load_scale_rows(scales, name):
+            raw = keep.tile([P, R], U8, name=name, align_bytes=64)
+            nc.scalar.dma_start(out=raw[rows, :].bitcast(I32), in_=scales.rearrange("a q r -> q a r").bitcast(I32))
+            return raw
+
+        def deal_scales(raw, dst):
+            nc.vector.tensor_copy(
+                out=dst.bitcast(I32).rearrange("p (b t g w) -> p b t g w", b=2, t=4, g=16),
+                in_=raw[rows, :].bitcast(I32).rearrange("p (b g t w) -> p b t g w", b=2, t=4, g=16),
+            )
+
+        def gather_scales(c0, c1, dst):
+            picked = keep.tile([P, (c1 - c0) * CH], U8, name="picked_scales%d" % c0, align_bytes=64)
+            for c in range(c0, c1):
+                nc.vector.tensor_copy(
+                    out=picked[:, (c - c0) * CH : (c - c0 + 1) * CH],
+                    in_=tscale[:].indirect(offsets[:, c * 32 : (c + 1) * 32]),
+                )
+            nc.vector.tensor_copy(out=dst.bitcast(I32), in_=picked[rows, :].bitcast(I32))
+
+        def place(staged, planes):
+            for q in range(4):
+                nc.scalar.dma_start(
+                    out=planes[32 * q : 32 * q + 4].bitcast(I32), in_=staged[96 + 8 * q : 104 + 8 * q, :].bitcast(I32)
+                )
+
+        def zeroed_planes(width, name):
+            planes = keep.tile([P, 2, width], U8, name=name, align_bytes=64)
+            nc.vector.memset(planes[:].rearrange("p a n -> p (a n)").bitcast(I32), 0)
+            return planes
+
+        wk_raw = load_weight_words(wk_words, "wk_raw")
+        wk_sraw = load_scale_rows(wk_scales, "wk_sraw")
+        wq_sraw = load_scale_rows(wq_scales, "wq_sraw")
+        first_w, rest_w = CH + R, J - CH + R + N // 2
+        staged_first = keep.tile([P, first_w], U8, name="staged_first", tag="staged_first", align_bytes=64)
+        staged_rest = keep.tile([P, rest_w], U8, name="staged_rest", align_bytes=64)
+        nc.scalar.dma_start(
+            out=staged_rest[rows, J - CH + R :].bitcast(I32),
+            in_=wv4_scales[0].rearrange("q (h n) -> (q h) n", h=2).bitcast(I32),
+        )
+        wv8_raw = keep.tile([P, 4, N], F32, name="wv8_raw", tag="raw_float", align_bytes=64)
+        nc.sync.dma_start(out=wv8_raw[:], in_=wv8.rearrange("(p j) n -> p j n", j=4))
+        nc.vector.memset(tscale[0:96, :].bitcast(I32), 0)
+        planes_first = zeroed_planes(first_w, "planes_first")
+        planes_rest = zeroed_planes(rest_w, "planes_rest")
+
+        def gather_words(c):
+            picked = ring.tile([P, CH], U32, name="picked")
+            nc.vector.tensor_copy(out=picked[:], in_=table[:].indirect(offsets[:, c * 32 : (c + 1) * 32]))
+            parted = keep.tile([P, 2, CH], U16, name="parted%d" % c, align_bytes=64)
+            nc.vector.tensor_copy(out=parted[:], in_=picked[:].bitcast(U16).rearrange("p (j d) -> p d j", d=2))
+            return parted
+
+        deal_scales(wk_sraw, staged_first[rows, CH:])
+        gather_scales(0, 1, staged_first[rows, :CH])
+        place(staged_first, planes_first)
+        cols = [gather_words(0)]
+        wk = deal(wk_raw[:], "wk", 4)
+        deal_scales(wq_sraw, staged_rest[rows, J - CH : J - CH + R])
+        gather_scales(1, NCH, staged_rest[rows, : J - CH])
+        place(staged_rest, planes_rest)
+        wk_s = planes_first[:, :, CH:]
+        wq_s = planes_rest[:, :, J - CH : J - CH + R]
+        wv4_s = planes_rest[:, :, J - CH + R :]
+        col_scales = [[planes_first[:, a, :CH] for a in range(2)]] + [
+            [planes_rest[:, a, (c - 1) * CH : c * CH] for a in range(2)] for c in range(1, NCH)
+        ]
+
+        wq_raw = load_weight_words(wq_words, "wq_raw")
+        wv4 = keep.tile([P, 2 * N], U8, name="wv4", tag="staged_first", align_bytes=64)
+        nc.sync.dma_start(out=wv4[:].bitcast(I32), in_=wv4_words[0].bitcast(I32))
+
+        warm = keep.tile([P, 2], F32, name="warm")
+        nc.vector.memset(warm[:, 0:1], 0.0)
+        nc.scalar.activation(out=warm[:, 1:2], in_=warm[:, 0:1], func=EXP)
+
+        def w_tile(dealt, dealt_s, a, b, t):
+            u = (2 * a + b) * 4 + t
+            return dealt[:, 64 * u : 64 * (u + 1)].bitcast(FP4X4), dealt_s[:, a, P * (4 * b + t) : P * (4 * b + t + 1)]
+
+        def project(dealt, dealt_s, b, moving, dst):
+            bank = psum.tile([P, 4, P], F32, name="bank", tag="bank")
+            for t in range(4):
+                for a in range(2):
+                    lhs, lhs_s = w_tile(dealt, dealt_s, a, b, t)
+                    nc.tensor.matmul_mx(
+                        out=bank[:, t, :], lhsT=lhs, lhsT_scale=lhs_s, rhs=moving[a][0], rhs_scale=moving[a][1],
+                        start=(a == 0), stop=(a == 1),
+                    )
+            nc.scalar.copy(out=dst, in_=bank[:].rearrange("p t j -> p j t"))
+
+        def keys(c):
+            made = []
+            for b in range(2):
+                kb = ring.tile([P, CH, 4], BF16, name="kb", bufs=3, align_bytes=64)
+                for s in range(SUB):
+                    js = slice(s * P, (s + 1) * P)
+                    moving = [(cols[c][:, a, js].bitcast(FP4X4), col_scales[c][a][:, js]) for a in range(2)]
+                    project(wk, wk_s, b, moving, kb[:, js, :])
+                kq = ring.tile([P, CH], U32, name="kq", bufs=4, align_bytes=64)
+                kq_s = ring.tile([P, CH], U8, name="kq_s", bufs=4, align_bytes=64)
+                nc.vector.quantize_mx(out=kq[:].bitcast(FP8X4), scales=kq_s[:], in_=kb[:].rearrange("p j t -> p (j t)"))
+                made.append((kq, kq_s))
+            return made
+
+        def values(c, wv8q, wv8q_s):
+            for nt in range(N // P):
+                ns = slice(nt * P, (nt + 1) * P)
+                bank = psum.tile([P, CH], F32, name="bank", tag="bank")
+                nc.tensor.matmul_mx(
+                    out=bank[:], lhsT=wv8q[:, ns].bitcast(FP8X4), lhsT_scale=wv8q_s[:, ns],
+                    rhs=cols[c][:, 0, :].bitcast(FP4X4), rhs_scale=col_scales[c][0], start=True, stop=False,
+                )
+                nc.tensor.matmul_mx(
+                    out=bank[:], lhsT=wv4[:, 2 * nt * P : 2 * (nt + 1) * P].bitcast(FP4X4), lhsT_scale=wv4_s[:, nt // 2, (nt % 2) * P : (nt % 2 + 1) * P],
+                    rhs=cols[c][:, 1, :].bitcast(FP4X4), rhs_scale=col_scales[c][1], start=False, stop=True,
+                )
+                staged = outs.tile([P, CH], F32, name="staged", tag="staged")
+                nc.vector.tensor_copy(out=staged[:], in_=bank[:])
+                nc.sync.dma_start(out=out_1[ns, c * CH : (c + 1) * CH], in_=staged[:])
+
+        def scores(c, made, qq, qq_s):
+            for mh in range(M // P):
+                ms = slice(mh * P, (mh + 1) * P)
+                bank = psum.tile([P, CH], F32, name="bank", tag="bank")
+                for b in range(2):
+                    nc.tensor.matmul_mx(
+                        out=bank[:], lhsT=qq[:, b, ms].bitcast(FP8X4), lhsT_scale=qq_s[:, b, ms],
+                        rhs=made[b][0][:].bitcast(FP8X4), rhs_scale=made[b][1][:], start=(b == 0), stop=(b == 1),
+                    )
+                staged = outs.tile([P, CH], F32, name="staged", tag="staged")
+                nc.scalar.activation(out=staged[:], in_=bank[:], func=EXP, scale=SCORE_SCALE)
+                nc.sync.dma_start(out=out_0[ms, c * CH : (c + 1) * CH], in_=staged[:])
+
+        wv8b = keep.tile([P, N, 4], BF16, name="wv8b", align_bytes=64)
+        nc.vector.tensor_copy(
+            out=wv8b[:].rearrange("p (c i) t -> p c t i", i=4), in_=wv8_raw[:].rearrange("p t (c i) -> p c t i", i=4)
+        )
+        x_raw = keep.tile([P, 2, 4, M], F32, name="x_raw", tag="raw_float", align_bytes=64)
+        nc.sync.dma_start(out=x_raw[:], in_=x.rearrange("(a p j) m -> p a j m", a=2, j=4))
+        cols.append(gather_words(1))
+        wv8q = keep.tile([P, N], U32, name="wv8q", align_bytes=64)
+        wv8q_s = keep.tile([P, N], U8, name="wv8q_s", align_bytes=64)
+        nc.vector.quantize_mx(out=wv8q[:].bitcast(FP8X4), scales=wv8q_s[:], in_=wv8b[:].rearrange("p n t -> p (n t)"))
+
+        made = [keys(0)]
+        wq = deal(wq_raw[:], "wq", 4)
+        values(0, wv8q, wv8q_s)
+
+        xb = keep.tile([P, 2, M, 4], BF16, name="xb", align_bytes=64)
+        for a in range(2):
+            nc.scalar.copy(
+                out=xb[:, a].rearrange("p (c i) t -> p c t i", i=4), in_=x_raw[:, a].rearrange("p t (c i) -> p c t i", i=4)
+            )
+        xq = keep.tile([P, 2, M], U32, name="xq", align_bytes=64)
+        xq_s = keep.tile([P, 2, M], U8, name="xq_s", align_bytes=64)
+        nc.vector.quantize_mx(
+            out=xq[:].rearrange("p a m -> p (a m)").bitcast(FP8X4),
+            scales=xq_s[:].rearrange("p a m -> p (a m)"),
+            in_=xb[:].rearrange("p a m t -> p (a m t)"),
+        )
+        cols.append(gather_words(2))
+        made.append(keys(1))
+
+        qb = keep.tile([P, 2, M, 4], BF16, name="qb", align_bytes=64)
+        for b in range(2):
+            for mh in range(M // P):
+                ms = slice(mh * P, (mh + 1) * P)
+                moving = [(xq[:, a, ms].bitcast(FP8X4), xq_s[:, a, ms]) for a in range(2)]
+                project(wq, wq_s, b, moving, qb[:, b, ms, :])
+        qq = keep.tile([P, 2, M], U32, name="qq", align_bytes=64)
+        qq_s = keep.tile([P, 2, M], U8, name="qq_s", align_bytes=64)
+        nc.vector.quantize_mx(
+            out=qq[:].rearrange("p a m -> p (a m)").bitcast(FP8X4),
+            scales=qq_s[:].rearrange("p a m -> p (a m)"),
+            in_=qb[:].rearrange("p a m t -> p (a m t)"),
+        )
+        values(1, wv8q, wv8q_s)
+        scores(0, made[0], qq, qq_s)
+        cols.append(gather_words(3))
+        made.append(keys(2))
+        scores(1, made[1], qq, qq_s)
+        values(2, wv8q, wv8q_s)
+        made.append(keys(3))
+        scores(2, made[2], qq, qq_s)
+        values(3, wv8q, wv8q_s)
+        scores(3, made[3], qq, qq_s)

@@ -16,9 +16,10 @@ FP4X4 = mybir.dt.float4_e2m1fn_x4
 EXP = mybir.ActivationFunctionType.Exp
 
 P = 128
+rows = slice(96, 128)
 CH = 512
 NCH = J // CH
-SUB = CH // P
+HALF = CH // 2
 SCORE_SCALE = 0.015625
 
 
@@ -32,31 +33,21 @@ def tile_list_kvt_qf_exp_kernel(
         outs = ctx.enter_context(tc.tile_pool(name="outs", bufs=6))
         psum = ctx.enter_context(tc.psum_pool(name="psum", bufs=8))
 
-        offsets = keep.tile([P, J // 16], U16, name="offsets")
-        nc.sync.dma_start(offsets[:], offs)
-        tscale = keep.tile([P, T], U8, name="tscale", align_bytes=64)
-        nc.sync.dma_start(out=tscale[96:128, :].bitcast(I32), in_=tab_scales.rearrange("a q t -> q a t").bitcast(I32))
-        table = keep.tile([P, T], U32, name="table", align_bytes=64)
-        nc.sync.dma_start(out=table[:].bitcast(I32), in_=tab_words[0].rearrange("p t b -> p (t b)").bitcast(I32))
 
-        def load_weight_words(words, name):
-            raw = keep.tile([P, 1024], I32, name=name, tag="raw_words", align_bytes=64)
-            nc.sync.dma_start(out=raw[:].rearrange("p (a n) -> p a n", a=2), in_=words.rearrange("a p n -> p a n").bitcast(I32))
+        def load_weight_words(words, name, tag):
+            raw = keep.tile([P, 2, words.shape[2] // 4], I32, name=name, tag=tag, align_bytes=64)
+            nc.sync.dma_start(out=raw[:], in_=words.rearrange("a p n -> p a n").bitcast(I32))
             return raw
 
-        def deal(raw, name, per_run):
-            dealt = keep.tile([P, 256 * per_run], I32, name=name, align_bytes=64)
+        def deal_words(raw, dst):
             nc.vector.tensor_copy(
-                out=dealt[:].rearrange("p (h t g w) -> p h t g w", h=4, t=4, g=16),
-                in_=raw.rearrange("p (h g t w) -> p h t g w", h=4, t=4, g=16),
+                out=dst.rearrange("p (a t g w) -> p a t g w", a=2, t=4, g=16),
+                in_=raw.rearrange("p a (g t w) -> p a t g w", t=4, g=16),
             )
-            return dealt
-
-        rows = slice(96, 128)
 
         def load_scale_rows(scales, name):
             raw = keep.tile([P, R], U8, name=name, align_bytes=64)
-            nc.scalar.dma_start(out=raw[rows, :].bitcast(I32), in_=scales.rearrange("a q r -> q a r").bitcast(I32))
+            nc.sync.dma_start(out=raw[rows, :].bitcast(I32), in_=scales.rearrange("a q r -> q a r").bitcast(I32))
             return raw
 
         def deal_scales(raw, dst):
@@ -65,18 +56,14 @@ def tile_list_kvt_qf_exp_kernel(
                 in_=raw[rows, :].bitcast(I32).rearrange("p (b g t w) -> p b t g w", b=2, t=4, g=16),
             )
 
-        def gather_scales(c0, c1, dst):
-            picked = keep.tile([P, (c1 - c0) * CH], U8, name="picked_scales%d" % c0, align_bytes=64)
-            for c in range(c0, c1):
-                nc.vector.tensor_copy(
-                    out=picked[:, (c - c0) * CH : (c - c0 + 1) * CH],
-                    in_=tscale[:].indirect(offsets[:, c * 32 : (c + 1) * 32]),
-                )
-            nc.vector.tensor_copy(out=dst.bitcast(I32), in_=picked[rows, :].bitcast(I32))
+        def gather_scales(c0, c1, tag):
+            picked = keep.tile([P, (c1 - c0) * CH], U8, name="picked_scales%d" % c0, tag=tag, align_bytes=64)
+            nc.vector.tensor_copy(out=picked[:], in_=tscale[:].indirect(offsets[:, c0 * 32 : c1 * 32]))
+            return picked
 
-        def place(staged, planes):
+        def place(queue, staged, planes):
             for q in range(4):
-                nc.scalar.dma_start(
+                queue.dma_start(
                     out=planes[32 * q : 32 * q + 4].bitcast(I32), in_=staged[96 + 8 * q : 104 + 8 * q, :].bitcast(I32)
                 )
 
@@ -85,54 +72,86 @@ def tile_list_kvt_qf_exp_kernel(
             nc.vector.memset(planes[:].rearrange("p a n -> p (a n)").bitcast(I32), 0)
             return planes
 
-        wk_raw = load_weight_words(wk_words, "wk_raw")
-        wk_sraw = load_scale_rows(wk_scales, "wk_sraw")
-        wq_sraw = load_scale_rows(wq_scales, "wq_sraw")
-        first_w, rest_w = CH + R, J - CH + R + N // 2
-        staged_first = keep.tile([P, first_w], U8, name="staged_first", tag="staged_first", align_bytes=64)
-        staged_rest = keep.tile([P, rest_w], U8, name="staged_rest", align_bytes=64)
-        nc.scalar.dma_start(
-            out=staged_rest[rows, J - CH + R :].bitcast(I32),
-            in_=wv4_scales[0].rearrange("q (h n) -> (q h) n", h=2).bitcast(I32),
-        )
-        wv8_raw = keep.tile([P, 4, N], F32, name="wv8_raw", tag="raw_float", align_bytes=64)
-        nc.sync.dma_start(out=wv8_raw[:], in_=wv8.rearrange("(p j) n -> p j n", j=4))
-        nc.vector.memset(tscale[0:96, :].bitcast(I32), 0)
-        planes_first = zeroed_planes(first_w, "planes_first")
-        planes_rest = zeroed_planes(rest_w, "planes_rest")
-
-        def gather_words(c):
-            picked = ring.tile([P, CH], U32, name="picked")
+        def gather_words(c, tag):
+            picked = keep.tile([P, CH], U32, name="picked", tag=tag, align_bytes=64)
             nc.vector.tensor_copy(out=picked[:], in_=table[:].indirect(offsets[:, c * 32 : (c + 1) * 32]))
             parted = keep.tile([P, 2, CH], U16, name="parted%d" % c, align_bytes=64)
             nc.vector.tensor_copy(out=parted[:], in_=picked[:].bitcast(U16).rearrange("p (j d) -> p d j", d=2))
             return parted
 
-        deal_scales(wk_sraw, staged_first[rows, CH:])
-        gather_scales(0, 1, staged_first[rows, :CH])
-        place(staged_first, planes_first)
-        cols = [gather_words(0)]
-        wk = deal(wk_raw[:], "wk", 4)
-        deal_scales(wq_sraw, staged_rest[rows, J - CH : J - CH + R])
-        gather_scales(1, NCH, staged_rest[rows, : J - CH])
-        place(staged_rest, planes_rest)
-        wk_s = planes_first[:, :, CH:]
-        wq_s = planes_rest[:, :, J - CH : J - CH + R]
-        wv4_s = planes_rest[:, :, J - CH + R :]
-        col_scales = [[planes_first[:, a, :CH] for a in range(2)]] + [
-            [planes_rest[:, a, (c - 1) * CH : c * CH] for a in range(2)] for c in range(1, NCH)
-        ]
-
-        wq_raw = load_weight_words(wq_words, "wq_raw")
-        wv4 = keep.tile([P, 2 * N], U8, name="wv4", tag="staged_first", align_bytes=64)
-        nc.sync.dma_start(out=wv4[:].bitcast(I32), in_=wv4_words[0].bitcast(I32))
-
+        offsets = keep.tile([P, J // 16], U16, name="offsets")
+        nc.sync.dma_start(offsets[:], offs)
+        tscale = keep.tile([P, T], U8, name="tscale", tag="tscale", align_bytes=64)
+        nc.sync.dma_start(out=tscale[rows, :].bitcast(I32), in_=tab_scales.rearrange("a q t -> q a t").bitcast(I32))
+        wk_sraw = load_scale_rows(wk_scales, "wk_sraw")
+        first_w = 2 * CH + R + N // 2
+        staged = keep.tile([P, first_w], U8, name="staged_rows", tag="staged_rows", align_bytes=64)
+        nc.sync.dma_start(
+            out=staged[rows, 2 * CH + R :].bitcast(I32),
+            in_=wv4_scales[0].rearrange("q (h n) -> (q h) n", h=2).bitcast(I32),
+        )
         warm = keep.tile([P, 2], F32, name="warm")
         nc.vector.memset(warm[:, 0:1], 0.0)
         nc.scalar.activation(out=warm[:, 1:2], in_=warm[:, 0:1], func=EXP)
+        wq_sraw = keep.tile([P, 2, R], U8, name="wq_sraw", align_bytes=64)
+        nc.vector.memset(wq_sraw[:].rearrange("p a r -> p (a r)").bitcast(I32), 0)
+        for q in range(4):
+            nc.scalar.dma_start(
+                out=wq_sraw[32 * q : 32 * q + 4].bitcast(I32),
+                in_=wq_scales[:, 4 * q : 4 * q + 4, :].rearrange("a r n -> r a n").bitcast(I32),
+            )
+        x_raw = keep.tile([P, 2, 4, M], F32, name="x_raw", tag="raw_float0", align_bytes=64)
+        nc.sync.dma_start(out=x_raw[:], in_=x.rearrange("(a p j) m -> p a j m", a=2, j=4))
+        wq_raw = load_weight_words(wq_words, "wq_raw", "wq_raw")
+        table = keep.tile([P, T], U32, name="table", align_bytes=64)
+        nc.sync.dma_start(out=table[:].bitcast(I32), in_=tab_words[0].rearrange("p t b -> p (t b)").bitcast(I32))
+
+        nc.vector.memset(tscale[0:96, :].bitcast(I32), 0)
+        planes_first = zeroed_planes(first_w, "planes_first")
+        planes_rest = zeroed_planes(J - 2 * CH, "planes_rest")
+
+        deal_scales(wk_sraw, staged[rows, 2 * CH : 2 * CH + R])
+        picked_first = gather_scales(0, 2, "picked_scales0")
+        wq_s = keep.tile([P, 2, R], U8, name="wq_s", align_bytes=64)
+        nc.vector.tensor_copy(
+            out=wq_s[:].rearrange("p a r -> p (a r)").bitcast(I32).rearrange("p (h t g w) -> p h t g w", h=4, t=4, g=16),
+            in_=wq_sraw[:].rearrange("p a r -> p (a r)").bitcast(I32).rearrange("p (h g t w) -> p h t g w", h=4, t=4, g=16),
+        )
+        nc.vector.tensor_copy(out=staged[rows, : 2 * CH].bitcast(I32), in_=picked_first[rows, :].bitcast(I32))
+        wk_s = planes_first[:, :, 2 * CH : 2 * CH + R]
+        wv4_s = planes_first[:, :, 2 * CH + R :]
+        col_scales = [
+            [(planes_first, planes_rest)[c // 2][:, a, (c % 2) * CH : (c % 2 + 1) * CH] for a in range(2)] for c in range(NCH)
+        ]
+
+        xb = keep.tile([P, 2, M, 4], BF16, name="xb", tag="xb", align_bytes=64)
+        for a, copy in enumerate((nc.scalar.copy, nc.vector.tensor_copy)):
+            copy(out=xb[:, a].rearrange("p (c i) t -> p c t i", i=4), in_=x_raw[:, a].rearrange("p t (c i) -> p c t i", i=4))
+        wq = keep.tile([P, 1024], I32, name="wq", align_bytes=64)
+        for b in range(2):
+            deal_words(wq_raw[:, :, 256 * b : 256 * (b + 1)], wq[:, 512 * b : 512 * (b + 1)])
+        wk_raw = [load_weight_words(wk_words[:, :, :R], "wk_raw0", "raw_float0")]
+        place(nc.sync, staged, planes_first)
+        wk_raw.append(load_weight_words(wk_words[:, :, R:], "wk_raw1", "raw_float1"))
+        xq = keep.tile([P, 2, M], U32, name="xq", align_bytes=64)
+        xq_s = keep.tile([P, 2, M], U8, name="xq_s", align_bytes=64)
+        nc.vector.quantize_mx(
+            out=xq[:].rearrange("p a m -> p (a m)").bitcast(FP8X4),
+            scales=xq_s[:].rearrange("p a m -> p (a m)"),
+            in_=xb[:].rearrange("p a m t -> p (a m t)"),
+        )
+        wv8_raw = keep.tile([P, 4, N], F32, name="wv8_raw", tag="xb", align_bytes=64)
+        nc.sync.dma_start(out=wv8_raw[:], in_=wv8.rearrange("(p j) n -> p j n", j=4))
+        place(nc.sync, gather_scales(2, NCH, "wq_raw"), planes_rest)
+        wv4 = keep.tile([P, 2 * N], U8, name="wv4", tag="staged_rows", align_bytes=64)
+        nc.sync.dma_start(out=wv4[:].bitcast(I32), in_=wv4_words[0].bitcast(I32))
+        cols = [gather_words(0, "tscale")]
+        wk = keep.tile([P, 1024], I32, name="wk", tag="tscale", align_bytes=64)
+        for b in range(2):
+            deal_words(wk_raw[b][:], wk[:, 512 * b : 512 * (b + 1)])
 
         def w_tile(dealt, dealt_s, a, b, t):
-            u = (2 * a + b) * 4 + t
+            u = 8 * b + 4 * a + t
             return dealt[:, 64 * u : 64 * (u + 1)].bitcast(FP4X4), dealt_s[:, a, P * (4 * b + t) : P * (4 * b + t + 1)]
 
         def project(dealt, dealt_s, b, moving, dst):
@@ -149,19 +168,36 @@ def tile_list_kvt_qf_exp_kernel(
         def keys(c):
             made = []
             for b in range(2):
-                kb = ring.tile([P, CH, 4], BF16, name="kb", bufs=3, align_bytes=64)
-                for s in range(SUB):
-                    js = slice(s * P, (s + 1) * P)
-                    moving = [(cols[c][:, a, js].bitcast(FP4X4), col_scales[c][a][:, js]) for a in range(2)]
-                    project(wk, wk_s, b, moving, kb[:, js, :])
+                pairs = ring.tile([P, 2, 2, HALF, 2], BF16, name="pairs", bufs=3, align_bytes=64)
+                for h in range(2):
+                    js = slice(h * HALF, (h + 1) * HALF)
+                    for u in range(2):
+                        bank = psum.tile([P, 2, HALF], F32, name="bank", tag="bank")
+                        for e in range(2):
+                            for a in range(2):
+                                lhs, lhs_s = w_tile(wk, wk_s, a, b, 2 * u + e)
+                                nc.tensor.matmul_mx(
+                                    out=bank[:, e, :], lhsT=lhs, lhsT_scale=lhs_s,
+                                    rhs=cols[c][:, a, js].bitcast(FP4X4), rhs_scale=col_scales[c][a][:, js],
+                                    start=(a == 0), stop=(a == 1),
+                                )
+                        nc.scalar.copy(out=pairs[:, h, u], in_=bank[:].rearrange("p e j -> p j e"))
+                if c == 0 and b == 0:
+                    kb = keep.tile([P, CH, 4], BF16, name="kb_first", tag="raw_float0", align_bytes=64)
+                else:
+                    kb = ring.tile([P, CH, 4], BF16, name="kb", bufs=2, align_bytes=64)
+                nc.vector.tensor_copy(
+                    out=kb[:].rearrange("p j t -> p (j t)").bitcast(I32).rearrange("p (h j u) -> p h j u", h=2, u=2),
+                    in_=pairs[:].rearrange("p h u j e -> p (h u j e)").bitcast(I32).rearrange("p (h u j) -> p h j u", h=2, u=2),
+                )
                 kq = ring.tile([P, CH], U32, name="kq", bufs=4, align_bytes=64)
                 kq_s = ring.tile([P, CH], U8, name="kq_s", bufs=4, align_bytes=64)
                 nc.vector.quantize_mx(out=kq[:].bitcast(FP8X4), scales=kq_s[:], in_=kb[:].rearrange("p j t -> p (j t)"))
                 made.append((kq, kq_s))
             return made
 
-        def values(c, wv8q, wv8q_s):
-            for nt in range(N // P):
+        def values(c, wv8q, wv8q_s, tiles=range(N // P)):
+            for nt in tiles:
                 ns = slice(nt * P, (nt + 1) * P)
                 bank = psum.tile([P, CH], F32, name="bank", tag="bank")
                 nc.tensor.matmul_mx(
@@ -189,56 +225,40 @@ def tile_list_kvt_qf_exp_kernel(
                 nc.scalar.activation(out=staged[:], in_=bank[:], func=EXP, scale=SCORE_SCALE)
                 nc.sync.dma_start(out=out_0[ms, c * CH : (c + 1) * CH], in_=staged[:])
 
-        wv8b = keep.tile([P, N, 4], BF16, name="wv8b", align_bytes=64)
-        nc.vector.tensor_copy(
-            out=wv8b[:].rearrange("p (c i) t -> p c t i", i=4), in_=wv8_raw[:].rearrange("p t (c i) -> p c t i", i=4)
-        )
-        x_raw = keep.tile([P, 2, 4, M], F32, name="x_raw", tag="raw_float", align_bytes=64)
-        nc.sync.dma_start(out=x_raw[:], in_=x.rearrange("(a p j) m -> p a j m", a=2, j=4))
-        cols.append(gather_words(1))
-        wv8q = keep.tile([P, N], U32, name="wv8q", align_bytes=64)
-        wv8q_s = keep.tile([P, N], U8, name="wv8q_s", align_bytes=64)
-        nc.vector.quantize_mx(out=wv8q[:].bitcast(FP8X4), scales=wv8q_s[:], in_=wv8b[:].rearrange("p n t -> p (n t)"))
-
-        made = [keys(0)]
-        wq = deal(wq_raw[:], "wq", 4)
-        values(0, wv8q, wv8q_s)
-
-        xb = keep.tile([P, 2, M, 4], BF16, name="xb", align_bytes=64)
-        for a in range(2):
-            nc.scalar.copy(
-                out=xb[:, a].rearrange("p (c i) t -> p c t i", i=4), in_=x_raw[:, a].rearrange("p t (c i) -> p c t i", i=4)
-            )
-        xq = keep.tile([P, 2, M], U32, name="xq", align_bytes=64)
-        xq_s = keep.tile([P, 2, M], U8, name="xq_s", align_bytes=64)
-        nc.vector.quantize_mx(
-            out=xq[:].rearrange("p a m -> p (a m)").bitcast(FP8X4),
-            scales=xq_s[:].rearrange("p a m -> p (a m)"),
-            in_=xb[:].rearrange("p a m t -> p (a m t)"),
-        )
-        cols.append(gather_words(2))
-        made.append(keys(1))
-
         qb = keep.tile([P, 2, M, 4], BF16, name="qb", align_bytes=64)
         for b in range(2):
             for mh in range(M // P):
                 ms = slice(mh * P, (mh + 1) * P)
                 moving = [(xq[:, a, ms].bitcast(FP8X4), xq_s[:, a, ms]) for a in range(2)]
                 project(wq, wq_s, b, moving, qb[:, b, ms, :])
-        qq = keep.tile([P, 2, M], U32, name="qq", align_bytes=64)
+        cols.append(gather_words(1, "raw_float0"))
+        qq = keep.tile([P, 2, M], U32, name="qq", tag="raw_float1", align_bytes=64)
         qq_s = keep.tile([P, 2, M], U8, name="qq_s", align_bytes=64)
         nc.vector.quantize_mx(
             out=qq[:].rearrange("p a m -> p (a m)").bitcast(FP8X4),
             scales=qq_s[:].rearrange("p a m -> p (a m)"),
             in_=qb[:].rearrange("p a m t -> p (a m t)"),
         )
-        values(1, wv8q, wv8q_s)
+        wv8b = keep.tile([P, N, 4], BF16, name="wv8b", tag="raw_float0", align_bytes=64)
+        nc.vector.tensor_copy(
+            out=wv8b[:].rearrange("p (c i) t -> p c t i", i=4), in_=wv8_raw[:].rearrange("p t (c i) -> p c t i", i=4)
+        )
+        wv8q = keep.tile([P, N], U32, name="wv8q", align_bytes=64)
+        wv8q_s = keep.tile([P, N], U8, name="wv8q_s", align_bytes=64)
+        nc.vector.quantize_mx(out=wv8q[:].bitcast(FP8X4), scales=wv8q_s[:], in_=wv8b[:].rearrange("p n t -> p (n t)"))
+
+        made = [keys(0)]
+        values(0, wv8q, wv8q_s)
+        cols.append(gather_words(2, "raw_float0"))
+        made.append(keys(1))
         scores(0, made[0], qq, qq_s)
-        cols.append(gather_words(3))
+        values(1, wv8q, wv8q_s)
+        cols.append(gather_words(3, "raw_float0"))
         made.append(keys(2))
         scores(1, made[1], qq, qq_s)
         values(2, wv8q, wv8q_s)
+        values(3, wv8q, wv8q_s, range(2))
         made.append(keys(3))
         scores(2, made[2], qq, qq_s)
-        values(3, wv8q, wv8q_s)
+        values(3, wv8q, wv8q_s, range(2, 4))
         scores(3, made[3], qq, qq_s)

@@ -209,21 +209,24 @@ def tile_list_kvt_qf_exp_kernel(
                     rhs=cols[c][:, 1, :].bitcast(FP4X4), rhs_scale=col_scales[c][1], start=False, stop=True,
                 )
                 staged = outs.tile([P, CH], F32, name="staged", tag="staged")
-                nc.vector.tensor_copy(out=staged[:], in_=bank[:])
+                if nt < (2 if c == 0 else 1):
+                    nc.scalar.copy(out=staged[:], in_=bank[:])
+                else:
+                    nc.vector.tensor_copy(out=staged[:], in_=bank[:])
                 nc.sync.dma_start(out=out_1[ns, c * CH : (c + 1) * CH], in_=staged[:])
 
-        def scores(c, made, qq, qq_s):
-            for mh in range(M // P):
-                ms = slice(mh * P, (mh + 1) * P)
-                bank = psum.tile([P, CH], F32, name="bank", tag="bank")
-                for b in range(2):
-                    nc.tensor.matmul_mx(
-                        out=bank[:], lhsT=qq[:, b, ms].bitcast(FP8X4), lhsT_scale=qq_s[:, b, ms],
-                        rhs=made[b][0][:].bitcast(FP8X4), rhs_scale=made[b][1][:], start=(b == 0), stop=(b == 1),
-                    )
-                staged = outs.tile([P, CH], F32, name="staged", tag="staged")
-                nc.scalar.activation(out=staged[:], in_=bank[:], func=EXP, scale=SCORE_SCALE)
-                nc.sync.dma_start(out=out_0[ms, c * CH : (c + 1) * CH], in_=staged[:])
+        def scores(c, made, qq, qq_s, mh, js=slice(0, CH)):
+            ms = slice(mh * P, (mh + 1) * P)
+            width = js.stop - js.start
+            bank = psum.tile([P, width], F32, name="bank", tag="bank")
+            for b in range(2):
+                nc.tensor.matmul_mx(
+                    out=bank[:], lhsT=qq[:, b, ms].bitcast(FP8X4), lhsT_scale=qq_s[:, b, ms],
+                    rhs=made[b][0][:, js].bitcast(FP8X4), rhs_scale=made[b][1][:, js], start=(b == 0), stop=(b == 1),
+                )
+            staged = outs.tile([P, width], F32, name="staged", tag="staged")
+            nc.scalar.activation(out=staged[:], in_=bank[:], func=EXP, scale=SCORE_SCALE)
+            nc.sync.dma_start(out=out_0[ms, c * CH + js.start : c * CH + js.stop], in_=staged[:])
 
         qb = keep.tile([P, 2, M, 4], BF16, name="qb", align_bytes=64)
         for b in range(2):
@@ -232,13 +235,6 @@ def tile_list_kvt_qf_exp_kernel(
                 moving = [(xq[:, a, ms].bitcast(FP8X4), xq_s[:, a, ms]) for a in range(2)]
                 project(wq, wq_s, b, moving, qb[:, b, ms, :])
         cols.append(gather_words(1, "raw_float0"))
-        qq = keep.tile([P, 2, M], U32, name="qq", tag="raw_float1", align_bytes=64)
-        qq_s = keep.tile([P, 2, M], U8, name="qq_s", align_bytes=64)
-        nc.vector.quantize_mx(
-            out=qq[:].rearrange("p a m -> p (a m)").bitcast(FP8X4),
-            scales=qq_s[:].rearrange("p a m -> p (a m)"),
-            in_=qb[:].rearrange("p a m t -> p (a m t)"),
-        )
         wv8b = keep.tile([P, N, 4], BF16, name="wv8b", tag="raw_float0", align_bytes=64)
         nc.vector.tensor_copy(
             out=wv8b[:].rearrange("p (c i) t -> p c t i", i=4), in_=wv8_raw[:].rearrange("p t (c i) -> p c t i", i=4)
@@ -247,18 +243,31 @@ def tile_list_kvt_qf_exp_kernel(
         wv8q_s = keep.tile([P, N], U8, name="wv8q_s", align_bytes=64)
         nc.vector.quantize_mx(out=wv8q[:].bitcast(FP8X4), scales=wv8q_s[:], in_=wv8b[:].rearrange("p n t -> p (n t)"))
 
+        qq = keep.tile([P, 2, M], U32, name="qq", tag="wq_raw", align_bytes=64)
+        qq_s = keep.tile([P, 2, M], U8, name="qq_s", align_bytes=64)
+        nc.vector.quantize_mx(
+            out=qq[:].rearrange("p a m -> p (a m)").bitcast(FP8X4),
+            scales=qq_s[:].rearrange("p a m -> p (a m)"),
+            in_=qb[:].rearrange("p a m t -> p (a m t)"),
+        )
         made = [keys(0)]
         values(0, wv8q, wv8q_s)
         cols.append(gather_words(2, "raw_float0"))
         made.append(keys(1))
-        scores(0, made[0], qq, qq_s)
+        scores(0, made[0], qq, qq_s, 0)
+        scores(0, made[0], qq, qq_s, 1)
         values(1, wv8q, wv8q_s)
         cols.append(gather_words(3, "raw_float0"))
         made.append(keys(2))
-        scores(1, made[1], qq, qq_s)
+        scores(1, made[1], qq, qq_s, 0)
+        scores(1, made[1], qq, qq_s, 1)
         values(2, wv8q, wv8q_s)
-        values(3, wv8q, wv8q_s, range(2))
+        values(3, wv8q, wv8q_s, range(1))
         made.append(keys(3))
-        scores(2, made[2], qq, qq_s)
-        values(3, wv8q, wv8q_s, range(2, 4))
-        scores(3, made[3], qq, qq_s)
+        scores(2, made[2], qq, qq_s, 0)
+        scores(2, made[2], qq, qq_s, 1)
+        values(3, wv8q, wv8q_s, range(1, 3))
+        scores(3, made[3], qq, qq_s, 0)
+        values(3, wv8q, wv8q_s, range(3, 4))
+        for h in range(2):
+            scores(3, made[3], qq, qq_s, 1, slice(h * HALF, (h + 1) * HALF))

@@ -33,7 +33,6 @@ def tile_list_kvt_qf_exp_kernel(
         outs = ctx.enter_context(tc.tile_pool(name="outs", bufs=6))
         psum = ctx.enter_context(tc.psum_pool(name="psum", bufs=8))
 
-
         def load_weight_words(words, name, tag):
             raw = keep.tile([P, 2, words.shape[2] // 4], I32, name=name, tag=tag, align_bytes=64)
             nc.sync.dma_start(out=raw[:], in_=words.rearrange("a p n -> p a n").bitcast(I32))
@@ -45,25 +44,9 @@ def tile_list_kvt_qf_exp_kernel(
                 in_=raw.rearrange("p a (g t w) -> p a t g w", t=4, g=16),
             )
 
-        def load_scale_rows(scales, name):
-            raw = keep.tile([P, R], U8, name=name, align_bytes=64)
-            nc.sync.dma_start(out=raw[rows, :].bitcast(I32), in_=scales.rearrange("a q r -> q a r").bitcast(I32))
-            return raw
-
-        def deal_scales(raw, dst):
-            nc.vector.tensor_copy(
-                out=dst.bitcast(I32).rearrange("p (b t g w) -> p b t g w", b=2, t=4, g=16),
-                in_=raw[rows, :].bitcast(I32).rearrange("p (b g t w) -> p b t g w", b=2, t=4, g=16),
-            )
-
-        def gather_scales(c0, c1, tag):
-            picked = keep.tile([P, (c1 - c0) * CH], U8, name="picked_scales%d" % c0, tag=tag, align_bytes=64)
-            nc.vector.tensor_copy(out=picked[:], in_=tscale[:].indirect(offsets[:, c0 * 32 : c1 * 32]))
-            return picked
-
-        def place(queue, staged, planes):
-            for q in range(4):
-                queue.dma_start(
+        def place(staged, planes):
+            for q in (0, 2, 1, 3):
+                nc.sync.dma_start(
                     out=planes[32 * q : 32 * q + 4].bitcast(I32), in_=staged[96 + 8 * q : 104 + 8 * q, :].bitcast(I32)
                 )
 
@@ -72,22 +55,36 @@ def tile_list_kvt_qf_exp_kernel(
             nc.vector.memset(planes[:].rearrange("p a n -> p (a n)").bitcast(I32), 0)
             return planes
 
-        def gather_words(c, tag):
-            picked = keep.tile([P, CH], U32, name="picked", tag=tag, align_bytes=64)
+        def gather_words(c):
+            picked = keep.tile([P, CH], U32, name="picked", tag="picked", align_bytes=64)
             nc.vector.tensor_copy(out=picked[:], in_=table[:].indirect(offsets[:, c * 32 : (c + 1) * 32]))
-            parted = keep.tile([P, 2, CH], U16, name="parted%d" % c, align_bytes=64)
-            nc.vector.tensor_copy(out=parted[:], in_=picked[:].bitcast(U16).rearrange("p (j d) -> p d j", d=2))
+            return picked
+
+        def part_words(picked, name, tag, pieces=1):
+            parted = keep.tile([P, 2, CH], U16, name=name, tag=tag, align_bytes=64)
+            halves = picked[:].bitcast(U16).rearrange("p (j d) -> p d j", d=2)
+            width = CH // pieces
+            for h in range(pieces):
+                js = slice(h * width, (h + 1) * width)
+                nc.vector.tensor_copy(out=parted[:, :, js], in_=halves[:, :, js])
             return parted
+
+        def gather_scales(c0, c1, tag):
+            picked = keep.tile([P, (c1 - c0) * CH], U8, name="picked_scales%d" % c0, tag=tag, align_bytes=64)
+            nc.vector.tensor_copy(out=picked[:], in_=tscale[:].indirect(offsets[:, c0 * 32 : c1 * 32]))
+            return picked
+
 
         offsets = keep.tile([P, J // 16], U16, name="offsets")
         nc.sync.dma_start(offsets[:], offs)
-        tscale = keep.tile([P, T], U8, name="tscale", tag="tscale", align_bytes=64)
+        tscale = keep.tile([P, T], U8, name="tscale", align_bytes=64)
         nc.sync.dma_start(out=tscale[rows, :].bitcast(I32), in_=tab_scales.rearrange("a q t -> q a t").bitcast(I32))
-        wk_sraw = load_scale_rows(wk_scales, "wk_sraw")
-        first_w = 2 * CH + R + N // 2
-        staged = keep.tile([P, first_w], U8, name="staged_rows", tag="staged_rows", align_bytes=64)
+        wk_sraw = keep.tile([P, R], U8, name="wk_sraw", align_bytes=64)
+        nc.sync.dma_start(out=wk_sraw[rows, :].bitcast(I32), in_=wk_scales.rearrange("a q r -> q a r").bitcast(I32))
+        first_w = CH + R + N // 2
+        staged_rows = keep.tile([P, first_w], U8, name="staged_rows", align_bytes=64)
         nc.sync.dma_start(
-            out=staged[rows, 2 * CH + R :].bitcast(I32),
+            out=staged_rows[rows, CH + R :].bitcast(I32),
             in_=wv4_scales[0].rearrange("q (h n) -> (q h) n", h=2).bitcast(I32),
         )
         warm = keep.tile([P, 2], F32, name="warm")
@@ -95,44 +92,54 @@ def tile_list_kvt_qf_exp_kernel(
         nc.scalar.activation(out=warm[:, 1:2], in_=warm[:, 0:1], func=EXP)
         wq_sraw = keep.tile([P, 2, R], U8, name="wq_sraw", align_bytes=64)
         nc.vector.memset(wq_sraw[:].rearrange("p a r -> p (a r)").bitcast(I32), 0)
-        for q in range(4):
+        for q in (0, 2, 1, 3):
             nc.scalar.dma_start(
                 out=wq_sraw[32 * q : 32 * q + 4].bitcast(I32),
                 in_=wq_scales[:, 4 * q : 4 * q + 4, :].rearrange("a r n -> r a n").bitcast(I32),
             )
-        x_raw = keep.tile([P, 2, 4, M], F32, name="x_raw", tag="raw_float0", align_bytes=64)
+        x_raw = keep.tile([P, 2, 4, M], F32, name="x_raw", align_bytes=64)
         nc.sync.dma_start(out=x_raw[:], in_=x.rearrange("(a p j) m -> p a j m", a=2, j=4))
         wq_raw = load_weight_words(wq_words, "wq_raw", "wq_raw")
         table = keep.tile([P, T], U32, name="table", align_bytes=64)
         nc.sync.dma_start(out=table[:].bitcast(I32), in_=tab_words[0].rearrange("p t b -> p (t b)").bitcast(I32))
+        wk_raw = [load_weight_words(wk_words[:, :, :R], "wk_raw0", "wk_raw0")]
 
         nc.vector.memset(tscale[0:96, :].bitcast(I32), 0)
-        planes_first = zeroed_planes(first_w, "planes_first")
-        planes_rest = zeroed_planes(J - 2 * CH, "planes_rest")
+        planes_a = zeroed_planes(first_w, "planes_a")
+        planes_b = zeroed_planes(2 * CH, "planes_b")
+        planes_c = zeroed_planes(CH, "planes_c")
 
-        deal_scales(wk_sraw, staged[rows, 2 * CH : 2 * CH + R])
-        picked_first = gather_scales(0, 2, "picked_scales0")
+        nc.vector.tensor_copy(
+            out=staged_rows[rows, CH : CH + R].bitcast(I32).rearrange("p (b t g w) -> p b t g w", b=2, t=4, g=16),
+            in_=wk_sraw[rows, :].bitcast(I32).rearrange("p (b g t w) -> p b t g w", b=2, t=4, g=16),
+        )
+        picked_a = gather_scales(0, 1, "picked_a")
+        nc.vector.tensor_copy(out=staged_rows[rows, :CH].bitcast(I32), in_=picked_a[rows, :].bitcast(I32))
+        place(staged_rows, planes_a)
+        wk_raw.append(load_weight_words(wk_words[:, :, R:], "wk_raw1", "wk_raw1"))
+        place(gather_scales(1, 3, "picked_b"), planes_b)
+        wv8_raw = keep.tile([P, 4, N], F32, name="wv8_raw", tag="wv8_raw", align_bytes=64)
+        nc.sync.dma_start(out=wv8_raw[:], in_=wv8.rearrange("(p j) n -> p j n", j=4))
+        wv4 = keep.tile([P, 2 * N], U8, name="wv4", align_bytes=64)
+        nc.sync.dma_start(out=wv4[:].bitcast(I32), in_=wv4_words[0].bitcast(I32))
+        wk_s = planes_a[:, :, CH : CH + R]
+        wv4_s = planes_a[:, :, CH + R :]
+        col_scales = [
+            [planes[:, a, first : first + CH] for a in range(2)]
+            for planes, first in ((planes_a, 0), (planes_b, 0), (planes_b, CH), (planes_c, 0))
+        ]
+
         wq_s = keep.tile([P, 2, R], U8, name="wq_s", align_bytes=64)
         nc.vector.tensor_copy(
             out=wq_s[:].rearrange("p a r -> p (a r)").bitcast(I32).rearrange("p (h t g w) -> p h t g w", h=4, t=4, g=16),
             in_=wq_sraw[:].rearrange("p a r -> p (a r)").bitcast(I32).rearrange("p (h g t w) -> p h t g w", h=4, t=4, g=16),
         )
-        nc.vector.tensor_copy(out=staged[rows, : 2 * CH].bitcast(I32), in_=picked_first[rows, :].bitcast(I32))
-        wk_s = planes_first[:, :, 2 * CH : 2 * CH + R]
-        wv4_s = planes_first[:, :, 2 * CH + R :]
-        col_scales = [
-            [(planes_first, planes_rest)[c // 2][:, a, (c % 2) * CH : (c % 2 + 1) * CH] for a in range(2)] for c in range(NCH)
-        ]
-
         xb = keep.tile([P, 2, M, 4], BF16, name="xb", tag="xb", align_bytes=64)
-        for a, copy in enumerate((nc.scalar.copy, nc.vector.tensor_copy)):
-            copy(out=xb[:, a].rearrange("p (c i) t -> p c t i", i=4), in_=x_raw[:, a].rearrange("p t (c i) -> p c t i", i=4))
+        for a in range(2):
+            nc.scalar.copy(out=xb[:, a].rearrange("p (c i) t -> p c t i", i=4), in_=x_raw[:, a].rearrange("p t (c i) -> p c t i", i=4))
         wq = keep.tile([P, 1024], I32, name="wq", align_bytes=64)
         for b in range(2):
             deal_words(wq_raw[:, :, 256 * b : 256 * (b + 1)], wq[:, 512 * b : 512 * (b + 1)])
-        wk_raw = [load_weight_words(wk_words[:, :, :R], "wk_raw0", "raw_float0")]
-        place(nc.sync, staged, planes_first)
-        wk_raw.append(load_weight_words(wk_words[:, :, R:], "wk_raw1", "raw_float1"))
         xq = keep.tile([P, 2, M], U32, name="xq", align_bytes=64)
         xq_s = keep.tile([P, 2, M], U8, name="xq_s", align_bytes=64)
         nc.vector.quantize_mx(
@@ -140,134 +147,156 @@ def tile_list_kvt_qf_exp_kernel(
             scales=xq_s[:].rearrange("p a m -> p (a m)"),
             in_=xb[:].rearrange("p a m t -> p (a m t)"),
         )
-        wv8_raw = keep.tile([P, 4, N], F32, name="wv8_raw", tag="xb", align_bytes=64)
-        nc.sync.dma_start(out=wv8_raw[:], in_=wv8.rearrange("(p j) n -> p j n", j=4))
-        place(nc.sync, gather_scales(2, NCH, "wq_raw"), planes_rest)
-        wv4 = keep.tile([P, 2 * N], U8, name="wv4", tag="staged_rows", align_bytes=64)
-        nc.sync.dma_start(out=wv4[:].bitcast(I32), in_=wv4_words[0].bitcast(I32))
-        cols = [gather_words(0, "tscale")]
-        wk = keep.tile([P, 1024], I32, name="wk", tag="tscale", align_bytes=64)
-        for b in range(2):
-            deal_words(wk_raw[b][:], wk[:, 512 * b : 512 * (b + 1)])
+        place(gather_scales(3, 4, "xb"), planes_c)
 
         def w_tile(dealt, dealt_s, a, b, t):
             u = 8 * b + 4 * a + t
             return dealt[:, 64 * u : 64 * (u + 1)].bitcast(FP4X4), dealt_s[:, a, P * (4 * b + t) : P * (4 * b + t + 1)]
 
-        def project(dealt, dealt_s, b, moving, dst):
+        def project(b, ms, dst):
             bank = psum.tile([P, 4, P], F32, name="bank", tag="bank")
             for t in range(4):
                 for a in range(2):
-                    lhs, lhs_s = w_tile(dealt, dealt_s, a, b, t)
+                    lhs, lhs_s = w_tile(wq, wq_s, a, b, t)
                     nc.tensor.matmul_mx(
-                        out=bank[:, t, :], lhsT=lhs, lhsT_scale=lhs_s, rhs=moving[a][0], rhs_scale=moving[a][1],
+                        out=bank[:, t, :], lhsT=lhs, lhsT_scale=lhs_s, rhs=xq[:, a, ms].bitcast(FP8X4), rhs_scale=xq_s[:, a, ms],
                         start=(a == 0), stop=(a == 1),
                     )
             nc.scalar.copy(out=dst, in_=bank[:].rearrange("p t j -> p j t"))
 
-        def keys(c):
-            made = []
-            for b in range(2):
-                pairs = ring.tile([P, 2, 2, HALF, 2], BF16, name="pairs", bufs=3, align_bytes=64)
-                for h in range(2):
-                    js = slice(h * HALF, (h + 1) * HALF)
-                    for u in range(2):
-                        bank = psum.tile([P, 2, HALF], F32, name="bank", tag="bank")
-                        for e in range(2):
-                            for a in range(2):
-                                lhs, lhs_s = w_tile(wk, wk_s, a, b, 2 * u + e)
-                                nc.tensor.matmul_mx(
-                                    out=bank[:, e, :], lhsT=lhs, lhsT_scale=lhs_s,
-                                    rhs=cols[c][:, a, js].bitcast(FP4X4), rhs_scale=col_scales[c][a][:, js],
-                                    start=(a == 0), stop=(a == 1),
-                                )
-                        nc.scalar.copy(out=pairs[:, h, u], in_=bank[:].rearrange("p e j -> p j e"))
-                if c == 0 and b == 0:
-                    kb = keep.tile([P, CH, 4], BF16, name="kb_first", tag="raw_float0", align_bytes=64)
-                else:
-                    kb = ring.tile([P, CH, 4], BF16, name="kb", bufs=2, align_bytes=64)
-                nc.vector.tensor_copy(
-                    out=kb[:].rearrange("p j t -> p (j t)").bitcast(I32).rearrange("p (h j u) -> p h j u", h=2, u=2),
-                    in_=pairs[:].rearrange("p h u j e -> p (h u j e)").bitcast(I32).rearrange("p (h u j) -> p h j u", h=2, u=2),
-                )
-                kq = ring.tile([P, CH], U32, name="kq", bufs=4, align_bytes=64)
-                kq_s = ring.tile([P, CH], U8, name="kq_s", bufs=4, align_bytes=64)
-                nc.vector.quantize_mx(out=kq[:].bitcast(FP8X4), scales=kq_s[:], in_=kb[:].rearrange("p j t -> p (j t)"))
-                made.append((kq, kq_s))
-            return made
+        def key_sums(c, b):
+            pairs = ring.tile([P, 2, 2, HALF, 2], BF16, name="pairs", bufs=4, align_bytes=64)
+            for h in range(2):
+                js = slice(h * HALF, (h + 1) * HALF)
+                for u in range(2):
+                    bank = psum.tile([P, 2, HALF], F32, name="bank", tag="bank")
+                    for e in range(2):
+                        for a in range(2):
+                            lhs, lhs_s = w_tile(wk, wk_s, a, b, 2 * u + e)
+                            nc.tensor.matmul_mx(
+                                out=bank[:, e, :], lhsT=lhs, lhsT_scale=lhs_s,
+                                rhs=cols[c][:, a, js].bitcast(FP4X4), rhs_scale=col_scales[c][a][:, js],
+                                start=(a == 0), stop=(a == 1),
+                            )
+                    nc.scalar.copy(out=pairs[:, h, u], in_=bank[:].rearrange("p e j -> p j e"))
+            return pairs
 
-        def values(c, wv8q, wv8q_s, tiles=range(N // P)):
-            for nt in tiles:
-                ns = slice(nt * P, (nt + 1) * P)
-                bank = psum.tile([P, CH], F32, name="bank", tag="bank")
-                nc.tensor.matmul_mx(
-                    out=bank[:], lhsT=wv8q[:, ns].bitcast(FP8X4), lhsT_scale=wv8q_s[:, ns],
-                    rhs=cols[c][:, 0, :].bitcast(FP4X4), rhs_scale=col_scales[c][0], start=True, stop=False,
-                )
-                nc.tensor.matmul_mx(
-                    out=bank[:], lhsT=wv4[:, 2 * nt * P : 2 * (nt + 1) * P].bitcast(FP4X4), lhsT_scale=wv4_s[:, nt // 2, (nt % 2) * P : (nt % 2 + 1) * P],
-                    rhs=cols[c][:, 1, :].bitcast(FP4X4), rhs_scale=col_scales[c][1], start=False, stop=True,
-                )
-                staged = outs.tile([P, CH], F32, name="staged", tag="staged")
-                if nt < (2 if c == 0 else 1):
-                    nc.scalar.copy(out=staged[:], in_=bank[:])
-                else:
-                    nc.vector.tensor_copy(out=staged[:], in_=bank[:])
-                nc.sync.dma_start(out=out_1[ns, c * CH : (c + 1) * CH], in_=staged[:])
+        def weave(pairs, hs=slice(0, 2), first=False):
+            count = hs.stop - hs.start
+            if first:
+                kb = keep.tile([P, count * HALF * 4], BF16, name="kb_first", tag="wv8_raw", align_bytes=64)
+            else:
+                kb = ring.tile([P, count * HALF * 4], BF16, name="kb", bufs=3, align_bytes=64)
+            nc.vector.tensor_copy(
+                out=kb[:].bitcast(I32).rearrange("p (h j u) -> p h j u", h=count, u=2),
+                in_=pairs[:].rearrange("p h u j e -> p (h u j e)").bitcast(I32).rearrange("p (h u j) -> p h j u", h=2, u=2)[:, hs],
+            )
+            return kb
 
-        def scores(c, made, qq, qq_s, mh, js=slice(0, CH)):
+        def quantised(kb):
+            width = kb.shape[1] // 4
+            kq = ring.tile([P, width], U32, name="kq", bufs=5, align_bytes=64)
+            kq_s = ring.tile([P, width], U8, name="kq_s", bufs=5, align_bytes=64)
+            nc.vector.quantize_mx(out=kq[:].bitcast(FP8X4), scales=kq_s[:], in_=kb[:])
+            return kq, kq_s
+
+        def values(c, nt, copy):
+            ns = slice(nt * P, (nt + 1) * P)
+            bank = psum.tile([P, CH], F32, name="bank", tag="bank")
+            nc.tensor.matmul_mx(
+                out=bank[:], lhsT=wv8q[:, ns].bitcast(FP8X4), lhsT_scale=wv8q_s[:, ns],
+                rhs=cols[c][:, 0, :].bitcast(FP4X4), rhs_scale=col_scales[c][0], start=True, stop=False,
+            )
+            nc.tensor.matmul_mx(
+                out=bank[:], lhsT=wv4[:, 2 * nt * P : 2 * (nt + 1) * P].bitcast(FP4X4), lhsT_scale=wv4_s[:, nt // 2, (nt % 2) * P : (nt % 2 + 1) * P],
+                rhs=cols[c][:, 1, :].bitcast(FP4X4), rhs_scale=col_scales[c][1], start=False, stop=True,
+            )
+            staged = outs.tile([P, CH], F32, name="staged", tag="staged")
+            copy(out=staged[:], in_=bank[:])
+            nc.sync.dma_start(out=out_1[ns, c * CH : (c + 1) * CH], in_=staged[:])
+
+        def scores(first, made, mh):
             ms = slice(mh * P, (mh + 1) * P)
-            width = js.stop - js.start
+            width = made[0][1].shape[1]
             bank = psum.tile([P, width], F32, name="bank", tag="bank")
             for b in range(2):
                 nc.tensor.matmul_mx(
                     out=bank[:], lhsT=qq[:, b, ms].bitcast(FP8X4), lhsT_scale=qq_s[:, b, ms],
-                    rhs=made[b][0][:, js].bitcast(FP8X4), rhs_scale=made[b][1][:, js], start=(b == 0), stop=(b == 1),
+                    rhs=made[b][0].bitcast(FP8X4), rhs_scale=made[b][1], start=(b == 0), stop=(b == 1),
                 )
             staged = outs.tile([P, width], F32, name="staged", tag="staged")
             nc.scalar.activation(out=staged[:], in_=bank[:], func=EXP, scale=SCORE_SCALE)
-            nc.sync.dma_start(out=out_0[ms, c * CH + js.start : c * CH + js.stop], in_=staged[:])
+            nc.sync.dma_start(out=out_0[ms, first : first + width], in_=staged[:])
+
+        def whole(made):
+            return [(kq[:], kq_s[:]) for kq, kq_s in made]
+
+        on_scalar, on_vector = nc.scalar.copy, nc.vector.tensor_copy
 
         qb = keep.tile([P, 2, M, 4], BF16, name="qb", align_bytes=64)
         for b in range(2):
             for mh in range(M // P):
                 ms = slice(mh * P, (mh + 1) * P)
-                moving = [(xq[:, a, ms].bitcast(FP8X4), xq_s[:, a, ms]) for a in range(2)]
-                project(wq, wq_s, b, moving, qb[:, b, ms, :])
-        cols.append(gather_words(1, "raw_float0"))
-        wv8b = keep.tile([P, N, 4], BF16, name="wv8b", tag="raw_float0", align_bytes=64)
-        nc.vector.tensor_copy(
-            out=wv8b[:].rearrange("p (c i) t -> p c t i", i=4), in_=wv8_raw[:].rearrange("p t (c i) -> p c t i", i=4)
-        )
-        wv8q = keep.tile([P, N], U32, name="wv8q", align_bytes=64)
-        wv8q_s = keep.tile([P, N], U8, name="wv8q_s", align_bytes=64)
-        nc.vector.quantize_mx(out=wv8q[:].bitcast(FP8X4), scales=wv8q_s[:], in_=wv8b[:].rearrange("p n t -> p (n t)"))
+                project(b, ms, qb[:, b, ms, :])
 
-        qq = keep.tile([P, 2, M], U32, name="qq", tag="wq_raw", align_bytes=64)
+        wk = keep.tile([P, 1024], I32, name="wk", align_bytes=64)
+        picked = gather_words(0)
+        deal_words(wk_raw[0][:], wk[:, :512])
+        cols = [part_words(picked, "parted0", "wk_raw0", 2)]
+        deal_words(wk_raw[1][:], wk[:, 512:])
+        picked = gather_words(1)
+        qq = keep.tile([P, 2, M], U32, name="qq", tag="wk_raw1", align_bytes=64)
         qq_s = keep.tile([P, 2, M], U8, name="qq_s", align_bytes=64)
         nc.vector.quantize_mx(
             out=qq[:].rearrange("p a m -> p (a m)").bitcast(FP8X4),
             scales=qq_s[:].rearrange("p a m -> p (a m)"),
             in_=qb[:].rearrange("p a m t -> p (a m t)"),
         )
-        made = [keys(0)]
-        values(0, wv8q, wv8q_s)
-        cols.append(gather_words(2, "raw_float0"))
-        made.append(keys(1))
-        scores(0, made[0], qq, qq_s, 0)
-        scores(0, made[0], qq, qq_s, 1)
-        values(1, wv8q, wv8q_s)
-        cols.append(gather_words(3, "raw_float0"))
-        made.append(keys(2))
-        scores(1, made[1], qq, qq_s, 0)
-        scores(1, made[1], qq, qq_s, 1)
-        values(2, wv8q, wv8q_s)
-        values(3, wv8q, wv8q_s, range(1))
-        made.append(keys(3))
-        scores(2, made[2], qq, qq_s, 0)
-        scores(2, made[2], qq, qq_s, 1)
-        values(3, wv8q, wv8q_s, range(1, 3))
-        scores(3, made[3], qq, qq_s, 0)
-        values(3, wv8q, wv8q_s, range(3, 4))
+        cols.append(part_words(picked, "parted1", "parted1"))
+        pairs = key_sums(0, 0)
+        wv8b = keep.tile([P, N, 4], BF16, name="wv8b", tag="picked", align_bytes=64)
+        nc.vector.tensor_copy(
+            out=wv8b[:].rearrange("p (c i) t -> p c t i", i=4), in_=wv8_raw[:].rearrange("p t (c i) -> p c t i", i=4)
+        )
+        kb = weave(pairs, first=True)
+        wv8q = keep.tile([P, N], U32, name="wv8q", align_bytes=64)
+        wv8q_s = keep.tile([P, N], U8, name="wv8q_s", align_bytes=64)
+        nc.vector.quantize_mx(out=wv8q[:].bitcast(FP8X4), scales=wv8q_s[:], in_=wv8b[:].rearrange("p n t -> p (n t)"))
+        made = {(0, 0): quantised(kb)}
+
+        def keys(c, b):
+            made[c, b] = quantised(weave(key_sums(c, b), first=(c == 0)))
+
+        def chunk_scores(c):
+            for mh in range(M // P):
+                scores(c * CH, whole([made[c, 0], made[c, 1]]), mh)
+
+        keys(0, 1)
+        keys(1, 0)
+        for nt in range(4):
+            values(0, nt, (on_scalar, on_vector)[nt % 2])
+        cols.append(part_words(gather_words(2), "parted2", "parted2"))
+        keys(1, 1)
+        chunk_scores(0)
+        values(1, 0, on_vector)
+        values(1, 1, on_vector)
+        keys(2, 0)
+        values(1, 2, on_vector)
+        values(1, 3, on_vector)
+        chunk_scores(1)
+        cols.append(part_words(gather_words(3), "parted3", "parted3"))
+        keys(2, 1)
+        for nt in range(4):
+            values(2, nt, (on_scalar, on_vector)[nt % 2])
+        keys(3, 0)
+        chunk_scores(2)
+        values(3, 0, on_vector)
+        values(3, 1, on_vector)
+        pairs = key_sums(3, 1)
+        last = [quantised(weave(pairs, slice(h, h + 1))) for h in range(2)]
+        values(3, 2, on_scalar)
+        values(3, 3, on_vector)
         for h in range(2):
-            scores(3, made[3], qq, qq_s, 1, slice(h * HALF, (h + 1) * HALF))
+            js = slice(h * HALF, (h + 1) * HALF)
+            for mh in range(M // P):
+                scores(3 * CH + h * HALF, [(made[3, 0][0][:, js], made[3, 0][1][:, js]), (last[h][0][:], last[h][1][:])], mh)

@@ -29,8 +29,9 @@ def tile_list_kvt_qf_exp_kernel(
     nc = tc.nc
     with ExitStack() as ctx:
         keep = ctx.enter_context(tc.tile_pool(name="keep", bufs=1))
+        shared = ctx.enter_context(tc.tile_pool(name="shared", bufs=1))
         ring = ctx.enter_context(tc.tile_pool(name="ring", bufs=2))
-        outs = ctx.enter_context(tc.tile_pool(name="outs", bufs=6))
+        outs = ctx.enter_context(tc.tile_pool(name="outs", bufs=8))
         psum = ctx.enter_context(tc.psum_pool(name="psum", bufs=8))
 
         def load_weight_words(words, name, tag):
@@ -42,6 +43,12 @@ def tile_list_kvt_qf_exp_kernel(
             nc.vector.tensor_copy(
                 out=dst.rearrange("p (a t g w) -> p a t g w", a=2, t=4, g=16),
                 in_=raw.rearrange("p a (g t w) -> p a t g w", t=4, g=16),
+            )
+
+        def deal_scales(raw, dst):
+            nc.vector.tensor_copy(
+                out=dst.bitcast(I32).rearrange("p (b t g w) -> p b t g w", b=2, t=4, g=16),
+                in_=raw[rows, :].bitcast(I32).rearrange("p (b g t w) -> p b t g w", b=2, t=4, g=16),
             )
 
         def place(staged, planes):
@@ -69,14 +76,19 @@ def tile_list_kvt_qf_exp_kernel(
                 nc.vector.tensor_copy(out=parted[:, :, js], in_=halves[:, :, js])
             return parted
 
-        def gather_scales(c0, c1, tag):
-            picked = keep.tile([P, (c1 - c0) * CH], U8, name="picked_scales%d" % c0, tag=tag, align_bytes=64)
-            nc.vector.tensor_copy(out=picked[:], in_=tscale[:].indirect(offsets[:, c0 * 32 : c1 * 32]))
+        def gather_scales(j0, j1, tag):
+            picked = keep.tile([P, j1 - j0], U8, name="picked_scales%d" % j0, tag=tag, align_bytes=64)
+            nc.vector.tensor_copy(out=picked[:], in_=tscale[:].indirect(offsets[:, j0 // 16 : j1 // 16]))
             return picked
 
 
+        warm = keep.tile([P, 2], F32, name="warm")
+        nc.vector.memset(warm[:, 0:1], 0.0)
+        nc.scalar.activation(out=warm[:, 1:2], in_=warm[:, 0:1], func=EXP)
         offsets = keep.tile([P, J // 16], U16, name="offsets")
         nc.sync.dma_start(offsets[:], offs)
+        wq_sraw = keep.tile([P, R], U8, name="wq_sraw", align_bytes=64)
+        nc.sync.dma_start(out=wq_sraw[rows, :].bitcast(I32), in_=wq_scales.rearrange("a q r -> q a r").bitcast(I32))
         tscale = keep.tile([P, T], U8, name="tscale", align_bytes=64)
         nc.sync.dma_start(out=tscale[rows, :].bitcast(I32), in_=tab_scales.rearrange("a q t -> q a t").bitcast(I32))
         wk_sraw = keep.tile([P, R], U8, name="wk_sraw", align_bytes=64)
@@ -87,38 +99,31 @@ def tile_list_kvt_qf_exp_kernel(
             out=staged_rows[rows, CH + R :].bitcast(I32),
             in_=wv4_scales[0].rearrange("q (h n) -> (q h) n", h=2).bitcast(I32),
         )
-        warm = keep.tile([P, 2], F32, name="warm")
-        nc.vector.memset(warm[:, 0:1], 0.0)
-        nc.scalar.activation(out=warm[:, 1:2], in_=warm[:, 0:1], func=EXP)
-        wq_sraw = keep.tile([P, 2, R], U8, name="wq_sraw", align_bytes=64)
-        nc.vector.memset(wq_sraw[:].rearrange("p a r -> p (a r)").bitcast(I32), 0)
-        for q in (0, 2, 1, 3):
-            nc.scalar.dma_start(
-                out=wq_sraw[32 * q : 32 * q + 4].bitcast(I32),
-                in_=wq_scales[:, 4 * q : 4 * q + 4, :].rearrange("a r n -> r a n").bitcast(I32),
-            )
-        x_raw = keep.tile([P, 2, 4, M], F32, name="x_raw", align_bytes=64)
-        nc.sync.dma_start(out=x_raw[:], in_=x.rearrange("(a p j) m -> p a j m", a=2, j=4))
+        x_raw = []
+        for a in range(2):
+            x_raw.append(keep.tile([P, 4, M], F32, name="x_raw%d" % a, align_bytes=64))
+            nc.sync.dma_start(out=x_raw[a][:], in_=x[512 * a : 512 * (a + 1)].rearrange("(p j) m -> p j m", j=4))
         wq_raw = load_weight_words(wq_words, "wq_raw", "wq_raw")
+        wq_s = zeroed_planes(R, "wq_s")
+        wq_rows = keep.tile([P, R], U8, name="wq_rows", align_bytes=64)
+        deal_scales(wq_sraw, wq_rows[rows, :])
+        place(wq_rows, wq_s)
         table = keep.tile([P, T], U32, name="table", align_bytes=64)
         nc.sync.dma_start(out=table[:].bitcast(I32), in_=tab_words[0].rearrange("p t b -> p (t b)").bitcast(I32))
         wk_raw = [load_weight_words(wk_words[:, :, :R], "wk_raw0", "wk_raw0")]
 
         nc.vector.memset(tscale[0:96, :].bitcast(I32), 0)
         planes_a = zeroed_planes(first_w, "planes_a")
-        planes_b = zeroed_planes(2 * CH, "planes_b")
-        planes_c = zeroed_planes(CH, "planes_c")
+        planes_b = zeroed_planes(J - CH, "planes_b")
+        split = (J - CH) // 2
 
-        nc.vector.tensor_copy(
-            out=staged_rows[rows, CH : CH + R].bitcast(I32).rearrange("p (b t g w) -> p b t g w", b=2, t=4, g=16),
-            in_=wk_sraw[rows, :].bitcast(I32).rearrange("p (b g t w) -> p b t g w", b=2, t=4, g=16),
-        )
-        picked_a = gather_scales(0, 1, "picked_a")
+        picked_a = gather_scales(0, CH, "picked_a")
+        deal_scales(wk_sraw, staged_rows[rows, CH : CH + R])
         nc.vector.tensor_copy(out=staged_rows[rows, :CH].bitcast(I32), in_=picked_a[rows, :].bitcast(I32))
         place(staged_rows, planes_a)
         wk_raw.append(load_weight_words(wk_words[:, :, R:], "wk_raw1", "wk_raw1"))
-        place(gather_scales(1, 3, "picked_b"), planes_b)
-        wv8_raw = keep.tile([P, 4, N], F32, name="wv8_raw", tag="wv8_raw", align_bytes=64)
+        place(gather_scales(CH, CH + split, "picked_b"), planes_b[:, :, :split])
+        wv8_raw = shared.tile([P, 4, N], F32, name="wv8_raw", offset=0, align_bytes=64)
         nc.sync.dma_start(out=wv8_raw[:], in_=wv8.rearrange("(p j) n -> p j n", j=4))
         wv4 = keep.tile([P, 2 * N], U8, name="wv4", align_bytes=64)
         nc.sync.dma_start(out=wv4[:].bitcast(I32), in_=wv4_words[0].bitcast(I32))
@@ -126,17 +131,12 @@ def tile_list_kvt_qf_exp_kernel(
         wv4_s = planes_a[:, :, CH + R :]
         col_scales = [
             [planes[:, a, first : first + CH] for a in range(2)]
-            for planes, first in ((planes_a, 0), (planes_b, 0), (planes_b, CH), (planes_c, 0))
+            for planes, first in ((planes_a, 0), (planes_b, 0), (planes_b, CH), (planes_b, 2 * CH))
         ]
 
-        wq_s = keep.tile([P, 2, R], U8, name="wq_s", align_bytes=64)
-        nc.vector.tensor_copy(
-            out=wq_s[:].rearrange("p a r -> p (a r)").bitcast(I32).rearrange("p (h t g w) -> p h t g w", h=4, t=4, g=16),
-            in_=wq_sraw[:].rearrange("p a r -> p (a r)").bitcast(I32).rearrange("p (h g t w) -> p h t g w", h=4, t=4, g=16),
-        )
         xb = keep.tile([P, 2, M, 4], BF16, name="xb", tag="xb", align_bytes=64)
         for a in range(2):
-            nc.scalar.copy(out=xb[:, a].rearrange("p (c i) t -> p c t i", i=4), in_=x_raw[:, a].rearrange("p t (c i) -> p c t i", i=4))
+            nc.scalar.copy(out=xb[:, a].rearrange("p (c i) t -> p c t i", i=4), in_=x_raw[a][:].rearrange("p t (c i) -> p c t i", i=4))
         wq = keep.tile([P, 1024], I32, name="wq", align_bytes=64)
         for b in range(2):
             deal_words(wq_raw[:, :, 256 * b : 256 * (b + 1)], wq[:, 512 * b : 512 * (b + 1)])
@@ -147,7 +147,7 @@ def tile_list_kvt_qf_exp_kernel(
             scales=xq_s[:].rearrange("p a m -> p (a m)"),
             in_=xb[:].rearrange("p a m t -> p (a m t)"),
         )
-        place(gather_scales(3, 4, "xb"), planes_c)
+        place(gather_scales(CH + split, J, "wq_raw"), planes_b[:, :, split:])
 
         def w_tile(dealt, dealt_s, a, b, t):
             u = 8 * b + 4 * a + t
@@ -184,7 +184,7 @@ def tile_list_kvt_qf_exp_kernel(
         def weave(pairs, hs=slice(0, 2), first=False):
             count = hs.stop - hs.start
             if first:
-                kb = keep.tile([P, count * HALF * 4], BF16, name="kb_first", tag="wv8_raw", align_bytes=64)
+                kb = shared.tile([P, count * HALF * 4], BF16, name="kb_first", offset=4096, align_bytes=64)
             else:
                 kb = ring.tile([P, count * HALF * 4], BF16, name="kb", bufs=3, align_bytes=64)
             nc.vector.tensor_copy(
@@ -195,8 +195,8 @@ def tile_list_kvt_qf_exp_kernel(
 
         def quantised(kb):
             width = kb.shape[1] // 4
-            kq = ring.tile([P, width], U32, name="kq", bufs=5, align_bytes=64)
-            kq_s = ring.tile([P, width], U8, name="kq_s", bufs=5, align_bytes=64)
+            kq = ring.tile([P, width], U32, name="kq", bufs=7, align_bytes=64)
+            kq_s = ring.tile([P, width], U8, name="kq_s", bufs=7, align_bytes=64)
             nc.vector.quantize_mx(out=kq[:].bitcast(FP8X4), scales=kq_s[:], in_=kb[:])
             return kq, kq_s
 
@@ -245,13 +245,6 @@ def tile_list_kvt_qf_exp_kernel(
         cols = [part_words(picked, "parted0", "wk_raw0", 2)]
         deal_words(wk_raw[1][:], wk[:, 512:])
         picked = gather_words(1)
-        qq = keep.tile([P, 2, M], U32, name="qq", tag="wk_raw1", align_bytes=64)
-        qq_s = keep.tile([P, 2, M], U8, name="qq_s", align_bytes=64)
-        nc.vector.quantize_mx(
-            out=qq[:].rearrange("p a m -> p (a m)").bitcast(FP8X4),
-            scales=qq_s[:].rearrange("p a m -> p (a m)"),
-            in_=qb[:].rearrange("p a m t -> p (a m t)"),
-        )
         cols.append(part_words(picked, "parted1", "parted1"))
         pairs = key_sums(0, 0)
         wv8b = keep.tile([P, N, 4], BF16, name="wv8b", tag="picked", align_bytes=64)
@@ -263,6 +256,13 @@ def tile_list_kvt_qf_exp_kernel(
         wv8q_s = keep.tile([P, N], U8, name="wv8q_s", align_bytes=64)
         nc.vector.quantize_mx(out=wv8q[:].bitcast(FP8X4), scales=wv8q_s[:], in_=wv8b[:].rearrange("p n t -> p (n t)"))
         made = {(0, 0): quantised(kb)}
+        qq = shared.tile([P, 2, M], U32, name="qq", offset=0, align_bytes=64)
+        qq_s = keep.tile([P, 2, M], U8, name="qq_s", align_bytes=64)
+        nc.vector.quantize_mx(
+            out=qq[:].rearrange("p a m -> p (a m)").bitcast(FP8X4),
+            scales=qq_s[:].rearrange("p a m -> p (a m)"),
+            in_=qb[:].rearrange("p a m t -> p (a m t)"),
+        )
 
         def keys(c, b):
             made[c, b] = quantised(weave(key_sums(c, b), first=(c == 0)))

@@ -67,13 +67,16 @@ def tile_list_kvt_qf_exp_kernel(
             nc.vector.tensor_copy(out=picked[:], in_=table[:].indirect(offsets[:, c * 32 : (c + 1) * 32]))
             return picked
 
-        def part_words(picked, name, tag, pieces=1):
-            parted = keep.tile([P, 2, CH], U16, name=name, tag=tag, align_bytes=64)
+        def part_words(picked, parted, pieces=1):
             halves = picked[:].bitcast(U16).rearrange("p (j d) -> p d j", d=2)
             width = CH // pieces
             for h in range(pieces):
                 js = slice(h * width, (h + 1) * width)
-                nc.vector.tensor_copy(out=parted[:, :, js], in_=halves[:, :, js])
+                if pieces == 1:
+                    nc.vector.tensor_copy(out=parted[:], in_=halves)
+                else:
+                    for a in range(2):
+                        nc.vector.tensor_copy(out=parted[:, a, js], in_=halves[:, a, js])
             return parted
 
         def gather_scales(j0, j1, tag):
@@ -103,13 +106,17 @@ def tile_list_kvt_qf_exp_kernel(
         for a in range(2):
             x_raw.append(keep.tile([P, 4, M], F32, name="x_raw%d" % a, align_bytes=64))
             nc.sync.dma_start(out=x_raw[a][:], in_=x[512 * a : 512 * (a + 1)].rearrange("(p j) m -> p j m", j=4))
-        wq_raw = load_weight_words(wq_words, "wq_raw", "wq_raw")
+        wq_raw = [load_weight_words(wq_words[:, :, :R], "wq_raw0", "wq_raw0")]
+        table = keep.tile([P, T], U32, name="table", align_bytes=64)
+        table_words = tab_words[0].rearrange("p t b -> p (t b)").bitcast(I32)
+        nc.sync.dma_start(out=table[:, : 2 * CH].bitcast(I32), in_=table_words[:, : 2 * CH])
         wq_s = zeroed_planes(R, "wq_s")
         wq_rows = keep.tile([P, R], U8, name="wq_rows", align_bytes=64)
         deal_scales(wq_sraw, wq_rows[rows, :])
         place(wq_rows, wq_s)
-        table = keep.tile([P, T], U32, name="table", align_bytes=64)
-        nc.sync.dma_start(out=table[:].bitcast(I32), in_=tab_words[0].rearrange("p t b -> p (t b)").bitcast(I32))
+        nc.sync.dma_start(out=table[:, 2 * CH : T - CH].bitcast(I32), in_=table_words[:, 2 * CH : T - CH])
+        wq_raw.append(load_weight_words(wq_words[:, :, R:], "wq_raw1", "wq_raw1"))
+        nc.sync.dma_start(out=table[:, T - CH :].bitcast(I32), in_=table_words[:, T - CH :])
         wk_raw = [load_weight_words(wk_words[:, :, :R], "wk_raw0", "wk_raw0")]
 
         nc.vector.memset(tscale[0:96, :].bitcast(I32), 0)
@@ -122,9 +129,9 @@ def tile_list_kvt_qf_exp_kernel(
         nc.vector.tensor_copy(out=staged_rows[rows, :CH].bitcast(I32), in_=picked_a[rows, :].bitcast(I32))
         place(staged_rows, planes_a)
         wk_raw.append(load_weight_words(wk_words[:, :, R:], "wk_raw1", "wk_raw1"))
-        place(gather_scales(CH, CH + split, "picked_b"), planes_b[:, :, :split])
         wv8_raw = shared.tile([P, 4, N], F32, name="wv8_raw", offset=0, align_bytes=64)
         nc.sync.dma_start(out=wv8_raw[:], in_=wv8.rearrange("(p j) n -> p j n", j=4))
+        place(gather_scales(CH, CH + split, "picked_b"), planes_b[:, :, :split])
         wv4 = keep.tile([P, 2 * N], U8, name="wv4", align_bytes=64)
         nc.sync.dma_start(out=wv4[:].bitcast(I32), in_=wv4_words[0].bitcast(I32))
         wk_s = planes_a[:, :, CH : CH + R]
@@ -138,8 +145,7 @@ def tile_list_kvt_qf_exp_kernel(
         for a in range(2):
             nc.scalar.copy(out=xb[:, a].rearrange("p (c i) t -> p c t i", i=4), in_=x_raw[a][:].rearrange("p t (c i) -> p c t i", i=4))
         wq = keep.tile([P, 1024], I32, name="wq", align_bytes=64)
-        for b in range(2):
-            deal_words(wq_raw[:, :, 256 * b : 256 * (b + 1)], wq[:, 512 * b : 512 * (b + 1)])
+        deal_words(wq_raw[0][:], wq[:, :512])
         xq = keep.tile([P, 2, M], U32, name="xq", align_bytes=64)
         xq_s = keep.tile([P, 2, M], U8, name="xq_s", align_bytes=64)
         nc.vector.quantize_mx(
@@ -147,7 +153,8 @@ def tile_list_kvt_qf_exp_kernel(
             scales=xq_s[:].rearrange("p a m -> p (a m)"),
             in_=xb[:].rearrange("p a m t -> p (a m t)"),
         )
-        place(gather_scales(CH + split, J, "wq_raw"), planes_b[:, :, split:])
+        place(gather_scales(CH + split, J, "xb"), planes_b[:, :, split:])
+        deal_words(wq_raw[1][:], wq[:, 512:])
 
         def w_tile(dealt, dealt_s, a, b, t):
             u = 8 * b + 4 * a + t
@@ -242,10 +249,10 @@ def tile_list_kvt_qf_exp_kernel(
         wk = keep.tile([P, 1024], I32, name="wk", align_bytes=64)
         picked = gather_words(0)
         deal_words(wk_raw[0][:], wk[:, :512])
-        cols = [part_words(picked, "parted0", "wk_raw0", 2)]
+        cols = [part_words(picked, keep.tile([P, 2, CH], U16, name="parted0", tag="wk_raw0", align_bytes=64), 2)]
         deal_words(wk_raw[1][:], wk[:, 512:])
         picked = gather_words(1)
-        cols.append(part_words(picked, "parted1", "parted1"))
+        cols.append(part_words(picked, keep.tile([P, 2, CH], U16, name="parted1", align_bytes=64)))
         pairs = key_sums(0, 0)
         wv8b = keep.tile([P, N, 4], BF16, name="wv8b", tag="picked", align_bytes=64)
         nc.vector.tensor_copy(
@@ -273,9 +280,11 @@ def tile_list_kvt_qf_exp_kernel(
 
         keys(0, 1)
         keys(1, 0)
-        for nt in range(4):
-            values(0, nt, (on_scalar, on_vector)[nt % 2])
-        cols.append(part_words(gather_words(2), "parted2", "parted2"))
+        values(0, 0, on_scalar)
+        values(0, 1, on_vector)
+        values(0, 2, on_scalar)
+        values(0, 3, on_vector)
+        cols.append(part_words(gather_words(2), keep.tile([P, 2, CH], U16, name="parted2", align_bytes=64)))
         keys(1, 1)
         chunk_scores(0)
         values(1, 0, on_vector)
@@ -284,7 +293,7 @@ def tile_list_kvt_qf_exp_kernel(
         values(1, 2, on_vector)
         values(1, 3, on_vector)
         chunk_scores(1)
-        cols.append(part_words(gather_words(3), "parted3", "parted3"))
+        cols.append(part_words(gather_words(3), keep.tile([P, 2, CH], U16, name="parted3", align_bytes=64)))
         keys(2, 1)
         for nt in range(4):
             values(2, nt, (on_scalar, on_vector)[nt % 2])

@@ -62,8 +62,8 @@ def tile_list_kvt_qf_exp_kernel(
             nc.vector.memset(planes[:].rearrange("p a n -> p (a n)").bitcast(I32), 0)
             return planes
 
-        def gather_words(c):
-            picked = keep.tile([P, CH], U32, name="picked", tag="picked", align_bytes=64)
+        def gather_words(c, tag="picked"):
+            picked = keep.tile([P, CH], U32, name="picked", tag=tag, align_bytes=64)
             nc.vector.tensor_copy(out=picked[:], in_=table[:].indirect(offsets[:, c * 32 : (c + 1) * 32]))
             return picked
 
@@ -90,8 +90,6 @@ def tile_list_kvt_qf_exp_kernel(
         nc.scalar.activation(out=warm[:, 1:2], in_=warm[:, 0:1], func=EXP)
         offsets = keep.tile([P, J // 16], U16, name="offsets")
         nc.sync.dma_start(offsets[:], offs)
-        wq_sraw = keep.tile([P, R], U8, name="wq_sraw", align_bytes=64)
-        nc.sync.dma_start(out=wq_sraw[rows, :].bitcast(I32), in_=wq_scales.rearrange("a q r -> q a r").bitcast(I32))
         tscale = keep.tile([P, T], U8, name="tscale", align_bytes=64)
         nc.sync.dma_start(out=tscale[rows, :].bitcast(I32), in_=tab_scales.rearrange("a q t -> q a t").bitcast(I32))
         wk_sraw = keep.tile([P, R], U8, name="wk_sraw", align_bytes=64)
@@ -102,27 +100,20 @@ def tile_list_kvt_qf_exp_kernel(
             out=staged_rows[rows, CH + R :].bitcast(I32),
             in_=wv4_scales[0].rearrange("q (h n) -> (q h) n", h=2).bitcast(I32),
         )
-        x_raw = []
-        for a in range(2):
-            x_raw.append(keep.tile([P, 4, M], F32, name="x_raw%d" % a, align_bytes=64))
-            nc.sync.dma_start(out=x_raw[a][:], in_=x[512 * a : 512 * (a + 1)].rearrange("(p j) m -> p j m", j=4))
-        wq_raw = [load_weight_words(wq_words[:, :, :R], "wq_raw0", "wq_raw0")]
+        wq_sraw = keep.tile([P, R], U8, name="wq_sraw", align_bytes=64)
+        nc.sync.dma_start(out=wq_sraw[rows, :].bitcast(I32), in_=wq_scales.rearrange("a q r -> q a r").bitcast(I32))
         table = keep.tile([P, T], U32, name="table", align_bytes=64)
         table_words = tab_words[0].rearrange("p t b -> p (t b)").bitcast(I32)
-        nc.sync.dma_start(out=table[:, : 2 * CH].bitcast(I32), in_=table_words[:, : 2 * CH])
-        wq_s = zeroed_planes(R, "wq_s")
-        wq_rows = keep.tile([P, R], U8, name="wq_rows", align_bytes=64)
-        deal_scales(wq_sraw, wq_rows[rows, :])
-        place(wq_rows, wq_s)
-        nc.sync.dma_start(out=table[:, 2 * CH : T - CH].bitcast(I32), in_=table_words[:, 2 * CH : T - CH])
-        wq_raw.append(load_weight_words(wq_words[:, :, R:], "wq_raw1", "wq_raw1"))
-        nc.sync.dma_start(out=table[:, T - CH :].bitcast(I32), in_=table_words[:, T - CH :])
+        nc.sync.dma_start(out=table[:, : T - 2 * CH].bitcast(I32), in_=table_words[:, : T - 2 * CH])
         wk_raw = [load_weight_words(wk_words[:, :, :R], "wk_raw0", "wk_raw0")]
+        nc.sync.dma_start(out=table[:, T - 2 * CH :].bitcast(I32), in_=table_words[:, T - 2 * CH :])
 
         nc.vector.memset(tscale[0:96, :].bitcast(I32), 0)
+        nc.vector.memset(wk_sraw[0:96, :].bitcast(I32), 0)
         planes_a = zeroed_planes(first_w, "planes_a")
-        planes_b = zeroed_planes(J - CH, "planes_b")
-        split = (J - CH) // 2
+        planes_b = zeroed_planes(CH, "planes_b")
+        planes_c = zeroed_planes(2 * CH, "planes_c")
+        wq_s = zeroed_planes(R, "wq_s")
 
         picked_a = gather_scales(0, CH, "picked_a")
         deal_scales(wk_sraw, staged_rows[rows, CH : CH + R])
@@ -131,30 +122,31 @@ def tile_list_kvt_qf_exp_kernel(
         wk_raw.append(load_weight_words(wk_words[:, :, R:], "wk_raw1", "wk_raw1"))
         wv8_raw = shared.tile([P, 4, N], F32, name="wv8_raw", offset=0, align_bytes=64)
         nc.sync.dma_start(out=wv8_raw[:], in_=wv8.rearrange("(p j) n -> p j n", j=4))
-        place(gather_scales(CH, CH + split, "picked_b"), planes_b[:, :, :split])
+        place(gather_scales(CH, 2 * CH, "picked_b"), planes_b)
         wv4 = keep.tile([P, 2 * N], U8, name="wv4", align_bytes=64)
         nc.sync.dma_start(out=wv4[:].bitcast(I32), in_=wv4_words[0].bitcast(I32))
+        wq_raw = load_weight_words(wq_words, "wq_raw", "wq_raw")
+        x_raw = []
+        for a in range(2):
+            x_raw.append(keep.tile([P, 4, M], F32, name="x_raw%d" % a, align_bytes=64))
+            nc.sync.dma_start(out=x_raw[a][:], in_=x[512 * a : 512 * (a + 1)].rearrange("(p j) m -> p j m", j=4))
         wk_s = planes_a[:, :, CH : CH + R]
         wv4_s = planes_a[:, :, CH + R :]
         col_scales = [
             [planes[:, a, first : first + CH] for a in range(2)]
-            for planes, first in ((planes_a, 0), (planes_b, 0), (planes_b, CH), (planes_b, 2 * CH))
+            for planes, first in ((planes_a, 0), (planes_b, 0), (planes_c, 0), (planes_c, CH))
         ]
-
-        xb = keep.tile([P, 2, M, 4], BF16, name="xb", tag="xb", align_bytes=64)
-        for a in range(2):
-            nc.scalar.copy(out=xb[:, a].rearrange("p (c i) t -> p c t i", i=4), in_=x_raw[a][:].rearrange("p t (c i) -> p c t i", i=4))
-        wq = keep.tile([P, 1024], I32, name="wq", align_bytes=64)
-        deal_words(wq_raw[0][:], wq[:, :512])
-        xq = keep.tile([P, 2, M], U32, name="xq", align_bytes=64)
-        xq_s = keep.tile([P, 2, M], U8, name="xq_s", align_bytes=64)
-        nc.vector.quantize_mx(
-            out=xq[:].rearrange("p a m -> p (a m)").bitcast(FP8X4),
-            scales=xq_s[:].rearrange("p a m -> p (a m)"),
-            in_=xb[:].rearrange("p a m t -> p (a m t)"),
-        )
-        place(gather_scales(CH + split, J, "xb"), planes_b[:, :, split:])
-        deal_words(wq_raw[1][:], wq[:, 512:])
+        wk = keep.tile([P, 1024], I32, name="wk", align_bytes=64)
+        deal_words(wk_raw[0][:], wk[:, :512])
+        wq_rows = keep.tile([P, R], U8, name="wq_rows", align_bytes=64)
+        deal_scales(wq_sraw, wq_rows[rows, :])
+        place(wq_rows, wq_s)
+        idle = psum.tile([P, CH], F32, name="bank", tag="bank")
+        for rep in range(4):
+            nc.tensor.matmul_mx(
+                out=idle[:], lhsT=wk[:, :64].bitcast(FP4X4), lhsT_scale=wk_sraw[:, :P],
+                rhs=wk[:, :256].bitcast(FP4X4), rhs_scale=wk_sraw[:, :CH], start=True, stop=True,
+            )
 
         def w_tile(dealt, dealt_s, a, b, t):
             u = 8 * b + 4 * a + t
@@ -172,7 +164,7 @@ def tile_list_kvt_qf_exp_kernel(
             nc.scalar.copy(out=dst, in_=bank[:].rearrange("p t j -> p j t"))
 
         def key_sums(c, b):
-            pairs = ring.tile([P, 2, 2, HALF, 2], BF16, name="pairs", bufs=4, align_bytes=64)
+            pairs = ring.tile([P, 2, 2, HALF, 2], BF16, name="pairs", bufs=5, align_bytes=64)
             for h in range(2):
                 js = slice(h * HALF, (h + 1) * HALF)
                 for u in range(2):
@@ -188,10 +180,12 @@ def tile_list_kvt_qf_exp_kernel(
                     nc.scalar.copy(out=pairs[:, h, u], in_=bank[:].rearrange("p e j -> p j e"))
             return pairs
 
-        def weave(pairs, hs=slice(0, 2), first=False):
+        def weave(pairs, hs=slice(0, 2), first=False, tag=None):
             count = hs.stop - hs.start
             if first:
                 kb = shared.tile([P, count * HALF * 4], BF16, name="kb_first", offset=4096, align_bytes=64)
+            elif tag:
+                kb = keep.tile([P, count * HALF * 4], BF16, name="kb_held", tag=tag, align_bytes=64)
             else:
                 kb = ring.tile([P, count * HALF * 4], BF16, name="kb", bufs=3, align_bytes=64)
             nc.vector.tensor_copy(
@@ -240,16 +234,8 @@ def tile_list_kvt_qf_exp_kernel(
 
         on_scalar, on_vector = nc.scalar.copy, nc.vector.tensor_copy
 
-        qb = keep.tile([P, 2, M, 4], BF16, name="qb", align_bytes=64)
-        for b in range(2):
-            for mh in range(M // P):
-                ms = slice(mh * P, (mh + 1) * P)
-                project(b, ms, qb[:, b, ms, :])
-
-        wk = keep.tile([P, 1024], I32, name="wk", align_bytes=64)
         picked = gather_words(0)
-        deal_words(wk_raw[0][:], wk[:, :512])
-        cols = [part_words(picked, keep.tile([P, 2, CH], U16, name="parted0", tag="wk_raw0", align_bytes=64), 2)]
+        cols = [part_words(picked, keep.tile([P, 2, CH], U16, name="parted0", align_bytes=64), 2)]
         deal_words(wk_raw[1][:], wk[:, 512:])
         picked = gather_words(1)
         cols.append(part_words(picked, keep.tile([P, 2, CH], U16, name="parted1", align_bytes=64)))
@@ -263,13 +249,7 @@ def tile_list_kvt_qf_exp_kernel(
         wv8q_s = keep.tile([P, N], U8, name="wv8q_s", align_bytes=64)
         nc.vector.quantize_mx(out=wv8q[:].bitcast(FP8X4), scales=wv8q_s[:], in_=wv8b[:].rearrange("p n t -> p (n t)"))
         made = {(0, 0): quantised(kb)}
-        qq = shared.tile([P, 2, M], U32, name="qq", offset=0, align_bytes=64)
-        qq_s = keep.tile([P, 2, M], U8, name="qq_s", align_bytes=64)
-        nc.vector.quantize_mx(
-            out=qq[:].rearrange("p a m -> p (a m)").bitcast(FP8X4),
-            scales=qq_s[:].rearrange("p a m -> p (a m)"),
-            in_=qb[:].rearrange("p a m t -> p (a m t)"),
-        )
+        place(gather_scales(2 * CH, J, "picked"), planes_c)
 
         def keys(c, b):
             made[c, b] = quantised(weave(key_sums(c, b), first=(c == 0)))
@@ -278,25 +258,54 @@ def tile_list_kvt_qf_exp_kernel(
             for mh in range(M // P):
                 scores(c * CH, whole([made[c, 0], made[c, 1]]), mh)
 
-        keys(0, 1)
-        keys(1, 0)
-        values(0, 0, on_scalar)
-        values(0, 1, on_vector)
-        values(0, 2, on_scalar)
-        values(0, 3, on_vector)
-        cols.append(part_words(gather_words(2), keep.tile([P, 2, CH], U16, name="parted2", align_bytes=64)))
-        keys(1, 1)
-        chunk_scores(0)
-        values(1, 0, on_vector)
-        values(1, 1, on_vector)
-        keys(2, 0)
-        values(1, 2, on_vector)
-        values(1, 3, on_vector)
-        chunk_scores(1)
-        cols.append(part_words(gather_words(3), keep.tile([P, 2, CH], U16, name="parted3", align_bytes=64)))
-        keys(2, 1)
+        pairs01 = key_sums(0, 1)
+        pairs10 = key_sums(1, 0)
+        xb = keep.tile([P, 2, M, 4], BF16, name="xb", tag="xb", align_bytes=64)
+        for a, copy in enumerate((on_scalar, on_vector)):
+            copy(out=xb[:, a].rearrange("p (c i) t -> p c t i", i=4), in_=x_raw[a][:].rearrange("p t (c i) -> p c t i", i=4))
+        wq = keep.tile([P, 1024], I32, name="wq", align_bytes=64)
+        deal_words(wq_raw[:, :, :256], wq[:, :512])
+        deal_words(wq_raw[:, :, 256:], wq[:, 512:])
         for nt in range(4):
-            values(2, nt, (on_scalar, on_vector)[nt % 2])
+            values(0, nt, on_vector)
+        xq = keep.tile([P, 2, M], U32, name="xq", align_bytes=64)
+        xq_s = keep.tile([P, 2, M], U8, name="xq_s", align_bytes=64)
+        nc.vector.quantize_mx(
+            out=xq[:].rearrange("p a m -> p (a m)").bitcast(FP8X4),
+            scales=xq_s[:].rearrange("p a m -> p (a m)"),
+            in_=xb[:].rearrange("p a m t -> p (a m t)"),
+        )
+        pairs11 = key_sums(1, 1)
+        values(1, 0, on_scalar)
+        values(1, 1, on_scalar)
+        values(1, 2, on_scalar)
+        qb = keep.tile([P, 2, M, 4], BF16, name="qb", tag="qb", align_bytes=64)
+        for b in range(2):
+            for mh in range(M // P):
+                ms = slice(mh * P, (mh + 1) * P)
+                project(b, ms, qb[:, b, ms, :])
+        cols.append(part_words(gather_words(2, "xb"), keep.tile([P, 2, CH], U16, name="parted2", align_bytes=64)))
+        made[0, 1] = quantised(weave(pairs01, tag="xb"))
+        values(1, 3, on_vector)
+        qq = keep.tile([P, 2, M], U32, name="qq", align_bytes=64)
+        qq_s = keep.tile([P, 2, M], U8, name="qq_s", align_bytes=64)
+        nc.vector.quantize_mx(
+            out=qq[:].rearrange("p a m -> p (a m)").bitcast(FP8X4),
+            scales=qq_s[:].rearrange("p a m -> p (a m)"),
+            in_=qb[:].rearrange("p a m t -> p (a m t)"),
+        )
+        pairs20 = key_sums(2, 0)
+        made[1, 0] = quantised(weave(pairs10, tag="qb"))
+        made[1, 1] = quantised(weave(pairs11, tag="qb"))
+        chunk_scores(0)
+        values(2, 0, on_vector)
+        values(2, 1, on_vector)
+        cols.append(part_words(gather_words(3, "qb"), keep.tile([P, 2, CH], U16, name="parted3", align_bytes=64)))
+        made[2, 0] = quantised(weave(pairs20))
+        keys(2, 1)
+        chunk_scores(1)
+        values(2, 2, on_vector)
+        values(2, 3, on_vector)
         keys(3, 0)
         chunk_scores(2)
         values(3, 0, on_vector)

@@ -94,14 +94,8 @@ def tile_list_kvt_qf_exp_kernel(
         nc.sync.dma_start(out=tscale[rows, :].bitcast(I32), in_=tab_scales.rearrange("a q t -> q a t").bitcast(I32))
         wk_sraw = keep.tile([P, R], U8, name="wk_sraw", align_bytes=64)
         nc.sync.dma_start(out=wk_sraw[rows, :].bitcast(I32), in_=wk_scales.rearrange("a q r -> q a r").bitcast(I32))
-        first_w = CH + R + N // 2
+        first_w = CH + R
         staged_rows = keep.tile([P, first_w], U8, name="staged_rows", align_bytes=64)
-        nc.sync.dma_start(
-            out=staged_rows[rows, CH + R :].bitcast(I32),
-            in_=wv4_scales[0].rearrange("q (h n) -> (q h) n", h=2).bitcast(I32),
-        )
-        wq_sraw = keep.tile([P, R], U8, name="wq_sraw", align_bytes=64)
-        nc.sync.dma_start(out=wq_sraw[rows, :].bitcast(I32), in_=wq_scales.rearrange("a q r -> q a r").bitcast(I32))
         table = keep.tile([P, T], U32, name="table", align_bytes=64)
         table_words = tab_words[0].rearrange("p t b -> p (t b)").bitcast(I32)
         nc.sync.dma_start(out=table[:, : T - 2 * CH].bitcast(I32), in_=table_words[:, : T - 2 * CH])
@@ -113,34 +107,41 @@ def tile_list_kvt_qf_exp_kernel(
         planes_a = zeroed_planes(first_w, "planes_a")
         planes_b = zeroed_planes(CH, "planes_b")
         planes_c = zeroed_planes(2 * CH, "planes_c")
-        wq_s = zeroed_planes(R, "wq_s")
+        planes_w = zeroed_planes(R + N // 2, "planes_w")
 
         picked_a = gather_scales(0, CH, "picked_a")
         deal_scales(wk_sraw, staged_rows[rows, CH : CH + R])
         nc.vector.tensor_copy(out=staged_rows[rows, :CH].bitcast(I32), in_=picked_a[rows, :].bitcast(I32))
         place(staged_rows, planes_a)
         wk_raw.append(load_weight_words(wk_words[:, :, R:], "wk_raw1", "wk_raw1"))
+        late_rows = keep.tile([P, R + N // 2], U8, name="late_rows", align_bytes=64)
+        wq_sraw = keep.tile([P, R], U8, name="wq_sraw", align_bytes=64)
+        nc.sync.dma_start(out=wq_sraw[rows, :].bitcast(I32), in_=wq_scales.rearrange("a q r -> q a r").bitcast(I32))
+        nc.sync.dma_start(
+            out=late_rows[rows, R:].bitcast(I32),
+            in_=wv4_scales[0].rearrange("q (h n) -> (q h) n", h=2).bitcast(I32),
+        )
         wv8_raw = shared.tile([P, 4, N], F32, name="wv8_raw", offset=0, align_bytes=64)
         nc.sync.dma_start(out=wv8_raw[:], in_=wv8.rearrange("(p j) n -> p j n", j=4))
         place(gather_scales(CH, 2 * CH, "picked_b"), planes_b)
         wv4 = keep.tile([P, 2 * N], U8, name="wv4", align_bytes=64)
         nc.sync.dma_start(out=wv4[:].bitcast(I32), in_=wv4_words[0].bitcast(I32))
+        deal_scales(wq_sraw, late_rows[rows, :R])
+        place(late_rows, planes_w)
         wq_raw = load_weight_words(wq_words, "wq_raw", "wq_raw")
         x_raw = []
         for a in range(2):
             x_raw.append(keep.tile([P, 4, M], F32, name="x_raw%d" % a, align_bytes=64))
             nc.sync.dma_start(out=x_raw[a][:], in_=x[512 * a : 512 * (a + 1)].rearrange("(p j) m -> p j m", j=4))
         wk_s = planes_a[:, :, CH : CH + R]
-        wv4_s = planes_a[:, :, CH + R :]
+        wq_s = planes_w[:, :, :R]
+        wv4_s = planes_w[:, :, R:]
         col_scales = [
             [planes[:, a, first : first + CH] for a in range(2)]
             for planes, first in ((planes_a, 0), (planes_b, 0), (planes_c, 0), (planes_c, CH))
         ]
         wk = keep.tile([P, 1024], I32, name="wk", align_bytes=64)
         deal_words(wk_raw[0][:], wk[:, :512])
-        wq_rows = keep.tile([P, R], U8, name="wq_rows", align_bytes=64)
-        deal_scales(wq_sraw, wq_rows[rows, :])
-        place(wq_rows, wq_s)
         idle = psum.tile([P, CH], F32, name="bank", tag="bank")
         for rep in range(4):
             nc.tensor.matmul_mx(
@@ -267,7 +268,7 @@ def tile_list_kvt_qf_exp_kernel(
         deal_words(wq_raw[:, :, :256], wq[:, :512])
         deal_words(wq_raw[:, :, 256:], wq[:, 512:])
         for nt in range(4):
-            values(0, nt, on_vector)
+            values(0, nt, (on_scalar, on_vector)[nt % 2])
         xq = keep.tile([P, 2, M], U32, name="xq", align_bytes=64)
         xq_s = keep.tile([P, 2, M], U8, name="xq_s", align_bytes=64)
         nc.vector.quantize_mx(
@@ -286,7 +287,7 @@ def tile_list_kvt_qf_exp_kernel(
                 project(b, ms, qb[:, b, ms, :])
         cols.append(part_words(gather_words(2, "xb"), keep.tile([P, 2, CH], U16, name="parted2", align_bytes=64)))
         made[0, 1] = quantised(weave(pairs01, tag="xb"))
-        values(1, 3, on_vector)
+        values(1, 3, on_scalar)
         qq = keep.tile([P, 2, M], U32, name="qq", align_bytes=64)
         qq_s = keep.tile([P, 2, M], U8, name="qq_s", align_bytes=64)
         nc.vector.quantize_mx(
@@ -298,13 +299,13 @@ def tile_list_kvt_qf_exp_kernel(
         made[1, 0] = quantised(weave(pairs10, tag="qb"))
         made[1, 1] = quantised(weave(pairs11, tag="qb"))
         chunk_scores(0)
-        values(2, 0, on_vector)
-        values(2, 1, on_vector)
+        values(2, 0, on_scalar)
+        values(2, 1, on_scalar)
         cols.append(part_words(gather_words(3, "qb"), keep.tile([P, 2, CH], U16, name="parted3", align_bytes=64)))
         made[2, 0] = quantised(weave(pairs20))
         keys(2, 1)
         chunk_scores(1)
-        values(2, 2, on_vector)
+        values(2, 2, on_scalar)
         values(2, 3, on_vector)
         keys(3, 0)
         chunk_scores(2)

@@ -16,11 +16,16 @@ FP4X4 = mybir.dt.float4_e2m1fn_x4
 EXP = mybir.ActivationFunctionType.Exp
 
 P = 128
-rows = slice(96, 128)
+ROWS = slice(96, 128)
 CH = 512
-NCH = J // CH
 HALF = CH // 2
 SCORE_SCALE = 0.015625
+
+WV8_RAW_AT = 0
+XB_AT = 8192
+X_RAW_AT = 16384
+WOVEN_BYTES = 4096
+OVERLAP = 64
 
 
 def tile_list_kvt_qf_exp_kernel(
@@ -34,9 +39,14 @@ def tile_list_kvt_qf_exp_kernel(
         outs = ctx.enter_context(tc.tile_pool(name="outs", bufs=8))
         psum = ctx.enter_context(tc.psum_pool(name="psum", bufs=8))
 
-        def load_weight_words(words, name, tag):
-            raw = keep.tile([P, 2, words.shape[2] // 4], I32, name=name, tag=tag, align_bytes=64)
+        def load_weight_words(words, name):
+            raw = keep.tile([P, 2, words.shape[2] // 4], I32, name=name, align_bytes=64)
             nc.sync.dma_start(out=raw[:], in_=words.rearrange("a p n -> p a n").bitcast(I32))
+            return raw
+
+        def load_scale_rows(scales, name):
+            raw = keep.tile([P, scales.shape[2]], U8, name=name, align_bytes=64)
+            nc.sync.dma_start(out=raw[ROWS, :].bitcast(I32), in_=scales.rearrange("a q n -> q a n").bitcast(I32))
             return raw
 
         def deal_words(raw, dst):
@@ -48,7 +58,7 @@ def tile_list_kvt_qf_exp_kernel(
         def deal_scales(raw, dst):
             nc.vector.tensor_copy(
                 out=dst.bitcast(I32).rearrange("p (b t g w) -> p b t g w", b=2, t=4, g=16),
-                in_=raw[rows, :].bitcast(I32).rearrange("p (b g t w) -> p b t g w", b=2, t=4, g=16),
+                in_=raw[ROWS, :].bitcast(I32).rearrange("p (b g t w) -> p b t g w", b=2, t=4, g=16),
             )
 
         def place(staged, planes):
@@ -62,21 +72,15 @@ def tile_list_kvt_qf_exp_kernel(
             nc.vector.memset(planes[:].rearrange("p a n -> p (a n)").bitcast(I32), 0)
             return planes
 
-        def gather_words(c, tag="picked"):
-            picked = keep.tile([P, CH], U32, name="picked", tag=tag, align_bytes=64)
-            nc.vector.tensor_copy(out=picked[:], in_=table[:].indirect(offsets[:, c * 32 : (c + 1) * 32]))
+        def gather_words(c, picked):
+            nc.vector.tensor_copy(out=picked[:], in_=table[:].indirect(offsets[:, c * CH // 16 : (c + 1) * CH // 16]))
             return picked
 
-        def part_words(picked, parted, pieces=1):
-            halves = picked[:].bitcast(U16).rearrange("p (j d) -> p d j", d=2)
-            width = CH // pieces
-            for h in range(pieces):
-                js = slice(h * width, (h + 1) * width)
-                if pieces == 1:
-                    nc.vector.tensor_copy(out=parted[:], in_=halves)
-                else:
-                    for a in range(2):
-                        nc.vector.tensor_copy(out=parted[:, a, js], in_=halves[:, a, js])
+        def by_pass(picked):
+            return picked[:].bitcast(U16).rearrange("p (j a) -> p a j", a=2)
+
+        def part_words(picked, parted):
+            nc.vector.tensor_copy(out=parted[:], in_=by_pass(picked))
             return parted
 
         def gather_scales(j0, j1, tag):
@@ -84,70 +88,58 @@ def tile_list_kvt_qf_exp_kernel(
             nc.vector.tensor_copy(out=picked[:], in_=tscale[:].indirect(offsets[:, j0 // 16 : j1 // 16]))
             return picked
 
+        def quantise(grouped, codes, scales):
+            nc.vector.quantize_mx(out=codes.bitcast(FP8X4), scales=scales, in_=grouped)
 
         warm = keep.tile([P, 2], F32, name="warm")
         nc.vector.memset(warm[:, 0:1], 0.0)
         nc.scalar.activation(out=warm[:, 1:2], in_=warm[:, 0:1], func=EXP)
+
         offsets = keep.tile([P, J // 16], U16, name="offsets")
         nc.sync.dma_start(offsets[:], offs)
-        tscale = keep.tile([P, T], U8, name="tscale", align_bytes=64)
-        nc.sync.dma_start(out=tscale[rows, :].bitcast(I32), in_=tab_scales.rearrange("a q t -> q a t").bitcast(I32))
-        wk_sraw = keep.tile([P, R], U8, name="wk_sraw", align_bytes=64)
-        nc.sync.dma_start(out=wk_sraw[rows, :].bitcast(I32), in_=wk_scales.rearrange("a q r -> q a r").bitcast(I32))
-        first_w = CH + R
-        staged_rows = keep.tile([P, first_w], U8, name="staged_rows", align_bytes=64)
-        table = keep.tile([P, T], U32, name="table", align_bytes=64)
-        table_words = tab_words[0].rearrange("p t b -> p (t b)").bitcast(I32)
-        nc.sync.dma_start(out=table[:, : T - 2 * CH].bitcast(I32), in_=table_words[:, : T - 2 * CH])
-        wk_raw = [load_weight_words(wk_words[:, :, :R], "wk_raw0", "wk_raw0")]
-        nc.sync.dma_start(out=table[:, T - 2 * CH :].bitcast(I32), in_=table_words[:, T - 2 * CH :])
-
-        nc.vector.memset(tscale[0:96, :].bitcast(I32), 0)
-        nc.vector.memset(wk_sraw[0:96, :].bitcast(I32), 0)
-        planes_a = zeroed_planes(first_w, "planes_a")
-        planes_b = zeroed_planes(CH, "planes_b")
-        planes_c = zeroed_planes(2 * CH, "planes_c")
-        planes_w = zeroed_planes(R + N // 2, "planes_w")
-
-        picked_a = gather_scales(0, CH, "picked_a")
-        deal_scales(wk_sraw, staged_rows[rows, CH : CH + R])
-        nc.vector.tensor_copy(out=staged_rows[rows, :CH].bitcast(I32), in_=picked_a[rows, :].bitcast(I32))
-        place(staged_rows, planes_a)
-        wk_raw.append(load_weight_words(wk_words[:, :, R:], "wk_raw1", "wk_raw1"))
+        tscale = load_scale_rows(tab_scales, "tscale")
+        wk_sraw = load_scale_rows(wk_scales, "wk_sraw")
+        first_rows = keep.tile([P, CH + R], U8, name="first_rows", align_bytes=64)
         late_rows = keep.tile([P, R + N // 2], U8, name="late_rows", align_bytes=64)
-        wq_sraw = keep.tile([P, R], U8, name="wq_sraw", align_bytes=64)
-        nc.sync.dma_start(out=wq_sraw[rows, :].bitcast(I32), in_=wq_scales.rearrange("a q r -> q a r").bitcast(I32))
+        wq_sraw = load_scale_rows(wq_scales, "wq_sraw")
         nc.sync.dma_start(
-            out=late_rows[rows, R:].bitcast(I32),
+            out=late_rows[ROWS, R:].bitcast(I32),
             in_=wv4_scales[0].rearrange("q (h n) -> (q h) n", h=2).bitcast(I32),
         )
-        wv8_raw = shared.tile([P, 4, N], F32, name="wv8_raw", offset=0, align_bytes=64)
-        nc.sync.dma_start(out=wv8_raw[:], in_=wv8.rearrange("(p j) n -> p j n", j=4))
-        place(gather_scales(CH, 2 * CH, "picked_b"), planes_b)
+        wk_raw = [load_weight_words(wk_words[:, :, :R], "wk_raw0")]
+        table = keep.tile([P, T], U32, name="table", align_bytes=64)
+        nc.sync.dma_start(out=table[:].bitcast(I32), in_=tab_words[0].rearrange("p t b -> p (t b)").bitcast(I32))
+
+        nc.vector.memset(tscale[: ROWS.start, :].bitcast(I32), 0)
+        planes_first = zeroed_planes(CH + R, "planes_first")
+        planes_second = zeroed_planes(CH, "planes_second")
+        planes_rest = zeroed_planes(2 * CH, "planes_rest")
+        planes_late = zeroed_planes(R + N // 2, "planes_late")
+
+        picked_first = gather_scales(0, CH, "picked_first")
+        deal_scales(wk_sraw, first_rows[ROWS, CH:])
+        nc.vector.tensor_copy(out=first_rows[ROWS, :CH].bitcast(I32), in_=picked_first[ROWS, :].bitcast(I32))
+        place(first_rows, planes_first)
+        wk_raw.append(load_weight_words(wk_words[:, :, R:], "wk_raw1"))
+        wv8_raw = shared.tile([P, 4, N], F32, name="wv8_raw", offset=WV8_RAW_AT, align_bytes=64)
+        nc.sync.dma_start(out=wv8_raw[:], in_=wv8.rearrange("(p t) n -> p t n", t=4))
+        place(gather_scales(CH, 2 * CH, "picked_second"), planes_second)
         wv4 = keep.tile([P, 2 * N], U8, name="wv4", align_bytes=64)
         nc.sync.dma_start(out=wv4[:].bitcast(I32), in_=wv4_words[0].bitcast(I32))
-        deal_scales(wq_sraw, late_rows[rows, :R])
-        place(late_rows, planes_w)
-        wq_raw = load_weight_words(wq_words, "wq_raw", "wq_raw")
-        x_raw = []
-        for a in range(2):
-            x_raw.append(keep.tile([P, 4, M], F32, name="x_raw%d" % a, align_bytes=64))
-            nc.sync.dma_start(out=x_raw[a][:], in_=x[512 * a : 512 * (a + 1)].rearrange("(p j) m -> p j m", j=4))
-        wk_s = planes_a[:, :, CH : CH + R]
-        wq_s = planes_w[:, :, :R]
-        wv4_s = planes_w[:, :, R:]
+        deal_scales(wq_sraw, late_rows[ROWS, :R])
+        place(late_rows, planes_late)
+        wq_raw = load_weight_words(wq_words, "wq_raw")
+        x_raw = shared.tile([P, 2, 4, M], F32, name="x_raw", offset=X_RAW_AT, align_bytes=64)
+        nc.sync.dma_start(out=x_raw[:], in_=x.rearrange("(a p t) m -> p a t m", a=2, t=4))
+        wk_s = planes_first[:, :, CH:]
+        wq_s = planes_late[:, :, :R]
+        wv4_s = planes_late[:, :, R:]
         col_scales = [
             [planes[:, a, first : first + CH] for a in range(2)]
-            for planes, first in ((planes_a, 0), (planes_b, 0), (planes_c, 0), (planes_c, CH))
+            for planes, first in ((planes_first, 0), (planes_second, 0), (planes_rest, 0), (planes_rest, CH))
         ]
         wk = keep.tile([P, 1024], I32, name="wk", align_bytes=64)
         deal_words(wk_raw[0][:], wk[:, :512])
-        idle = psum.tile([P, CH], F32, name="bank", tag="bank")
-        for rep in range(4):
-            nc.tensor.matmul_mx(
-                out=idle[:], lhsT=wk[:, :64].bitcast(FP4X4), lhsT_scale=wk_sraw[:, :P],
-                rhs=wk[:, :256].bitcast(FP4X4), rhs_scale=wk_sraw[:, :CH], start=True, stop=True,
-            )
 
         def w_tile(dealt, dealt_s, a, b, t):
             u = 8 * b + 4 * a + t
@@ -162,7 +154,7 @@ def tile_list_kvt_qf_exp_kernel(
                         out=bank[:, t, :], lhsT=lhs, lhsT_scale=lhs_s, rhs=xq[:, a, ms].bitcast(FP8X4), rhs_scale=xq_s[:, a, ms],
                         start=(a == 0), stop=(a == 1),
                     )
-            nc.scalar.copy(out=dst, in_=bank[:].rearrange("p t j -> p j t"))
+            nc.scalar.copy(out=dst, in_=bank[:].rearrange("p t m -> p m t"))
 
         def key_sums(c, b):
             pairs = ring.tile([P, 2, 2, HALF, 2], BF16, name="pairs", bufs=5, align_bytes=64)
@@ -181,28 +173,24 @@ def tile_list_kvt_qf_exp_kernel(
                     nc.scalar.copy(out=pairs[:, h, u], in_=bank[:].rearrange("p e j -> p j e"))
             return pairs
 
-        def weave(pairs, hs=slice(0, 2), first=False, tag=None):
+        def weave(pairs, woven=None, hs=slice(0, 2)):
             count = hs.stop - hs.start
-            if first:
-                kb = shared.tile([P, count * HALF * 4], BF16, name="kb_first", offset=4096, align_bytes=64)
-            elif tag:
-                kb = keep.tile([P, count * HALF * 4], BF16, name="kb_held", tag=tag, align_bytes=64)
-            else:
-                kb = ring.tile([P, count * HALF * 4], BF16, name="kb", bufs=3, align_bytes=64)
+            if woven is None:
+                woven = ring.tile([P, count * HALF * 4], BF16, name="woven", bufs=3, align_bytes=64)
             nc.vector.tensor_copy(
-                out=kb[:].bitcast(I32).rearrange("p (h j u) -> p h j u", h=count, u=2),
+                out=woven[:].bitcast(I32).rearrange("p (h j u) -> p h j u", h=count, u=2),
                 in_=pairs[:].rearrange("p h u j e -> p (h u j e)").bitcast(I32).rearrange("p (h u j) -> p h j u", h=2, u=2)[:, hs],
             )
-            return kb
+            return woven
 
-        def quantised(kb):
-            width = kb.shape[1] // 4
+        def quantised_keys(woven):
+            width = woven.shape[1] // 4
             kq = ring.tile([P, width], U32, name="kq", bufs=7, align_bytes=64)
             kq_s = ring.tile([P, width], U8, name="kq_s", bufs=7, align_bytes=64)
-            nc.vector.quantize_mx(out=kq[:].bitcast(FP8X4), scales=kq_s[:], in_=kb[:])
+            quantise(woven[:], kq[:], kq_s[:])
             return kq, kq_s
 
-        def values(c, nt, copy):
+        def values(c, nt, copy, staged=None):
             ns = slice(nt * P, (nt + 1) * P)
             bank = psum.tile([P, CH], F32, name="bank", tag="bank")
             nc.tensor.matmul_mx(
@@ -210,112 +198,114 @@ def tile_list_kvt_qf_exp_kernel(
                 rhs=cols[c][:, 0, :].bitcast(FP4X4), rhs_scale=col_scales[c][0], start=True, stop=False,
             )
             nc.tensor.matmul_mx(
-                out=bank[:], lhsT=wv4[:, 2 * nt * P : 2 * (nt + 1) * P].bitcast(FP4X4), lhsT_scale=wv4_s[:, nt // 2, (nt % 2) * P : (nt % 2 + 1) * P],
+                out=bank[:], lhsT=wv4[:, 2 * nt * P : 2 * (nt + 1) * P].bitcast(FP4X4),
+                lhsT_scale=wv4_s[:, nt // 2, (nt % 2) * P : (nt % 2 + 1) * P],
                 rhs=cols[c][:, 1, :].bitcast(FP4X4), rhs_scale=col_scales[c][1], start=False, stop=True,
             )
-            staged = outs.tile([P, CH], F32, name="staged", tag="staged")
+            if staged is None:
+                staged = outs.tile([P, CH], F32, name="staged", tag="staged")
             copy(out=staged[:], in_=bank[:])
             nc.sync.dma_start(out=out_1[ns, c * CH : (c + 1) * CH], in_=staged[:])
 
-        def scores(first, made, mh):
+        def scores(first, operands, mh):
             ms = slice(mh * P, (mh + 1) * P)
-            width = made[0][1].shape[1]
+            width = operands[0][1].shape[1]
             bank = psum.tile([P, width], F32, name="bank", tag="bank")
             for b in range(2):
                 nc.tensor.matmul_mx(
                     out=bank[:], lhsT=qq[:, b, ms].bitcast(FP8X4), lhsT_scale=qq_s[:, b, ms],
-                    rhs=made[b][0].bitcast(FP8X4), rhs_scale=made[b][1], start=(b == 0), stop=(b == 1),
+                    rhs=operands[b][0].bitcast(FP8X4), rhs_scale=operands[b][1], start=(b == 0), stop=(b == 1),
                 )
             staged = outs.tile([P, width], F32, name="staged", tag="staged")
             nc.scalar.activation(out=staged[:], in_=bank[:], func=EXP, scale=SCORE_SCALE)
             nc.sync.dma_start(out=out_0[ms, first : first + width], in_=staged[:])
 
-        def whole(made):
-            return [(kq[:], kq_s[:]) for kq, kq_s in made]
+        def chunk_scores(c):
+            for mh in range(M // P):
+                scores(c * CH, [(kq[:], kq_s[:]) for kq, kq_s in (keys[c, 0], keys[c, 1])], mh)
 
         on_scalar, on_vector = nc.scalar.copy, nc.vector.tensor_copy
 
-        picked = gather_words(0)
-        cols = [part_words(picked, keep.tile([P, 2, CH], U16, name="parted0", align_bytes=64), 2)]
+        picked = gather_words(0, keep.tile([P, CH], U32, name="picked0", tag="picked", align_bytes=64))
+        cols = [keep.tile([P, 2, CH], U16, name="parted0", align_bytes=64)]
+        for h in range(2):
+            for a in range(2):
+                js = slice(h * HALF, (h + 1) * HALF)
+                nc.vector.tensor_copy(out=cols[0][:, a, js], in_=by_pass(picked)[:, a, js])
         deal_words(wk_raw[1][:], wk[:, 512:])
-        picked = gather_words(1)
-        cols.append(part_words(picked, keep.tile([P, 2, CH], U16, name="parted1", align_bytes=64)))
-        pairs = key_sums(0, 0)
-        wv8b = keep.tile([P, N, 4], BF16, name="wv8b", tag="picked", align_bytes=64)
+        picked = gather_words(1, keep.tile([P, CH], U32, name="picked1", tag="picked", align_bytes=64))
+        wv8b = keep.tile([P, N, 4], BF16, name="wv8b", align_bytes=64)
         nc.vector.tensor_copy(
             out=wv8b[:].rearrange("p (c i) t -> p c t i", i=4), in_=wv8_raw[:].rearrange("p t (c i) -> p c t i", i=4)
         )
-        kb = weave(pairs, first=True)
+        cols.append(part_words(picked, shared.tile([P, 2, CH], U16, name="parted1", offset=WV8_RAW_AT, align_bytes=64)))
         wv8q = keep.tile([P, N], U32, name="wv8q", align_bytes=64)
         wv8q_s = keep.tile([P, N], U8, name="wv8q_s", align_bytes=64)
-        nc.vector.quantize_mx(out=wv8q[:].bitcast(FP8X4), scales=wv8q_s[:], in_=wv8b[:].rearrange("p n t -> p (n t)"))
-        made = {(0, 0): quantised(kb)}
-        place(gather_scales(2 * CH, J, "picked"), planes_c)
+        quantise(wv8b[:].rearrange("p n t -> p (n t)"), wv8q[:], wv8q_s[:])
+        place(gather_scales(2 * CH, J, "picked"), planes_rest)
 
-        def keys(c, b):
-            made[c, b] = quantised(weave(key_sums(c, b), first=(c == 0)))
-
-        def chunk_scores(c):
-            for mh in range(M // P):
-                scores(c * CH, whole([made[c, 0], made[c, 1]]), mh)
-
+        pairs00 = key_sums(0, 0)
         pairs01 = key_sums(0, 1)
         pairs10 = key_sums(1, 0)
-        xb = keep.tile([P, 2, M, 4], BF16, name="xb", tag="xb", align_bytes=64)
-        for a, copy in enumerate((on_scalar, on_vector)):
-            copy(out=xb[:, a].rearrange("p (c i) t -> p c t i", i=4), in_=x_raw[a][:].rearrange("p t (c i) -> p c t i", i=4))
+        xb = shared.tile([P, 2, M, 4], BF16, name="xb", offset=XB_AT, align_bytes=64)
+        nc.vector.tensor_copy(
+            out=xb[:].rearrange("p a (c i) t -> p a c t i", i=4), in_=x_raw[:].rearrange("p a t (c i) -> p a c t i", i=4)
+        )
         wq = keep.tile([P, 1024], I32, name="wq", align_bytes=64)
         deal_words(wq_raw[:, :, :256], wq[:, :512])
         deal_words(wq_raw[:, :, 256:], wq[:, 512:])
-        for nt in range(4):
-            values(0, nt, (on_scalar, on_vector)[nt % 2])
         xq = keep.tile([P, 2, M], U32, name="xq", align_bytes=64)
         xq_s = keep.tile([P, 2, M], U8, name="xq_s", align_bytes=64)
-        nc.vector.quantize_mx(
-            out=xq[:].rearrange("p a m -> p (a m)").bitcast(FP8X4),
-            scales=xq_s[:].rearrange("p a m -> p (a m)"),
-            in_=xb[:].rearrange("p a m t -> p (a m t)"),
-        )
+        quantise(xb[:].rearrange("p a m t -> p (a m t)"), xq[:].rearrange("p a m -> p (a m)"), xq_s[:].rearrange("p a m -> p (a m)"))
+        for i in range(2):
+            values(0, 2 * i, on_scalar)
+            values(0, 2 * i + 1, on_vector, shared.tile([P, CH], F32, name="staged_x%d" % i, offset=X_RAW_AT + 4096 * i, align_bytes=64))
         pairs11 = key_sums(1, 1)
-        values(1, 0, on_scalar)
-        values(1, 1, on_scalar)
-        values(1, 2, on_scalar)
+        for nt in range(3):
+            values(1, nt, on_scalar)
         qb = keep.tile([P, 2, M, 4], BF16, name="qb", tag="qb", align_bytes=64)
         for b in range(2):
             for mh in range(M // P):
                 ms = slice(mh * P, (mh + 1) * P)
                 project(b, ms, qb[:, b, ms, :])
-        cols.append(part_words(gather_words(2, "xb"), keep.tile([P, 2, CH], U16, name="parted2", align_bytes=64)))
-        made[0, 1] = quantised(weave(pairs01, tag="xb"))
+
+        def woven_over_xb(name, offset):
+            return shared.tile([P, 4 * CH], BF16, name=name, offset=offset, align_bytes=64)
+
+        above, below = XB_AT + WOVEN_BYTES - OVERLAP, XB_AT - WOVEN_BYTES + OVERLAP
+        picked = gather_words(2, shared.tile([P, CH], U32, name="picked2", offset=XB_AT, align_bytes=64))
+        woven00 = weave(pairs00, woven_over_xb("woven_above", above))
+        cols.append(part_words(picked, keep.tile([P, 2, CH], U16, name="parted2", align_bytes=64)))
+        keys = {(0, 0): quantised_keys(woven00)}
+        keys[0, 1] = quantised_keys(weave(pairs01, woven_over_xb("woven_below", below)))
+        keys[1, 1] = quantised_keys(weave(pairs11, woven_over_xb("woven_above", above)))
         values(1, 3, on_scalar)
         qq = keep.tile([P, 2, M], U32, name="qq", align_bytes=64)
         qq_s = keep.tile([P, 2, M], U8, name="qq_s", align_bytes=64)
-        nc.vector.quantize_mx(
-            out=qq[:].rearrange("p a m -> p (a m)").bitcast(FP8X4),
-            scales=qq_s[:].rearrange("p a m -> p (a m)"),
-            in_=qb[:].rearrange("p a m t -> p (a m t)"),
-        )
+        quantise(qb[:].rearrange("p b m t -> p (b m t)"), qq[:].rearrange("p b m -> p (b m)"), qq_s[:].rearrange("p b m -> p (b m)"))
+
         pairs20 = key_sums(2, 0)
-        made[1, 0] = quantised(weave(pairs10, tag="qb"))
-        made[1, 1] = quantised(weave(pairs11, tag="qb"))
+        keys[1, 0] = quantised_keys(weave(pairs10, keep.tile([P, 4 * CH], BF16, name="woven10", tag="qb", align_bytes=64)))
         chunk_scores(0)
         values(2, 0, on_scalar)
         values(2, 1, on_scalar)
-        cols.append(part_words(gather_words(3, "qb"), keep.tile([P, 2, CH], U16, name="parted3", align_bytes=64)))
-        made[2, 0] = quantised(weave(pairs20))
-        keys(2, 1)
+        picked = gather_words(3, keep.tile([P, CH], U32, name="picked3", tag="qb", align_bytes=64))
+        cols.append(part_words(picked, keep.tile([P, 2, CH], U16, name="parted3", align_bytes=64)))
+        keys[2, 0] = quantised_keys(weave(pairs20))
+        keys[2, 1] = quantised_keys(weave(key_sums(2, 1)))
         chunk_scores(1)
         values(2, 2, on_scalar)
         values(2, 3, on_vector)
-        keys(3, 0)
+        keys[3, 0] = quantised_keys(weave(key_sums(3, 0)))
         chunk_scores(2)
-        values(3, 0, on_vector)
+        values(3, 0, on_scalar)
         values(3, 1, on_vector)
-        pairs = key_sums(3, 1)
-        last = [quantised(weave(pairs, slice(h, h + 1))) for h in range(2)]
+
+        pairs31 = key_sums(3, 1)
+        last = [quantised_keys(weave(pairs31, hs=slice(h, h + 1))) for h in range(2)]
         values(3, 2, on_scalar)
         values(3, 3, on_vector)
         for h in range(2):
             js = slice(h * HALF, (h + 1) * HALF)
             for mh in range(M // P):
-                scores(3 * CH + h * HALF, [(made[3, 0][0][:, js], made[3, 0][1][:, js]), (last[h][0][:], last[h][1][:])], mh)
+                scores(3 * CH + h * HALF, [(keys[3, 0][0][:, js], keys[3, 0][1][:, js]), (last[h][0][:], last[h][1][:])], mh)

@@ -20,6 +20,7 @@ ROWS = slice(96, 128)
 CH = 512
 HALF = CH // 2
 SCORE_SCALE = 0.015625
+WARM_PASSES = 4
 
 WV8_RAW_AT = 0
 XB_AT = 8192
@@ -225,6 +226,13 @@ def tile_list_kvt_qf_exp_kernel(
                 scores(c * CH, [(kq[:], kq_s[:]) for kq, kq_s in (keys[c, 0], keys[c, 1])], mh)
 
         on_scalar, on_vector = nc.scalar.copy, nc.vector.tensor_copy
+
+        idle = psum.tile([P, CH], F32, name="bank", tag="bank")
+        for i in range(WARM_PASSES):
+            nc.tensor.matmul_mx(
+                out=idle[:], lhsT=wk[:, :64].bitcast(FP4X4), lhsT_scale=picked_first[:, :P],
+                rhs=table[:, : CH // 2].bitcast(FP4X4), rhs_scale=picked_first[:], start=(i == 0), stop=(i == WARM_PASSES - 1),
+            )
 
         picked = gather_words(0, keep.tile([P, CH], U32, name="picked0", tag="picked", align_bytes=64))
         cols = [keep.tile([P, 2, CH], U16, name="parted0", align_bytes=64)]

@@ -20,6 +20,7 @@ ROWS = slice(96, 128)
 CH = 512
 HALF = CH // 2
 SCORE_SCALE = 0.015625
+ALIGN = 256
 WARM_PASSES = 4
 
 WV8_RAW_AT = 0
@@ -41,12 +42,12 @@ def tile_list_kvt_qf_exp_kernel(
         psum = ctx.enter_context(tc.psum_pool(name="psum", bufs=8))
 
         def load_weight_words(words, name):
-            raw = keep.tile([P, 2, words.shape[2] // 4], I32, name=name, align_bytes=64)
+            raw = keep.tile([P, 2, words.shape[2] // 4], I32, name=name, align_bytes=ALIGN)
             nc.sync.dma_start(out=raw[:], in_=words.rearrange("a p n -> p a n").bitcast(I32))
             return raw
 
         def load_scale_rows(scales, name):
-            raw = keep.tile([P, scales.shape[2]], U8, name=name, align_bytes=64)
+            raw = keep.tile([P, scales.shape[2]], U8, name=name, align_bytes=ALIGN)
             nc.sync.dma_start(out=raw[ROWS, :].bitcast(I32), in_=scales.rearrange("a q n -> q a n").bitcast(I32))
             return raw
 
@@ -68,8 +69,8 @@ def tile_list_kvt_qf_exp_kernel(
                     out=planes[32 * q : 32 * q + 4].bitcast(I32), in_=staged[96 + 8 * q : 104 + 8 * q, :].bitcast(I32)
                 )
 
-        def zeroed_planes(width, name):
-            planes = keep.tile([P, 2, width], U8, name=name, align_bytes=64)
+        def zeroed_planes(width, name, tag):
+            planes = keep.tile([P, 2, width], U8, name=name, tag=tag, align_bytes=ALIGN)
             nc.vector.memset(planes[:].rearrange("p a n -> p (a n)").bitcast(I32), 0)
             return planes
 
@@ -85,7 +86,7 @@ def tile_list_kvt_qf_exp_kernel(
             return parted
 
         def gather_scales(j0, j1, tag):
-            picked = keep.tile([P, j1 - j0], U8, name="picked_scales%d" % j0, tag=tag, align_bytes=64)
+            picked = keep.tile([P, j1 - j0], U8, name="picked_scales%d" % j0, tag=tag, align_bytes=ALIGN)
             nc.vector.tensor_copy(out=picked[:], in_=tscale[:].indirect(offsets[:, j0 // 16 : j1 // 16]))
             return picked
 
@@ -100,37 +101,37 @@ def tile_list_kvt_qf_exp_kernel(
         nc.sync.dma_start(offsets[:], offs)
         tscale = load_scale_rows(tab_scales, "tscale")
         wk_sraw = load_scale_rows(wk_scales, "wk_sraw")
-        first_rows = keep.tile([P, CH + R], U8, name="first_rows", align_bytes=64)
-        late_rows = keep.tile([P, R + N // 2], U8, name="late_rows", align_bytes=64)
+        first_rows = keep.tile([P, CH + R], U8, name="first_rows", align_bytes=ALIGN)
+        late_rows = keep.tile([P, R + N // 2], U8, name="late_rows", align_bytes=ALIGN)
         wq_sraw = load_scale_rows(wq_scales, "wq_sraw")
         nc.sync.dma_start(
             out=late_rows[ROWS, R:].bitcast(I32),
             in_=wv4_scales[0].rearrange("q (h n) -> (q h) n", h=2).bitcast(I32),
         )
         wk_raw = [load_weight_words(wk_words[:, :, :R], "wk_raw0")]
-        table = keep.tile([P, T], U32, name="table", align_bytes=64)
+        table = keep.tile([P, T], U32, name="table", align_bytes=ALIGN)
         nc.sync.dma_start(out=table[:].bitcast(I32), in_=tab_words[0].rearrange("p t b -> p (t b)").bitcast(I32))
 
         nc.vector.memset(tscale[: ROWS.start, :].bitcast(I32), 0)
-        planes_first = zeroed_planes(CH + R, "planes_first")
-        planes_second = zeroed_planes(CH, "planes_second")
-        planes_rest = zeroed_planes(2 * CH, "planes_rest")
-        planes_late = zeroed_planes(R + N // 2, "planes_late")
+        planes_first = zeroed_planes(CH + R, "planes_first", "planes_first")
+        planes_rest = zeroed_planes(2 * CH, "planes_rest", "planes_rest")
 
         picked_first = gather_scales(0, CH, "picked_first")
         deal_scales(wk_sraw, first_rows[ROWS, CH:])
         nc.vector.tensor_copy(out=first_rows[ROWS, :CH].bitcast(I32), in_=picked_first[ROWS, :].bitcast(I32))
         place(first_rows, planes_first)
         wk_raw.append(load_weight_words(wk_words[:, :, R:], "wk_raw1"))
-        wv8_raw = shared.tile([P, 4, N], F32, name="wv8_raw", offset=WV8_RAW_AT, align_bytes=64)
+        wv8_raw = shared.tile([P, 4, N], F32, name="wv8_raw", offset=WV8_RAW_AT, align_bytes=ALIGN)
         nc.sync.dma_start(out=wv8_raw[:], in_=wv8.rearrange("(p t) n -> p t n", t=4))
-        place(gather_scales(CH, 2 * CH, "picked_second"), planes_second)
-        wv4 = keep.tile([P, 2 * N], U8, name="wv4", align_bytes=64)
+        planes_second = zeroed_planes(CH, "planes_second", "picked_first")
+        place(gather_scales(CH, 2 * CH, "wk_sraw"), planes_second)
+        wv4 = keep.tile([P, 2 * N], U8, name="wv4", align_bytes=ALIGN)
         nc.sync.dma_start(out=wv4[:].bitcast(I32), in_=wv4_words[0].bitcast(I32))
         deal_scales(wq_sraw, late_rows[ROWS, :R])
+        planes_late = zeroed_planes(R + N // 2, "planes_late", "wq_sraw")
         place(late_rows, planes_late)
         wq_raw = load_weight_words(wq_words, "wq_raw")
-        x_raw = shared.tile([P, 2, 4, M], F32, name="x_raw", offset=X_RAW_AT, align_bytes=64)
+        x_raw = shared.tile([P, 2, 4, M], F32, name="x_raw", offset=X_RAW_AT, align_bytes=ALIGN)
         nc.sync.dma_start(out=x_raw[:], in_=x.rearrange("(a p t) m -> p a t m", a=2, t=4))
         wk_s = planes_first[:, :, CH:]
         wq_s = planes_late[:, :, :R]
@@ -139,7 +140,7 @@ def tile_list_kvt_qf_exp_kernel(
             [planes[:, a, first : first + CH] for a in range(2)]
             for planes, first in ((planes_first, 0), (planes_second, 0), (planes_rest, 0), (planes_rest, CH))
         ]
-        wk = keep.tile([P, 1024], I32, name="wk", align_bytes=64)
+        wk = keep.tile([P, 1024], I32, name="wk", align_bytes=ALIGN)
         deal_words(wk_raw[0][:], wk[:, :512])
 
         def w_tile(dealt, dealt_s, a, b, t):
@@ -158,7 +159,7 @@ def tile_list_kvt_qf_exp_kernel(
             nc.scalar.copy(out=dst, in_=bank[:].rearrange("p t m -> p m t"))
 
         def key_sums(c, b):
-            pairs = ring.tile([P, 2, 2, HALF, 2], BF16, name="pairs", bufs=5, align_bytes=64)
+            pairs = ring.tile([P, 2, 2, HALF, 2], BF16, name="pairs", bufs=5, align_bytes=ALIGN)
             for h in range(2):
                 js = slice(h * HALF, (h + 1) * HALF)
                 for u in range(2):
@@ -177,7 +178,7 @@ def tile_list_kvt_qf_exp_kernel(
         def weave(pairs, woven=None, hs=slice(0, 2)):
             count = hs.stop - hs.start
             if woven is None:
-                woven = ring.tile([P, count * HALF * 4], BF16, name="woven", bufs=3, align_bytes=64)
+                woven = ring.tile([P, count * HALF * 4], BF16, name="woven", bufs=3, align_bytes=ALIGN)
             nc.vector.tensor_copy(
                 out=woven[:].bitcast(I32).rearrange("p (h j u) -> p h j u", h=count, u=2),
                 in_=pairs[:].rearrange("p h u j e -> p (h u j e)").bitcast(I32).rearrange("p (h u j) -> p h j u", h=2, u=2)[:, hs],
@@ -186,8 +187,8 @@ def tile_list_kvt_qf_exp_kernel(
 
         def quantised_keys(woven):
             width = woven.shape[1] // 4
-            kq = ring.tile([P, width], U32, name="kq", bufs=7, align_bytes=64)
-            kq_s = ring.tile([P, width], U8, name="kq_s", bufs=7, align_bytes=64)
+            kq = ring.tile([P, width], U32, name="kq", bufs=7, align_bytes=ALIGN)
+            kq_s = ring.tile([P, width], U8, name="kq_s", bufs=7, align_bytes=ALIGN)
             quantise(woven[:], kq[:], kq_s[:])
             return kq, kq_s
 
@@ -230,48 +231,48 @@ def tile_list_kvt_qf_exp_kernel(
         idle = psum.tile([P, CH], F32, name="bank", tag="bank")
         for i in range(WARM_PASSES):
             nc.tensor.matmul_mx(
-                out=idle[:], lhsT=wk[:, :64].bitcast(FP4X4), lhsT_scale=picked_first[:, :P],
-                rhs=table[:, : CH // 2].bitcast(FP4X4), rhs_scale=picked_first[:], start=(i == 0), stop=(i == WARM_PASSES - 1),
+                out=idle[:], lhsT=wk[:, :64].bitcast(FP4X4), lhsT_scale=tscale[:, :P],
+                rhs=table[:, : CH // 2].bitcast(FP4X4), rhs_scale=tscale[:, :CH], start=(i == 0), stop=(i == WARM_PASSES - 1),
             )
 
-        picked = gather_words(0, keep.tile([P, CH], U32, name="picked0", tag="picked", align_bytes=64))
-        cols = [keep.tile([P, 2, CH], U16, name="parted0", align_bytes=64)]
+        picked = gather_words(0, keep.tile([P, CH], U32, name="picked0", tag="picked", align_bytes=ALIGN))
+        cols = [keep.tile([P, 2, CH], U16, name="parted0", align_bytes=ALIGN)]
         for h in range(2):
             for a in range(2):
                 js = slice(h * HALF, (h + 1) * HALF)
                 nc.vector.tensor_copy(out=cols[0][:, a, js], in_=by_pass(picked)[:, a, js])
         deal_words(wk_raw[1][:], wk[:, 512:])
-        picked = gather_words(1, keep.tile([P, CH], U32, name="picked1", tag="picked", align_bytes=64))
-        wv8b = keep.tile([P, N, 4], BF16, name="wv8b", align_bytes=64)
+        picked = gather_words(1, keep.tile([P, CH], U32, name="picked1", tag="picked", align_bytes=ALIGN))
+        wv8b = keep.tile([P, N, 4], BF16, name="wv8b", align_bytes=ALIGN)
         nc.vector.tensor_copy(
             out=wv8b[:].rearrange("p (c i) t -> p c t i", i=4), in_=wv8_raw[:].rearrange("p t (c i) -> p c t i", i=4)
         )
-        cols.append(part_words(picked, shared.tile([P, 2, CH], U16, name="parted1", offset=WV8_RAW_AT, align_bytes=64)))
-        wv8q = keep.tile([P, N], U32, name="wv8q", align_bytes=64)
-        wv8q_s = keep.tile([P, N], U8, name="wv8q_s", align_bytes=64)
+        cols.append(part_words(picked, shared.tile([P, 2, CH], U16, name="parted1", offset=WV8_RAW_AT, align_bytes=ALIGN)))
+        wv8q = keep.tile([P, N], U32, name="wv8q", align_bytes=ALIGN)
+        wv8q_s = keep.tile([P, N], U8, name="wv8q_s", align_bytes=ALIGN)
         quantise(wv8b[:].rearrange("p n t -> p (n t)"), wv8q[:], wv8q_s[:])
         place(gather_scales(2 * CH, J, "picked"), planes_rest)
 
         pairs00 = key_sums(0, 0)
         pairs01 = key_sums(0, 1)
         pairs10 = key_sums(1, 0)
-        xb = shared.tile([P, 2, M, 4], BF16, name="xb", offset=XB_AT, align_bytes=64)
+        xb = shared.tile([P, 2, M, 4], BF16, name="xb", offset=XB_AT, align_bytes=ALIGN)
         nc.vector.tensor_copy(
             out=xb[:].rearrange("p a (c i) t -> p a c t i", i=4), in_=x_raw[:].rearrange("p a t (c i) -> p a c t i", i=4)
         )
-        wq = keep.tile([P, 1024], I32, name="wq", align_bytes=64)
+        wq = keep.tile([P, 1024], I32, name="wq", align_bytes=ALIGN)
         deal_words(wq_raw[:, :, :256], wq[:, :512])
         deal_words(wq_raw[:, :, 256:], wq[:, 512:])
-        xq = keep.tile([P, 2, M], U32, name="xq", align_bytes=64)
-        xq_s = keep.tile([P, 2, M], U8, name="xq_s", align_bytes=64)
+        xq = keep.tile([P, 2, M], U32, name="xq", align_bytes=ALIGN)
+        xq_s = keep.tile([P, 2, M], U8, name="xq_s", align_bytes=ALIGN)
         quantise(xb[:].rearrange("p a m t -> p (a m t)"), xq[:].rearrange("p a m -> p (a m)"), xq_s[:].rearrange("p a m -> p (a m)"))
         for i in range(2):
             values(0, 2 * i, on_scalar)
-            values(0, 2 * i + 1, on_vector, shared.tile([P, CH], F32, name="staged_x%d" % i, offset=X_RAW_AT + 4096 * i, align_bytes=64))
+            values(0, 2 * i + 1, on_vector, shared.tile([P, CH], F32, name="staged_x%d" % i, offset=X_RAW_AT + 4096 * i, align_bytes=ALIGN))
         pairs11 = key_sums(1, 1)
         for nt in range(3):
             values(1, nt, on_scalar)
-        qb = keep.tile([P, 2, M, 4], BF16, name="qb", tag="qb", align_bytes=64)
+        qb = keep.tile([P, 2, M, 4], BF16, name="qb", tag="qb", align_bytes=ALIGN)
         for b in range(2):
             for mh in range(M // P):
                 ms = slice(mh * P, (mh + 1) * P)
@@ -281,32 +282,32 @@ def tile_list_kvt_qf_exp_kernel(
             return shared.tile([P, 4 * CH], BF16, name=name, offset=offset, align_bytes=64)
 
         above, below = XB_AT + WOVEN_BYTES - OVERLAP, XB_AT - WOVEN_BYTES + OVERLAP
-        picked = gather_words(2, shared.tile([P, CH], U32, name="picked2", offset=XB_AT, align_bytes=64))
+        picked = gather_words(2, shared.tile([P, CH], U32, name="picked2", offset=XB_AT, align_bytes=ALIGN))
         woven00 = weave(pairs00, woven_over_xb("woven_above", above))
-        cols.append(part_words(picked, keep.tile([P, 2, CH], U16, name="parted2", align_bytes=64)))
+        cols.append(part_words(picked, keep.tile([P, 2, CH], U16, name="parted2", align_bytes=ALIGN)))
         keys = {(0, 0): quantised_keys(woven00)}
         keys[0, 1] = quantised_keys(weave(pairs01, woven_over_xb("woven_below", below)))
         keys[1, 1] = quantised_keys(weave(pairs11, woven_over_xb("woven_above", above)))
         values(1, 3, on_scalar)
-        qq = keep.tile([P, 2, M], U32, name="qq", align_bytes=64)
-        qq_s = keep.tile([P, 2, M], U8, name="qq_s", align_bytes=64)
+        qq = keep.tile([P, 2, M], U32, name="qq", align_bytes=ALIGN)
+        qq_s = keep.tile([P, 2, M], U8, name="qq_s", align_bytes=ALIGN)
         quantise(qb[:].rearrange("p b m t -> p (b m t)"), qq[:].rearrange("p b m -> p (b m)"), qq_s[:].rearrange("p b m -> p (b m)"))
 
         pairs20 = key_sums(2, 0)
-        keys[1, 0] = quantised_keys(weave(pairs10, keep.tile([P, 4 * CH], BF16, name="woven10", tag="qb", align_bytes=64)))
+        keys[1, 0] = quantised_keys(weave(pairs10, keep.tile([P, 4 * CH], BF16, name="woven10", tag="qb", align_bytes=ALIGN)))
         chunk_scores(0)
         values(2, 0, on_scalar)
         values(2, 1, on_scalar)
-        picked = gather_words(3, keep.tile([P, CH], U32, name="picked3", tag="qb", align_bytes=64))
-        cols.append(part_words(picked, keep.tile([P, 2, CH], U16, name="parted3", align_bytes=64)))
+        picked = gather_words(3, keep.tile([P, CH], U32, name="picked3", tag="qb", align_bytes=ALIGN))
+        cols.append(part_words(picked, keep.tile([P, 2, CH], U16, name="parted3", align_bytes=ALIGN)))
         keys[2, 0] = quantised_keys(weave(pairs20))
         keys[2, 1] = quantised_keys(weave(key_sums(2, 1)))
         chunk_scores(1)
-        values(2, 2, on_scalar)
+        values(2, 2, on_vector)
         values(2, 3, on_vector)
         keys[3, 0] = quantised_keys(weave(key_sums(3, 0)))
         chunk_scores(2)
-        values(3, 0, on_scalar)
+        values(3, 0, on_vector)
         values(3, 1, on_vector)
 
         pairs31 = key_sums(3, 1)

@@ -66,11 +66,11 @@ def tile_list_kvt_qf_exp_kernel(
         def place(staged, planes):
             for q in (0, 2, 1, 3):
                 nc.sync.dma_start(
-                    out=planes[32 * q : 32 * q + 4].bitcast(I32), in_=staged[96 + 8 * q : 104 + 8 * q, :].bitcast(I32)
+                    out=planes[32 * q : 32 * q + 4].bitcast(I32), in_=staged[96 + 8 * q : 104 + 8 * q].bitcast(I32)
                 )
 
-        def zeroed_planes(width, name, tag):
-            planes = keep.tile([P, 2, width], U8, name=name, tag=tag, align_bytes=ALIGN)
+        def zeroed_planes(width, name):
+            planes = keep.tile([P, 2, width], U8, name=name, align_bytes=ALIGN)
             nc.vector.memset(planes[:].rearrange("p a n -> p (a n)").bitcast(I32), 0)
             return planes
 
@@ -101,51 +101,48 @@ def tile_list_kvt_qf_exp_kernel(
         nc.sync.dma_start(offsets[:], offs)
         tscale = load_scale_rows(tab_scales, "tscale")
         wk_sraw = load_scale_rows(wk_scales, "wk_sraw")
-        first_rows = keep.tile([P, CH + R], U8, name="first_rows", align_bytes=ALIGN)
+        early_rows = keep.tile([P, CH + R + CH], U8, name="early_rows", align_bytes=ALIGN)
         late_rows = keep.tile([P, R + N // 2], U8, name="late_rows", align_bytes=ALIGN)
         wq_sraw = load_scale_rows(wq_scales, "wq_sraw")
         nc.sync.dma_start(
             out=late_rows[ROWS, R:].bitcast(I32),
             in_=wv4_scales[0].rearrange("q (h n) -> (q h) n", h=2).bitcast(I32),
         )
-        wk_raw = [load_weight_words(wk_words[:, :, :R], "wk_raw0")]
         table = keep.tile([P, T], U32, name="table", align_bytes=ALIGN)
         nc.sync.dma_start(out=table[:].bitcast(I32), in_=tab_words[0].rearrange("p t b -> p (t b)").bitcast(I32))
+        wk_raw = [load_weight_words(wk_words[:, :, :R], "wk_raw0")]
 
         nc.vector.memset(tscale[: ROWS.start, :].bitcast(I32), 0)
-        planes_first = zeroed_planes(CH + R, "planes_first", "planes_first")
-        planes_rest = zeroed_planes(2 * CH, "planes_rest", "planes_rest")
+        planes_first = zeroed_planes(CH + R // 2, "planes_first")
+        planes_second = zeroed_planes(R // 2 + CH, "planes_second")
+        planes_late = zeroed_planes(R + N // 2, "planes_late")
 
         picked_first = gather_scales(0, CH, "picked_first")
-        deal_scales(wk_sraw, first_rows[ROWS, CH:])
-        nc.vector.tensor_copy(out=first_rows[ROWS, :CH].bitcast(I32), in_=picked_first[ROWS, :].bitcast(I32))
-        place(first_rows, planes_first)
+        deal_scales(wk_sraw, early_rows[ROWS, CH : CH + R])
+        nc.vector.tensor_copy(out=early_rows[ROWS, :CH].bitcast(I32), in_=picked_first[ROWS, :].bitcast(I32))
+        place(early_rows[:, : CH + R // 2], planes_first)
         wk_raw.append(load_weight_words(wk_words[:, :, R:], "wk_raw1"))
+        picked_second = gather_scales(CH, 2 * CH, "wk_sraw")
+        nc.vector.tensor_copy(out=early_rows[ROWS, CH + R :].bitcast(I32), in_=picked_second[ROWS, :].bitcast(I32))
+        place(early_rows[:, CH + R // 2 :], planes_second)
         wv8_raw = shared.tile([P, 4, N], F32, name="wv8_raw", offset=WV8_RAW_AT, align_bytes=ALIGN)
         nc.sync.dma_start(out=wv8_raw[:], in_=wv8.rearrange("(p t) n -> p t n", t=4))
-        planes_second = zeroed_planes(CH, "planes_second", "picked_first")
-        place(gather_scales(CH, 2 * CH, "wk_sraw"), planes_second)
         wv4 = keep.tile([P, 2 * N], U8, name="wv4", align_bytes=ALIGN)
         nc.sync.dma_start(out=wv4[:].bitcast(I32), in_=wv4_words[0].bitcast(I32))
         deal_scales(wq_sraw, late_rows[ROWS, :R])
-        planes_late = zeroed_planes(R + N // 2, "planes_late", "wq_sraw")
-        place(late_rows, planes_late)
-        wq_raw = load_weight_words(wq_words, "wq_raw")
+        place(late_rows[:], planes_late)
         x_raw = shared.tile([P, 2, 4, M], F32, name="x_raw", offset=X_RAW_AT, align_bytes=ALIGN)
         nc.sync.dma_start(out=x_raw[:], in_=x.rearrange("(a p t) m -> p a t m", a=2, t=4))
-        wk_s = planes_first[:, :, CH:]
-        wq_s = planes_late[:, :, :R]
+        wq_raw = load_weight_words(wq_words, "wq_raw")
+        wk_s = [planes_first[:, :, CH:], planes_second[:, :, : R // 2]]
+        wq_s = [planes_late[:, :, : R // 2], planes_late[:, :, R // 2 : R]]
         wv4_s = planes_late[:, :, R:]
-        col_scales = [
-            [planes[:, a, first : first + CH] for a in range(2)]
-            for planes, first in ((planes_first, 0), (planes_second, 0), (planes_rest, 0), (planes_rest, CH))
-        ]
+        col_scales = [[planes[:, a, first : first + CH] for a in range(2)] for planes, first in ((planes_first, 0), (planes_second, R // 2))]
         wk = keep.tile([P, 1024], I32, name="wk", align_bytes=ALIGN)
-        deal_words(wk_raw[0][:], wk[:, :512])
 
         def w_tile(dealt, dealt_s, a, b, t):
             u = 8 * b + 4 * a + t
-            return dealt[:, 64 * u : 64 * (u + 1)].bitcast(FP4X4), dealt_s[:, a, P * (4 * b + t) : P * (4 * b + t + 1)]
+            return dealt[:, 64 * u : 64 * (u + 1)].bitcast(FP4X4), dealt_s[b][:, a, P * t : P * (t + 1)]
 
         def project(b, ms, dst):
             bank = psum.tile([P, 4, P], F32, name="bank", tag="bank")
@@ -231,27 +228,31 @@ def tile_list_kvt_qf_exp_kernel(
         idle = psum.tile([P, CH], F32, name="bank", tag="bank")
         for i in range(WARM_PASSES):
             nc.tensor.matmul_mx(
-                out=idle[:], lhsT=wk[:, :64].bitcast(FP4X4), lhsT_scale=tscale[:, :P],
+                out=idle[:], lhsT=table[:, :64].bitcast(FP4X4), lhsT_scale=tscale[:, :P],
                 rhs=table[:, : CH // 2].bitcast(FP4X4), rhs_scale=tscale[:, :CH], start=(i == 0), stop=(i == WARM_PASSES - 1),
             )
 
         picked = gather_words(0, keep.tile([P, CH], U32, name="picked0", tag="picked", align_bytes=ALIGN))
-        cols = [keep.tile([P, 2, CH], U16, name="parted0", align_bytes=ALIGN)]
+        deal_words(wk_raw[0][:], wk[:, :512])
+        cols = [keep.tile([P, 2, CH], U16, name="parted0", tag="wk_raw0", align_bytes=ALIGN)]
         for h in range(2):
             for a in range(2):
                 js = slice(h * HALF, (h + 1) * HALF)
                 nc.vector.tensor_copy(out=cols[0][:, a, js], in_=by_pass(picked)[:, a, js])
         deal_words(wk_raw[1][:], wk[:, 512:])
         picked = gather_words(1, keep.tile([P, CH], U32, name="picked1", tag="picked", align_bytes=ALIGN))
+        cols.append(part_words(picked, keep.tile([P, 2, CH], U16, name="parted1", tag="wk_raw1", align_bytes=ALIGN)))
         wv8b = keep.tile([P, N, 4], BF16, name="wv8b", align_bytes=ALIGN)
         nc.vector.tensor_copy(
             out=wv8b[:].rearrange("p (c i) t -> p c t i", i=4), in_=wv8_raw[:].rearrange("p t (c i) -> p c t i", i=4)
         )
-        cols.append(part_words(picked, shared.tile([P, 2, CH], U16, name="parted1", offset=WV8_RAW_AT, align_bytes=ALIGN)))
+        planes_rest = shared.tile([P, 2, 2 * CH], U8, name="planes_rest", offset=WV8_RAW_AT, align_bytes=ALIGN)
+        nc.vector.memset(planes_rest[:].rearrange("p a n -> p (a n)").bitcast(I32), 0)
+        col_scales.extend([planes_rest[:, a, first : first + CH] for a in range(2)] for first in (0, CH))
         wv8q = keep.tile([P, N], U32, name="wv8q", align_bytes=ALIGN)
         wv8q_s = keep.tile([P, N], U8, name="wv8q_s", align_bytes=ALIGN)
         quantise(wv8b[:].rearrange("p n t -> p (n t)"), wv8q[:], wv8q_s[:])
-        place(gather_scales(2 * CH, J, "picked"), planes_rest)
+        place(gather_scales(2 * CH, J, "wv8b")[:], planes_rest)
 
         pairs00 = key_sums(0, 0)
         pairs01 = key_sums(0, 1)

@@ -21,7 +21,7 @@ CH = 512
 HALF = CH // 2
 SCORE_SCALE = 0.015625
 ALIGN = 256
-WARM_PASSES = 4
+WARM_PASSES = 6
 
 WV8_RAW_AT = 0
 XB_AT = 8192
@@ -51,10 +51,10 @@ def tile_list_kvt_qf_exp_kernel(
             nc.sync.dma_start(out=raw[ROWS, :].bitcast(I32), in_=scales.rearrange("a q n -> q a n").bitcast(I32))
             return raw
 
-        def deal_words(raw, dst):
-            nc.vector.tensor_copy(
-                out=dst.rearrange("p (a t g w) -> p a t g w", a=2, t=4, g=16),
-                in_=raw.rearrange("p a (g t w) -> p a t g w", t=4, g=16),
+        def deal_words(raw, dst, copy=nc.vector.tensor_copy, ts=slice(0, 4)):
+            copy(
+                out=dst.rearrange("p (t a g w) -> p t a g w", a=2, t=4, g=16)[:, ts],
+                in_=raw.bitcast(U32).rearrange("p a (g t w) -> p t a g w", t=4, g=16)[:, ts],
             )
 
         def deal_scales(raw, dst):
@@ -71,11 +71,11 @@ def tile_list_kvt_qf_exp_kernel(
 
         def zeroed_planes(width, name):
             planes = keep.tile([P, 2, width], U8, name=name, align_bytes=ALIGN)
-            nc.vector.memset(planes[:].rearrange("p a n -> p (a n)").bitcast(I32), 0)
+            nc.gpsimd.memset(planes[:].rearrange("p a n -> p (a n)").bitcast(I32), 0)
             return planes
 
-        def gather_words(c, picked):
-            nc.vector.tensor_copy(out=picked[:], in_=table[:].indirect(offsets[:, c * CH // 16 : (c + 1) * CH // 16]))
+        def gather_words(first, picked):
+            nc.vector.tensor_copy(out=picked[:], in_=table[:].indirect(offsets[:, first // 16 : (first + picked.shape[1]) // 16]))
             return picked
 
         def by_pass(picked):
@@ -104,6 +104,7 @@ def tile_list_kvt_qf_exp_kernel(
         early_rows = keep.tile([P, CH + R + CH], U8, name="early_rows", align_bytes=ALIGN)
         late_rows = keep.tile([P, R + N // 2], U8, name="late_rows", align_bytes=ALIGN)
         wq_sraw = load_scale_rows(wq_scales, "wq_sraw")
+        nc.vector.memset(late_rows[: ROWS.start, :R].bitcast(I32), 0)
         nc.sync.dma_start(
             out=late_rows[ROWS, R:].bitcast(I32),
             in_=wv4_scales[0].rearrange("q (h n) -> (q h) n", h=2).bitcast(I32),
@@ -122,14 +123,14 @@ def tile_list_kvt_qf_exp_kernel(
         nc.vector.tensor_copy(out=early_rows[ROWS, :CH].bitcast(I32), in_=picked_first[ROWS, :].bitcast(I32))
         place(early_rows[:, : CH + R // 2], planes_first)
         wk_raw.append(load_weight_words(wk_words[:, :, R:], "wk_raw1"))
-        picked_second = gather_scales(CH, 2 * CH, "wk_sraw")
+        deal_scales(wq_sraw, late_rows[ROWS, :R])
+        picked_second = gather_scales(CH, 2 * CH, "wq_sraw")
         nc.vector.tensor_copy(out=early_rows[ROWS, CH + R :].bitcast(I32), in_=picked_second[ROWS, :].bitcast(I32))
         place(early_rows[:, CH + R // 2 :], planes_second)
         wv8_raw = shared.tile([P, 4, N], F32, name="wv8_raw", offset=WV8_RAW_AT, align_bytes=ALIGN)
         nc.sync.dma_start(out=wv8_raw[:], in_=wv8.rearrange("(p t) n -> p t n", t=4))
         wv4 = keep.tile([P, 2 * N], U8, name="wv4", align_bytes=ALIGN)
         nc.sync.dma_start(out=wv4[:].bitcast(I32), in_=wv4_words[0].bitcast(I32))
-        deal_scales(wq_sraw, late_rows[ROWS, :R])
         place(late_rows[:], planes_late)
         x_raw = shared.tile([P, 2, 4, M], F32, name="x_raw", offset=X_RAW_AT, align_bytes=ALIGN)
         nc.sync.dma_start(out=x_raw[:], in_=x.rearrange("(a p t) m -> p a t m", a=2, t=4))
@@ -138,11 +139,11 @@ def tile_list_kvt_qf_exp_kernel(
         wq_s = [planes_late[:, :, : R // 2], planes_late[:, :, R // 2 : R]]
         wv4_s = planes_late[:, :, R:]
         col_scales = [[planes[:, a, first : first + CH] for a in range(2)] for planes, first in ((planes_first, 0), (planes_second, R // 2))]
-        wk = keep.tile([P, 1024], I32, name="wk", align_bytes=ALIGN)
+        wk = [keep.tile([P, 512], U32, name="wk0", align_bytes=ALIGN)]
 
         def w_tile(dealt, dealt_s, a, b, t):
-            u = 8 * b + 4 * a + t
-            return dealt[:, 64 * u : 64 * (u + 1)].bitcast(FP4X4), dealt_s[b][:, a, P * t : P * (t + 1)]
+            u = 2 * t + a
+            return dealt[b][:, 64 * u : 64 * (u + 1)].bitcast(FP4X4), dealt_s[b][:, a, P * t : P * (t + 1)]
 
         def project(b, ms, dst):
             bank = psum.tile([P, 4, P], F32, name="bank", tag="bank")
@@ -228,20 +229,21 @@ def tile_list_kvt_qf_exp_kernel(
         idle = psum.tile([P, CH], F32, name="bank", tag="bank")
         for i in range(WARM_PASSES):
             nc.tensor.matmul_mx(
-                out=idle[:], lhsT=table[:, :64].bitcast(FP4X4), lhsT_scale=tscale[:, :P],
-                rhs=table[:, : CH // 2].bitcast(FP4X4), rhs_scale=tscale[:, :CH], start=(i == 0), stop=(i == WARM_PASSES - 1),
+                out=idle[:], lhsT=late_rows[:, : 2 * P].bitcast(FP4X4), lhsT_scale=late_rows[:, :P],
+                rhs=late_rows[:, : 2 * CH].bitcast(FP4X4), rhs_scale=late_rows[:, :CH], start=(i == 0), stop=(i == WARM_PASSES - 1),
             )
 
-        picked = gather_words(0, keep.tile([P, CH], U32, name="picked0", tag="picked", align_bytes=ALIGN))
-        deal_words(wk_raw[0][:], wk[:, :512])
-        cols = [keep.tile([P, 2, CH], U16, name="parted0", tag="wk_raw0", align_bytes=ALIGN)]
+        for u in range(2):
+            deal_words(wk_raw[0][:], wk[0][:], nc.scalar.copy, slice(2 * u, 2 * u + 2))
+        cols = [keep.tile([P, 2, CH], U16, name="parted0", align_bytes=ALIGN)]
         for h in range(2):
+            picked = gather_words(h * HALF, keep.tile([P, HALF], U32, name="picked0%d" % h, tag="picked", align_bytes=ALIGN))
             for a in range(2):
-                js = slice(h * HALF, (h + 1) * HALF)
-                nc.vector.tensor_copy(out=cols[0][:, a, js], in_=by_pass(picked)[:, a, js])
-        deal_words(wk_raw[1][:], wk[:, 512:])
-        picked = gather_words(1, keep.tile([P, CH], U32, name="picked1", tag="picked", align_bytes=ALIGN))
-        cols.append(part_words(picked, keep.tile([P, 2, CH], U16, name="parted1", tag="wk_raw1", align_bytes=ALIGN)))
+                nc.vector.tensor_copy(out=cols[0][:, a, h * HALF : (h + 1) * HALF], in_=by_pass(picked)[:, a, :])
+        wk.append(keep.tile([P, 512], U32, name="wk1", tag="picked", align_bytes=ALIGN))
+        deal_words(wk_raw[1][:], wk[1][:])
+        picked = gather_words(CH, keep.tile([P, CH], U32, name="picked1", tag="wk_raw1", align_bytes=ALIGN))
+        cols.append(part_words(picked, keep.tile([P, 2, CH], U16, name="parted1", align_bytes=ALIGN)))
         wv8b = keep.tile([P, N, 4], BF16, name="wv8b", align_bytes=ALIGN)
         nc.vector.tensor_copy(
             out=wv8b[:].rearrange("p (c i) t -> p c t i", i=4), in_=wv8_raw[:].rearrange("p t (c i) -> p c t i", i=4)
@@ -257,22 +259,22 @@ def tile_list_kvt_qf_exp_kernel(
         pairs00 = key_sums(0, 0)
         pairs01 = key_sums(0, 1)
         pairs10 = key_sums(1, 0)
+        pairs11 = key_sums(1, 1)
         xb = shared.tile([P, 2, M, 4], BF16, name="xb", offset=XB_AT, align_bytes=ALIGN)
         nc.vector.tensor_copy(
             out=xb[:].rearrange("p a (c i) t -> p a c t i", i=4), in_=x_raw[:].rearrange("p a t (c i) -> p a c t i", i=4)
         )
-        wq = keep.tile([P, 1024], I32, name="wq", align_bytes=ALIGN)
-        deal_words(wq_raw[:, :, :256], wq[:, :512])
-        deal_words(wq_raw[:, :, 256:], wq[:, 512:])
+        wq = [keep.tile([P, 512], U32, name="wq%d" % b, align_bytes=ALIGN) for b in range(2)]
+        for b in range(2):
+            deal_words(wq_raw[:, :, 256 * b : 256 * (b + 1)], wq[b][:])
         xq = keep.tile([P, 2, M], U32, name="xq", align_bytes=ALIGN)
         xq_s = keep.tile([P, 2, M], U8, name="xq_s", align_bytes=ALIGN)
         quantise(xb[:].rearrange("p a m t -> p (a m t)"), xq[:].rearrange("p a m -> p (a m)"), xq_s[:].rearrange("p a m -> p (a m)"))
-        for i in range(2):
-            values(0, 2 * i, on_scalar)
-            values(0, 2 * i + 1, on_vector, shared.tile([P, CH], F32, name="staged_x%d" % i, offset=X_RAW_AT + 4096 * i, align_bytes=ALIGN))
-        pairs11 = key_sums(1, 1)
-        for nt in range(3):
-            values(1, nt, on_scalar)
+        keys = {(0, 0): quantised_keys(weave(pairs00))}
+        keys[0, 1] = quantised_keys(weave(pairs01))
+        for c in range(2):
+            for nt in range(4):
+                values(c, nt, on_scalar)
         qb = keep.tile([P, 2, M, 4], BF16, name="qb", tag="qb", align_bytes=ALIGN)
         for b in range(2):
             for mh in range(M // P):
@@ -283,23 +285,20 @@ def tile_list_kvt_qf_exp_kernel(
             return shared.tile([P, 4 * CH], BF16, name=name, offset=offset, align_bytes=64)
 
         above, below = XB_AT + WOVEN_BYTES - OVERLAP, XB_AT - WOVEN_BYTES + OVERLAP
-        picked = gather_words(2, shared.tile([P, CH], U32, name="picked2", offset=XB_AT, align_bytes=ALIGN))
-        woven00 = weave(pairs00, woven_over_xb("woven_above", above))
+        picked = gather_words(2 * CH, shared.tile([P, CH], U32, name="picked2", offset=XB_AT, align_bytes=ALIGN))
+        woven10 = weave(pairs10, woven_over_xb("woven_above", above))
         cols.append(part_words(picked, keep.tile([P, 2, CH], U16, name="parted2", align_bytes=ALIGN)))
-        keys = {(0, 0): quantised_keys(woven00)}
-        keys[0, 1] = quantised_keys(weave(pairs01, woven_over_xb("woven_below", below)))
-        keys[1, 1] = quantised_keys(weave(pairs11, woven_over_xb("woven_above", above)))
-        values(1, 3, on_scalar)
+        keys[1, 0] = quantised_keys(woven10)
+        keys[1, 1] = quantised_keys(weave(pairs11, woven_over_xb("woven_below", below)))
         qq = keep.tile([P, 2, M], U32, name="qq", align_bytes=ALIGN)
         qq_s = keep.tile([P, 2, M], U8, name="qq_s", align_bytes=ALIGN)
         quantise(qb[:].rearrange("p b m t -> p (b m t)"), qq[:].rearrange("p b m -> p (b m)"), qq_s[:].rearrange("p b m -> p (b m)"))
 
         pairs20 = key_sums(2, 0)
-        keys[1, 0] = quantised_keys(weave(pairs10, keep.tile([P, 4 * CH], BF16, name="woven10", tag="qb", align_bytes=ALIGN)))
         chunk_scores(0)
-        values(2, 0, on_scalar)
-        values(2, 1, on_scalar)
-        picked = gather_words(3, keep.tile([P, CH], U32, name="picked3", tag="qb", align_bytes=ALIGN))
+        values(2, 0, on_vector)
+        values(2, 1, on_vector)
+        picked = gather_words(3 * CH, keep.tile([P, CH], U32, name="picked3", tag="qb", align_bytes=ALIGN))
         cols.append(part_words(picked, keep.tile([P, 2, CH], U16, name="parted3", align_bytes=ALIGN)))
         keys[2, 0] = quantised_keys(weave(pairs20))
         keys[2, 1] = quantised_keys(weave(key_sums(2, 1)))

@@ -71,7 +71,7 @@ def tile_list_kvt_qf_exp_kernel(
 
         def zeroed_planes(width, name):
             planes = keep.tile([P, 2, width], U8, name=name, align_bytes=ALIGN)
-            nc.gpsimd.memset(planes[:].rearrange("p a n -> p (a n)").bitcast(I32), 0)
+            nc.vector.memset(planes[:].rearrange("p a n -> p (a n)").bitcast(I32), 0)
             return planes
 
         def gather_words(first, picked):
@@ -145,33 +145,26 @@ def tile_list_kvt_qf_exp_kernel(
             u = 2 * t + a
             return dealt[b][:, 64 * u : 64 * (u + 1)].bitcast(FP4X4), dealt_s[b][:, a, P * t : P * (t + 1)]
 
-        def project(b, ms, dst):
-            bank = psum.tile([P, 4, P], F32, name="bank", tag="bank")
-            for t in range(4):
-                for a in range(2):
-                    lhs, lhs_s = w_tile(wq, wq_s, a, b, t)
-                    nc.tensor.matmul_mx(
-                        out=bank[:, t, :], lhsT=lhs, lhsT_scale=lhs_s, rhs=xq[:, a, ms].bitcast(FP8X4), rhs_scale=xq_s[:, a, ms],
-                        start=(a == 0), stop=(a == 1),
-                    )
-            nc.scalar.copy(out=dst, in_=bank[:].rearrange("p t m -> p m t"))
-
-        def key_sums(c, b):
+        def paired_sums(weights, weight_scales, halves):
             pairs = ring.tile([P, 2, 2, HALF, 2], BF16, name="pairs", bufs=5, align_bytes=ALIGN)
-            for h in range(2):
-                js = slice(h * HALF, (h + 1) * HALF)
+            for h, (b, moving) in enumerate(halves):
                 for u in range(2):
                     bank = psum.tile([P, 2, HALF], F32, name="bank", tag="bank")
                     for e in range(2):
                         for a in range(2):
-                            lhs, lhs_s = w_tile(wk, wk_s, a, b, 2 * u + e)
+                            lhs, lhs_s = w_tile(weights, weight_scales, a, b, 2 * u + e)
                             nc.tensor.matmul_mx(
-                                out=bank[:, e, :], lhsT=lhs, lhsT_scale=lhs_s,
-                                rhs=cols[c][:, a, js].bitcast(FP4X4), rhs_scale=col_scales[c][a][:, js],
+                                out=bank[:, e, :], lhsT=lhs, lhsT_scale=lhs_s, rhs=moving[a][0], rhs_scale=moving[a][1],
                                 start=(a == 0), stop=(a == 1),
                             )
                     nc.scalar.copy(out=pairs[:, h, u], in_=bank[:].rearrange("p e j -> p j e"))
             return pairs
+
+        def key_sums(c, b):
+            spans = [slice(h * HALF, (h + 1) * HALF) for h in range(2)]
+            return paired_sums(
+                wk, wk_s, [(b, [(cols[c][:, a, js].bitcast(FP4X4), col_scales[c][a][:, js]) for a in range(2)]) for js in spans]
+            )
 
         def weave(pairs, woven=None, hs=slice(0, 2)):
             count = hs.stop - hs.start
@@ -240,9 +233,9 @@ def tile_list_kvt_qf_exp_kernel(
             picked = gather_words(h * HALF, keep.tile([P, HALF], U32, name="picked0%d" % h, tag="picked", align_bytes=ALIGN))
             for a in range(2):
                 nc.vector.tensor_copy(out=cols[0][:, a, h * HALF : (h + 1) * HALF], in_=by_pass(picked)[:, a, :])
-        wk.append(keep.tile([P, 512], U32, name="wk1", tag="picked", align_bytes=ALIGN))
-        deal_words(wk_raw[1][:], wk[1][:])
-        picked = gather_words(CH, keep.tile([P, CH], U32, name="picked1", tag="wk_raw1", align_bytes=ALIGN))
+        wk.append(keep.tile([P, 512], U32, name="wk1", align_bytes=ALIGN))
+        deal_words(wk_raw[1][:], wk[1][:], nc.scalar.copy)
+        picked = gather_words(CH, keep.tile([P, CH], U32, name="picked1", tag="picked", align_bytes=ALIGN))
         cols.append(part_words(picked, keep.tile([P, 2, CH], U16, name="parted1", align_bytes=ALIGN)))
         wv8b = keep.tile([P, N, 4], BF16, name="wv8b", align_bytes=ALIGN)
         nc.vector.tensor_copy(
@@ -270,45 +263,43 @@ def tile_list_kvt_qf_exp_kernel(
         xq = keep.tile([P, 2, M], U32, name="xq", align_bytes=ALIGN)
         xq_s = keep.tile([P, 2, M], U8, name="xq_s", align_bytes=ALIGN)
         quantise(xb[:].rearrange("p a m t -> p (a m t)"), xq[:].rearrange("p a m -> p (a m)"), xq_s[:].rearrange("p a m -> p (a m)"))
-        keys = {(0, 0): quantised_keys(weave(pairs00))}
-        keys[0, 1] = quantised_keys(weave(pairs01))
         for c in range(2):
             for nt in range(4):
                 values(c, nt, on_scalar)
-        qb = keep.tile([P, 2, M, 4], BF16, name="qb", tag="qb", align_bytes=ALIGN)
-        for b in range(2):
-            for mh in range(M // P):
-                ms = slice(mh * P, (mh + 1) * P)
-                project(b, ms, qb[:, b, ms, :])
+        queries = [(xq[:, a, :].bitcast(FP8X4), xq_s[:, a, :]) for a in range(2)]
+        pairs_q = paired_sums(wq, wq_s, [(b, queries) for b in range(2)])
 
         def woven_over_xb(name, offset):
             return shared.tile([P, 4 * CH], BF16, name=name, offset=offset, align_bytes=64)
 
         above, below = XB_AT + WOVEN_BYTES - OVERLAP, XB_AT - WOVEN_BYTES + OVERLAP
         picked = gather_words(2 * CH, shared.tile([P, CH], U32, name="picked2", offset=XB_AT, align_bytes=ALIGN))
-        woven10 = weave(pairs10, woven_over_xb("woven_above", above))
+        woven00 = weave(pairs00, woven_over_xb("woven_above", above))
         cols.append(part_words(picked, keep.tile([P, 2, CH], U16, name="parted2", align_bytes=ALIGN)))
-        keys[1, 0] = quantised_keys(woven10)
-        keys[1, 1] = quantised_keys(weave(pairs11, woven_over_xb("woven_below", below)))
+        keys = {(0, 0): quantised_keys(woven00)}
+        keys[0, 1] = quantised_keys(weave(pairs01, woven_over_xb("woven_below", below)))
+        keys[1, 0] = quantised_keys(weave(pairs10, woven_over_xb("woven_above", above)))
         qq = keep.tile([P, 2, M], U32, name="qq", align_bytes=ALIGN)
         qq_s = keep.tile([P, 2, M], U8, name="qq_s", align_bytes=ALIGN)
-        quantise(qb[:].rearrange("p b m t -> p (b m t)"), qq[:].rearrange("p b m -> p (b m)"), qq_s[:].rearrange("p b m -> p (b m)"))
+        qb = weave(pairs_q, keep.tile([P, 4 * CH], BF16, name="qb", tag="qb", align_bytes=ALIGN))
+        quantise(qb[:], qq[:].rearrange("p b m -> p (b m)"), qq_s[:].rearrange("p b m -> p (b m)"))
 
         pairs20 = key_sums(2, 0)
-        chunk_scores(0)
+        keys[1, 1] = quantised_keys(weave(pairs11, keep.tile([P, 4 * CH], BF16, name="woven11", tag="qb", align_bytes=ALIGN)))
         values(2, 0, on_vector)
         values(2, 1, on_vector)
+        chunk_scores(0)
         picked = gather_words(3 * CH, keep.tile([P, CH], U32, name="picked3", tag="qb", align_bytes=ALIGN))
         cols.append(part_words(picked, keep.tile([P, 2, CH], U16, name="parted3", align_bytes=ALIGN)))
         keys[2, 0] = quantised_keys(weave(pairs20))
         keys[2, 1] = quantised_keys(weave(key_sums(2, 1)))
-        chunk_scores(1)
         values(2, 2, on_vector)
         values(2, 3, on_vector)
+        chunk_scores(1)
         keys[3, 0] = quantised_keys(weave(key_sums(3, 0)))
-        chunk_scores(2)
         values(3, 0, on_vector)
         values(3, 1, on_vector)
+        chunk_scores(2)
 
         pairs31 = key_sums(3, 1)
         last = [quantised_keys(weave(pairs31, hs=slice(h, h + 1))) for h in range(2)]

@@ -22,6 +22,7 @@ HALF = CH // 2
 SCORE_SCALE = 0.015625
 ALIGN = 256
 WARM_PASSES = 6
+WARM_EARLY = 4
 
 WV8_RAW_AT = 0
 XB_AT = 8192
@@ -221,9 +222,10 @@ def tile_list_kvt_qf_exp_kernel(
 
         idle = psum.tile([P, CH], F32, name="bank", tag="bank")
         for i in range(WARM_PASSES):
+            moving = late_rows[:, : 2 * CH] if i < WARM_EARLY else wk_raw[0][:, 0, :]
             nc.tensor.matmul_mx(
                 out=idle[:], lhsT=late_rows[:, : 2 * P].bitcast(FP4X4), lhsT_scale=late_rows[:, :P],
-                rhs=late_rows[:, : 2 * CH].bitcast(FP4X4), rhs_scale=late_rows[:, :CH], start=(i == 0), stop=(i == WARM_PASSES - 1),
+                rhs=moving.bitcast(FP4X4), rhs_scale=late_rows[:, :CH], start=(i == 0), stop=(i == WARM_PASSES - 1),
             )
 
         for u in range(2):

@@ -42,6 +42,10 @@ def tile_list_kvt_qf_exp_kernel(
         outs = ctx.enter_context(tc.tile_pool(name="outs", bufs=8))
         psum = ctx.enter_context(tc.psum_pool(name="psum", bufs=8))
 
+        def shifted(pool, rows, width, dtype, shift, name, **placing):
+            whole = pool.tile([P, shift + rows * width], dtype, name=name, align_bytes=ALIGN, **placing)
+            return whole[:, shift:].rearrange("p (a n) -> p a n", a=rows)
+
         def load_weight_words(words, name):
             raw = keep.tile([P, 2, words.shape[2] // 4], I32, name=name, align_bytes=ALIGN)
             nc.sync.dma_start(out=raw[:], in_=words.rearrange("a p n -> p a n").bitcast(I32))
@@ -71,7 +75,7 @@ def tile_list_kvt_qf_exp_kernel(
                 )
 
         def zeroed_planes(width, name):
-            planes = keep.tile([P, 2, width], U8, name=name, align_bytes=ALIGN)
+            planes = shifted(keep, 2, width, U8, 64, name)
             nc.vector.memset(planes[:].rearrange("p a n -> p (a n)").bitcast(I32), 0)
             return planes
 
@@ -179,8 +183,8 @@ def tile_list_kvt_qf_exp_kernel(
 
         def quantised_keys(woven):
             width = woven.shape[1] // 4
-            kq = ring.tile([P, width], U32, name="kq", bufs=7, align_bytes=ALIGN)
-            kq_s = ring.tile([P, width], U8, name="kq_s", bufs=7, align_bytes=ALIGN)
+            kq = shifted(ring, 1, width, U32, 32, "kq", bufs=7)[:, 0]
+            kq_s = shifted(ring, 1, width, U8, 64, "kq_s", bufs=7)[:, 0]
             quantise(woven[:], kq[:], kq_s[:])
             return kq, kq_s
 
@@ -230,7 +234,7 @@ def tile_list_kvt_qf_exp_kernel(
 
         for u in range(2):
             deal_words(wk_raw[0][:], wk[0][:], nc.scalar.copy, slice(2 * u, 2 * u + 2))
-        cols = [keep.tile([P, 2, CH], U16, name="parted0", align_bytes=ALIGN)]
+        cols = [shifted(keep, 2, CH, U16, 64, "parted0")]
         for h in range(2):
             picked = gather_words(h * HALF, keep.tile([P, HALF], U32, name="picked0%d" % h, tag="picked", align_bytes=ALIGN))
             for a in range(2):
@@ -238,16 +242,16 @@ def tile_list_kvt_qf_exp_kernel(
         wk.append(keep.tile([P, 512], U32, name="wk1", align_bytes=ALIGN))
         deal_words(wk_raw[1][:], wk[1][:], nc.scalar.copy)
         picked = gather_words(CH, keep.tile([P, CH], U32, name="picked1", tag="picked", align_bytes=ALIGN))
-        cols.append(part_words(picked, keep.tile([P, 2, CH], U16, name="parted1", align_bytes=ALIGN)))
+        cols.append(part_words(picked, shifted(keep, 2, CH, U16, 64, "parted1")))
         wv8b = keep.tile([P, N, 4], BF16, name="wv8b", align_bytes=ALIGN)
         nc.vector.tensor_copy(
             out=wv8b[:].rearrange("p (c i) t -> p c t i", i=4), in_=wv8_raw[:].rearrange("p t (c i) -> p c t i", i=4)
         )
-        planes_rest = shared.tile([P, 2, 2 * CH], U8, name="planes_rest", offset=WV8_RAW_AT, align_bytes=ALIGN)
+        planes_rest = shifted(shared, 2, 2 * CH, U8, 64, "planes_rest", offset=WV8_RAW_AT)
         nc.vector.memset(planes_rest[:].rearrange("p a n -> p (a n)").bitcast(I32), 0)
         col_scales.extend([planes_rest[:, a, first : first + CH] for a in range(2)] for first in (0, CH))
         wv8q = keep.tile([P, N], U32, name="wv8q", align_bytes=ALIGN)
-        wv8q_s = keep.tile([P, N], U8, name="wv8q_s", align_bytes=ALIGN)
+        wv8q_s = shifted(keep, 1, N, U8, 192, "wv8q_s")[:, 0]
         quantise(wv8b[:].rearrange("p n t -> p (n t)"), wv8q[:], wv8q_s[:])
         place(gather_scales(2 * CH, J, "wv8b")[:], planes_rest)
 
@@ -262,8 +266,8 @@ def tile_list_kvt_qf_exp_kernel(
         wq = [keep.tile([P, 512], U32, name="wq%d" % b, align_bytes=ALIGN) for b in range(2)]
         for b in range(2):
             deal_words(wq_raw[:, :, 256 * b : 256 * (b + 1)], wq[b][:])
-        xq = keep.tile([P, 2, M], U32, name="xq", align_bytes=ALIGN)
-        xq_s = keep.tile([P, 2, M], U8, name="xq_s", align_bytes=ALIGN)
+        xq = shifted(keep, 2, M, U32, 32, "xq")
+        xq_s = shifted(keep, 2, M, U8, 192, "xq_s")
         quantise(xb[:].rearrange("p a m t -> p (a m t)"), xq[:].rearrange("p a m -> p (a m)"), xq_s[:].rearrange("p a m -> p (a m)"))
         for c in range(2):
             for nt in range(4):
@@ -277,12 +281,12 @@ def tile_list_kvt_qf_exp_kernel(
         above, below = XB_AT + WOVEN_BYTES - OVERLAP, XB_AT - WOVEN_BYTES + OVERLAP
         picked = gather_words(2 * CH, shared.tile([P, CH], U32, name="picked2", offset=XB_AT, align_bytes=ALIGN))
         woven00 = weave(pairs00, woven_over_xb("woven_above", above))
-        cols.append(part_words(picked, keep.tile([P, 2, CH], U16, name="parted2", align_bytes=ALIGN)))
+        cols.append(part_words(picked, shifted(keep, 2, CH, U16, 64, "parted2")))
         keys = {(0, 0): quantised_keys(woven00)}
         keys[0, 1] = quantised_keys(weave(pairs01, woven_over_xb("woven_below", below)))
         keys[1, 0] = quantised_keys(weave(pairs10, woven_over_xb("woven_above", above)))
         qq = keep.tile([P, 2, M], U32, name="qq", align_bytes=ALIGN)
-        qq_s = keep.tile([P, 2, M], U8, name="qq_s", align_bytes=ALIGN)
+        qq_s = shifted(keep, 2, M, U8, 192, "qq_s")
         qb = weave(pairs_q, keep.tile([P, 4 * CH], BF16, name="qb", tag="qb", align_bytes=ALIGN))
         quantise(qb[:], qq[:].rearrange("p b m -> p (b m)"), qq_s[:].rearrange("p b m -> p (b m)"))
 
@@ -292,7 +296,7 @@ def tile_list_kvt_qf_exp_kernel(
         values(2, 1, on_vector)
         chunk_scores(0)
         picked = gather_words(3 * CH, keep.tile([P, CH], U32, name="picked3", tag="qb", align_bytes=ALIGN))
-        cols.append(part_words(picked, keep.tile([P, 2, CH], U16, name="parted3", align_bytes=ALIGN)))
+        cols.append(part_words(picked, shifted(keep, 2, CH, U16, 64, "parted3")))
         keys[2, 0] = quantised_keys(weave(pairs20))
         keys[2, 1] = quantised_keys(weave(key_sums(2, 1)))
         values(2, 2, on_vector)

@@ -21,8 +21,11 @@ CH = 512
 HALF = CH // 2
 SCORE_SCALE = 0.015625
 ALIGN = 256
-WARM_PASSES = 6
+MOVING_AT = 128
+PLANE_AT = 64
+OTHER_PLANE_AT = 192
 WARM_EARLY = 4
+WARM_PASSES = WARM_EARLY + 2
 
 WV8_RAW_AT = 0
 XB_AT = 8192
@@ -43,8 +46,9 @@ def tile_list_kvt_qf_exp_kernel(
         psum = ctx.enter_context(tc.psum_pool(name="psum", bufs=8))
 
         def shifted(pool, rows, width, dtype, shift, name, **placing):
-            whole = pool.tile([P, shift + rows * width], dtype, name=name, align_bytes=ALIGN, **placing)
-            return whole[:, shift:].rearrange("p (a n) -> p a n", a=rows)
+            lead = shift // {U8: 1, U16: 2, U32: 4}[dtype]
+            whole = pool.tile([P, lead + rows * width], dtype, name=name, align_bytes=ALIGN, **placing)
+            return whole[:, lead:].rearrange("p (a n) -> p a n", a=rows)
 
         def load_weight_words(words, name):
             raw = keep.tile([P, 2, words.shape[2] // 4], I32, name=name, align_bytes=ALIGN)
@@ -56,7 +60,7 @@ def tile_list_kvt_qf_exp_kernel(
             nc.sync.dma_start(out=raw[ROWS, :].bitcast(I32), in_=scales.rearrange("a q n -> q a n").bitcast(I32))
             return raw
 
-        def deal_words(raw, dst, copy=nc.vector.tensor_copy, ts=slice(0, 4)):
+        def deal_words(raw, dst, copy, ts):
             copy(
                 out=dst.rearrange("p (t a g w) -> p t a g w", a=2, t=4, g=16)[:, ts],
                 in_=raw.bitcast(U32).rearrange("p a (g t w) -> p t a g w", t=4, g=16)[:, ts],
@@ -75,7 +79,7 @@ def tile_list_kvt_qf_exp_kernel(
                 )
 
         def zeroed_planes(width, name):
-            planes = shifted(keep, 2, width, U8, 64, name)
+            planes = shifted(keep, 2, width, U8, PLANE_AT, name)
             nc.vector.memset(planes[:].rearrange("p a n -> p (a n)").bitcast(I32), 0)
             return planes
 
@@ -97,10 +101,6 @@ def tile_list_kvt_qf_exp_kernel(
 
         def quantise(grouped, codes, scales):
             nc.vector.quantize_mx(out=codes.bitcast(FP8X4), scales=scales, in_=grouped)
-
-        warm = keep.tile([P, 2], F32, name="warm")
-        nc.vector.memset(warm[:, 0:1], 0.0)
-        nc.scalar.activation(out=warm[:, 1:2], in_=warm[:, 0:1], func=EXP)
 
         offsets = keep.tile([P, J // 16], U16, name="offsets")
         nc.sync.dma_start(offsets[:], offs)
@@ -183,12 +183,12 @@ def tile_list_kvt_qf_exp_kernel(
 
         def quantised_keys(woven):
             width = woven.shape[1] // 4
-            kq = shifted(ring, 1, width, U32, 32, "kq", bufs=7)[:, 0]
-            kq_s = shifted(ring, 1, width, U8, 64, "kq_s", bufs=7)[:, 0]
+            kq = shifted(ring, 1, width, U32, MOVING_AT, "kq", bufs=7)[:, 0]
+            kq_s = shifted(ring, 1, width, U8, PLANE_AT, "kq_s", bufs=7)[:, 0]
             quantise(woven[:], kq[:], kq_s[:])
             return kq, kq_s
 
-        def values(c, nt, copy, staged=None):
+        def values(c, nt, copy):
             ns = slice(nt * P, (nt + 1) * P)
             bank = psum.tile([P, CH], F32, name="bank", tag="bank")
             nc.tensor.matmul_mx(
@@ -200,8 +200,7 @@ def tile_list_kvt_qf_exp_kernel(
                 lhsT_scale=wv4_s[:, nt // 2, (nt % 2) * P : (nt % 2 + 1) * P],
                 rhs=cols[c][:, 1, :].bitcast(FP4X4), rhs_scale=col_scales[c][1], start=False, stop=True,
             )
-            if staged is None:
-                staged = outs.tile([P, CH], F32, name="staged", tag="staged")
+            staged = outs.tile([P, CH], F32, name="staged", tag="staged")
             copy(out=staged[:], in_=bank[:])
             nc.sync.dma_start(out=out_1[ns, c * CH : (c + 1) * CH], in_=staged[:])
 
@@ -233,25 +232,25 @@ def tile_list_kvt_qf_exp_kernel(
             )
 
         for u in range(2):
-            deal_words(wk_raw[0][:], wk[0][:], nc.scalar.copy, slice(2 * u, 2 * u + 2))
-        cols = [shifted(keep, 2, CH, U16, 64, "parted0")]
+            deal_words(wk_raw[0][:], wk[0][:], on_scalar, slice(2 * u, 2 * u + 2))
+        cols = [shifted(keep, 2, CH, U16, MOVING_AT, "parted0")]
         for h in range(2):
             picked = gather_words(h * HALF, keep.tile([P, HALF], U32, name="picked0%d" % h, tag="picked", align_bytes=ALIGN))
             for a in range(2):
                 nc.vector.tensor_copy(out=cols[0][:, a, h * HALF : (h + 1) * HALF], in_=by_pass(picked)[:, a, :])
         wk.append(keep.tile([P, 512], U32, name="wk1", align_bytes=ALIGN))
-        deal_words(wk_raw[1][:], wk[1][:], nc.scalar.copy)
+        deal_words(wk_raw[1][:], wk[1][:], on_scalar, slice(0, 4))
         picked = gather_words(CH, keep.tile([P, CH], U32, name="picked1", tag="picked", align_bytes=ALIGN))
-        cols.append(part_words(picked, shifted(keep, 2, CH, U16, 64, "parted1")))
+        cols.append(part_words(picked, shifted(keep, 2, CH, U16, MOVING_AT, "parted1")))
         wv8b = keep.tile([P, N, 4], BF16, name="wv8b", align_bytes=ALIGN)
         nc.vector.tensor_copy(
             out=wv8b[:].rearrange("p (c i) t -> p c t i", i=4), in_=wv8_raw[:].rearrange("p t (c i) -> p c t i", i=4)
         )
-        planes_rest = shifted(shared, 2, 2 * CH, U8, 64, "planes_rest", offset=WV8_RAW_AT)
+        planes_rest = shifted(shared, 2, 2 * CH, U8, PLANE_AT, "planes_rest", offset=WV8_RAW_AT)
         nc.vector.memset(planes_rest[:].rearrange("p a n -> p (a n)").bitcast(I32), 0)
         col_scales.extend([planes_rest[:, a, first : first + CH] for a in range(2)] for first in (0, CH))
         wv8q = keep.tile([P, N], U32, name="wv8q", align_bytes=ALIGN)
-        wv8q_s = shifted(keep, 1, N, U8, 192, "wv8q_s")[:, 0]
+        wv8q_s = shifted(keep, 1, N, U8, OTHER_PLANE_AT, "wv8q_s")[:, 0]
         quantise(wv8b[:].rearrange("p n t -> p (n t)"), wv8q[:], wv8q_s[:])
         place(gather_scales(2 * CH, J, "wv8b")[:], planes_rest)
 
@@ -265,9 +264,9 @@ def tile_list_kvt_qf_exp_kernel(
         )
         wq = [keep.tile([P, 512], U32, name="wq%d" % b, align_bytes=ALIGN) for b in range(2)]
         for b in range(2):
-            deal_words(wq_raw[:, :, 256 * b : 256 * (b + 1)], wq[b][:])
-        xq = shifted(keep, 2, M, U32, 32, "xq")
-        xq_s = shifted(keep, 2, M, U8, 192, "xq_s")
+            deal_words(wq_raw[:, :, 256 * b : 256 * (b + 1)], wq[b][:], on_vector, slice(0, 4))
+        xq = shifted(keep, 2, M, U32, MOVING_AT, "xq")
+        xq_s = shifted(keep, 2, M, U8, OTHER_PLANE_AT, "xq_s")
         quantise(xb[:].rearrange("p a m t -> p (a m t)"), xq[:].rearrange("p a m -> p (a m)"), xq_s[:].rearrange("p a m -> p (a m)"))
         for c in range(2):
             for nt in range(4):
@@ -281,12 +280,12 @@ def tile_list_kvt_qf_exp_kernel(
         above, below = XB_AT + WOVEN_BYTES - OVERLAP, XB_AT - WOVEN_BYTES + OVERLAP
         picked = gather_words(2 * CH, shared.tile([P, CH], U32, name="picked2", offset=XB_AT, align_bytes=ALIGN))
         woven00 = weave(pairs00, woven_over_xb("woven_above", above))
-        cols.append(part_words(picked, shifted(keep, 2, CH, U16, 64, "parted2")))
+        cols.append(part_words(picked, shifted(keep, 2, CH, U16, MOVING_AT, "parted2")))
         keys = {(0, 0): quantised_keys(woven00)}
         keys[0, 1] = quantised_keys(weave(pairs01, woven_over_xb("woven_below", below)))
         keys[1, 0] = quantised_keys(weave(pairs10, woven_over_xb("woven_above", above)))
         qq = keep.tile([P, 2, M], U32, name="qq", align_bytes=ALIGN)
-        qq_s = shifted(keep, 2, M, U8, 192, "qq_s")
+        qq_s = shifted(keep, 2, M, U8, OTHER_PLANE_AT, "qq_s")
         qb = weave(pairs_q, keep.tile([P, 4 * CH], BF16, name="qb", tag="qb", align_bytes=ALIGN))
         quantise(qb[:], qq[:].rearrange("p b m -> p (b m)"), qq_s[:].rearrange("p b m -> p (b m)"))
 
@@ -296,7 +295,7 @@ def tile_list_kvt_qf_exp_kernel(
         values(2, 1, on_vector)
         chunk_scores(0)
         picked = gather_words(3 * CH, keep.tile([P, CH], U32, name="picked3", tag="qb", align_bytes=ALIGN))
-        cols.append(part_words(picked, shifted(keep, 2, CH, U16, 64, "parted3")))
+        cols.append(part_words(picked, shifted(keep, 2, CH, U16, MOVING_AT, "parted3")))
         keys[2, 0] = quantised_keys(weave(pairs20))
         keys[2, 1] = quantised_keys(weave(key_sums(2, 1)))
         values(2, 2, on_vector)

@@ -151,7 +151,7 @@ def tile_list_kvt_qf_exp_kernel(
             return dealt[b][:, 64 * u : 64 * (u + 1)].bitcast(FP4X4), dealt_s[b][:, a, P * t : P * (t + 1)]
 
         def paired_sums(weights, weight_scales, halves):
-            pairs = ring.tile([P, 2, 2, HALF, 2], BF16, name="pairs", bufs=5, align_bytes=ALIGN)
+            pairs = ring.tile([P, 2, 2, HALF, 2], BF16, name="pairs", bufs=6, align_bytes=ALIGN)
             for h, (b, moving) in enumerate(halves):
                 for u in range(2):
                     bank = psum.tile([P, 2, HALF], F32, name="bank", tag="bank")
@@ -283,24 +283,26 @@ def tile_list_kvt_qf_exp_kernel(
         cols.append(part_words(picked, shifted(keep, 2, CH, U16, MOVING_AT, "parted2")))
         keys = {(0, 0): quantised_keys(woven00)}
         keys[0, 1] = quantised_keys(weave(pairs01, woven_over_xb("woven_below", below)))
-        keys[1, 0] = quantised_keys(weave(pairs10, woven_over_xb("woven_above", above)))
         qq = keep.tile([P, 2, M], U32, name="qq", align_bytes=ALIGN)
         qq_s = shifted(keep, 2, M, U8, OTHER_PLANE_AT, "qq_s")
         qb = weave(pairs_q, keep.tile([P, 4 * CH], BF16, name="qb", tag="qb", align_bytes=ALIGN))
         quantise(qb[:], qq[:].rearrange("p b m -> p (b m)"), qq_s[:].rearrange("p b m -> p (b m)"))
 
         pairs20 = key_sums(2, 0)
-        keys[1, 1] = quantised_keys(weave(pairs11, keep.tile([P, 4 * CH], BF16, name="woven11", tag="qb", align_bytes=ALIGN)))
+        keys[1, 0] = quantised_keys(weave(pairs10, keep.tile([P, 4 * CH], BF16, name="woven10", tag="qb", align_bytes=ALIGN)))
         values(2, 0, on_vector)
         values(2, 1, on_vector)
-        chunk_scores(0)
+        pairs21 = key_sums(2, 1)
         picked = gather_words(3 * CH, keep.tile([P, CH], U32, name="picked3", tag="qb", align_bytes=ALIGN))
+        woven11 = weave(pairs11, woven_over_xb("woven_above", above))
         cols.append(part_words(picked, shifted(keep, 2, CH, U16, MOVING_AT, "parted3")))
+        keys[1, 1] = quantised_keys(woven11)
+        chunk_scores(0)
         keys[2, 0] = quantised_keys(weave(pairs20))
-        keys[2, 1] = quantised_keys(weave(key_sums(2, 1)))
         values(2, 2, on_vector)
         values(2, 3, on_vector)
         chunk_scores(1)
+        keys[2, 1] = quantised_keys(weave(pairs21))
         keys[3, 0] = quantised_keys(weave(key_sums(3, 0)))
         values(3, 0, on_vector)
         values(3, 1, on_vector)

@@ -17,6 +17,7 @@ EXP = mybir.ActivationFunctionType.Exp
 
 P = 128
 ROWS = slice(96, 128)
+OTHER_ROWS = slice(32, 64)
 CH = 512
 HALF = CH // 2
 SCORE_SCALE = 0.015625
@@ -55,9 +56,9 @@ def tile_list_kvt_qf_exp_kernel(
             nc.sync.dma_start(out=raw[:], in_=words.rearrange("a p n -> p a n").bitcast(I32))
             return raw
 
-        def load_scale_rows(scales, name):
+        def load_scale_rows(scales, rows, name):
             raw = keep.tile([P, scales.shape[2]], U8, name=name, align_bytes=ALIGN)
-            nc.sync.dma_start(out=raw[ROWS, :].bitcast(I32), in_=scales.rearrange("a q n -> q a n").bitcast(I32))
+            nc.sync.dma_start(out=raw[rows, :].bitcast(I32), in_=scales.rearrange("a q n -> q a n").bitcast(I32))
             return raw
 
         def deal_words(raw, dst, copy, ts):
@@ -69,13 +70,13 @@ def tile_list_kvt_qf_exp_kernel(
         def deal_scales(raw, dst):
             nc.vector.tensor_copy(
                 out=dst.bitcast(I32).rearrange("p (b t g w) -> p b t g w", b=2, t=4, g=16),
-                in_=raw[ROWS, :].bitcast(I32).rearrange("p (b g t w) -> p b t g w", b=2, t=4, g=16),
+                in_=raw.bitcast(I32).rearrange("p (b g t w) -> p b t g w", b=2, t=4, g=16),
             )
 
-        def place(staged, planes):
+        def place(staged, rows, planes):
             for q in (0, 2, 1, 3):
                 nc.sync.dma_start(
-                    out=planes[32 * q : 32 * q + 4].bitcast(I32), in_=staged[96 + 8 * q : 104 + 8 * q].bitcast(I32)
+                    out=planes[32 * q : 32 * q + 4].bitcast(I32), in_=staged[rows.start + 8 * q : rows.start + 8 * q + 8].bitcast(I32)
                 )
 
         def zeroed_planes(width, name):
@@ -104,14 +105,15 @@ def tile_list_kvt_qf_exp_kernel(
 
         offsets = keep.tile([P, J // 16], U16, name="offsets")
         nc.sync.dma_start(offsets[:], offs)
-        tscale = load_scale_rows(tab_scales, "tscale")
-        wk_sraw = load_scale_rows(wk_scales, "wk_sraw")
+        tscale = load_scale_rows(tab_scales, ROWS, "tscale")
         early_rows = keep.tile([P, CH + R + CH], U8, name="early_rows", align_bytes=ALIGN)
         late_rows = keep.tile([P, R + N // 2], U8, name="late_rows", align_bytes=ALIGN)
-        wq_sraw = load_scale_rows(wq_scales, "wq_sraw")
-        nc.vector.memset(late_rows[: ROWS.start, :R].bitcast(I32), 0)
+        wk_sraw = load_scale_rows(wk_scales, ROWS, "wk_sraw")
+        wq_sraw = load_scale_rows(wq_scales, OTHER_ROWS, "wq_sraw")
+        for others in (slice(0, OTHER_ROWS.start), slice(OTHER_ROWS.stop, P)):
+            nc.vector.memset(late_rows[others, :R].bitcast(I32), 0)
         nc.sync.dma_start(
-            out=late_rows[ROWS, R:].bitcast(I32),
+            out=late_rows[OTHER_ROWS, R:].bitcast(I32),
             in_=wv4_scales[0].rearrange("q (h n) -> (q h) n", h=2).bitcast(I32),
         )
         table = keep.tile([P, T], U32, name="table", align_bytes=ALIGN)
@@ -124,19 +126,19 @@ def tile_list_kvt_qf_exp_kernel(
         planes_late = zeroed_planes(R + N // 2, "planes_late")
 
         picked_first = gather_scales(0, CH, "picked_first")
-        deal_scales(wk_sraw, early_rows[ROWS, CH : CH + R])
+        deal_scales(wk_sraw[ROWS, :], early_rows[ROWS, CH : CH + R])
         nc.vector.tensor_copy(out=early_rows[ROWS, :CH].bitcast(I32), in_=picked_first[ROWS, :].bitcast(I32))
-        place(early_rows[:, : CH + R // 2], planes_first)
+        place(early_rows[:, : CH + R // 2], ROWS, planes_first)
         wk_raw.append(load_weight_words(wk_words[:, :, R:], "wk_raw1"))
-        deal_scales(wq_sraw, late_rows[ROWS, :R])
+        deal_scales(wq_sraw[OTHER_ROWS, :], late_rows[OTHER_ROWS, :R])
         picked_second = gather_scales(CH, 2 * CH, "wq_sraw")
         nc.vector.tensor_copy(out=early_rows[ROWS, CH + R :].bitcast(I32), in_=picked_second[ROWS, :].bitcast(I32))
-        place(early_rows[:, CH + R // 2 :], planes_second)
+        place(early_rows[:, CH + R // 2 :], ROWS, planes_second)
         wv8_raw = shared.tile([P, 4, N], F32, name="wv8_raw", offset=WV8_RAW_AT, align_bytes=ALIGN)
         nc.sync.dma_start(out=wv8_raw[:], in_=wv8.rearrange("(p t) n -> p t n", t=4))
         wv4 = keep.tile([P, 2 * N], U8, name="wv4", align_bytes=ALIGN)
         nc.sync.dma_start(out=wv4[:].bitcast(I32), in_=wv4_words[0].bitcast(I32))
-        place(late_rows[:], planes_late)
+        place(late_rows[:], OTHER_ROWS, planes_late)
         x_raw = shared.tile([P, 2, 4, M], F32, name="x_raw", offset=X_RAW_AT, align_bytes=ALIGN)
         nc.sync.dma_start(out=x_raw[:], in_=x.rearrange("(a p t) m -> p a t m", a=2, t=4))
         wq_raw = load_weight_words(wq_words, "wq_raw")
@@ -188,21 +190,22 @@ def tile_list_kvt_qf_exp_kernel(
             quantise(woven[:], kq[:], kq_s[:])
             return kq, kq_s
 
-        def values(c, nt, copy):
+        def values(c, nt, copy, js=slice(0, CH)):
             ns = slice(nt * P, (nt + 1) * P)
-            bank = psum.tile([P, CH], F32, name="bank", tag="bank")
+            width = js.stop - js.start
+            bank = psum.tile([P, width], F32, name="bank", tag="bank")
             nc.tensor.matmul_mx(
                 out=bank[:], lhsT=wv8q[:, ns].bitcast(FP8X4), lhsT_scale=wv8q_s[:, ns],
-                rhs=cols[c][:, 0, :].bitcast(FP4X4), rhs_scale=col_scales[c][0], start=True, stop=False,
+                rhs=cols[c][:, 0, js].bitcast(FP4X4), rhs_scale=col_scales[c][0][:, js], start=True, stop=False,
             )
             nc.tensor.matmul_mx(
                 out=bank[:], lhsT=wv4[:, 2 * nt * P : 2 * (nt + 1) * P].bitcast(FP4X4),
                 lhsT_scale=wv4_s[:, nt // 2, (nt % 2) * P : (nt % 2 + 1) * P],
-                rhs=cols[c][:, 1, :].bitcast(FP4X4), rhs_scale=col_scales[c][1], start=False, stop=True,
+                rhs=cols[c][:, 1, js].bitcast(FP4X4), rhs_scale=col_scales[c][1][:, js], start=False, stop=True,
             )
-            staged = outs.tile([P, CH], F32, name="staged", tag="staged")
+            staged = outs.tile([P, width], F32, name="staged", tag="staged")
             copy(out=staged[:], in_=bank[:])
-            nc.sync.dma_start(out=out_1[ns, c * CH : (c + 1) * CH], in_=staged[:])
+            nc.sync.dma_start(out=out_1[ns, c * CH + js.start : c * CH + js.stop], in_=staged[:])
 
         def scores(first, operands, mh):
             ms = slice(mh * P, (mh + 1) * P)
@@ -252,7 +255,7 @@ def tile_list_kvt_qf_exp_kernel(
         wv8q = keep.tile([P, N], U32, name="wv8q", align_bytes=ALIGN)
         wv8q_s = shifted(keep, 1, N, U8, OTHER_PLANE_AT, "wv8q_s")[:, 0]
         quantise(wv8b[:].rearrange("p n t -> p (n t)"), wv8q[:], wv8q_s[:])
-        place(gather_scales(2 * CH, J, "wv8b")[:], planes_rest)
+        place(gather_scales(2 * CH, J, "wv8b")[:], ROWS, planes_rest)
 
         pairs00 = key_sums(0, 0)
         pairs01 = key_sums(0, 1)
@@ -305,14 +308,28 @@ def tile_list_kvt_qf_exp_kernel(
         keys[2, 1] = quantised_keys(weave(pairs21))
         keys[3, 0] = quantised_keys(weave(key_sums(3, 0)))
         values(3, 0, on_vector)
-        values(3, 1, on_vector)
         chunk_scores(2)
+        values(3, 1, on_vector)
 
         pairs31 = key_sums(3, 1)
         last = [quantised_keys(weave(pairs31, hs=slice(h, h + 1))) for h in range(2)]
-        values(3, 2, on_scalar)
-        values(3, 3, on_vector)
-        for h in range(2):
-            js = slice(h * HALF, (h + 1) * HALF)
+        spans = [slice(h * HALF, (h + 1) * HALF) for h in range(2)]
+        operands = [[(keys[3, 0][0][:, js], keys[3, 0][1][:, js]), (last[h][0][:], last[h][1][:])] for h, js in enumerate(spans)]
+        values(3, 2, on_vector, spans[0])
+        values(3, 2, on_scalar, spans[1])
+        values(3, 3, on_scalar, spans[0])
+        for mh in range(M // P):
+            scores(3 * CH, operands[0], mh)
+        values(3, 3, on_vector, spans[1])
+        banks = [psum.tile([P, HALF], F32, name="bank", tag="bank") for mh in range(M // P)]
+        for b in range(2):
             for mh in range(M // P):
-                scores(3 * CH + h * HALF, [(keys[3, 0][0][:, js], keys[3, 0][1][:, js]), (last[h][0][:], last[h][1][:])], mh)
+                ms = slice(mh * P, (mh + 1) * P)
+                nc.tensor.matmul_mx(
+                    out=banks[mh][:], lhsT=qq[:, b, ms].bitcast(FP8X4), lhsT_scale=qq_s[:, b, ms],
+                    rhs=operands[1][b][0].bitcast(FP8X4), rhs_scale=operands[1][b][1], start=(b == 0), stop=(b == 1),
+                )
+        for mh in range(M // P):
+            staged = outs.tile([P, HALF], F32, name="staged", tag="staged")
+            nc.scalar.activation(out=staged[:], in_=banks[mh][:], func=EXP, scale=SCORE_SCALE)
+            nc.sync.dma_start(out=out_0[mh * P : (mh + 1) * P, 3 * CH + HALF :], in_=staged[:])

@@ -56,6 +56,11 @@ def tile_list_kvt_qf_exp_kernel(
             nc.sync.dma_start(out=raw[:], in_=words.rearrange("a p n -> p a n").bitcast(I32))
             return raw
 
+        def load_wv8_half(h):
+            raw = shared.tile([P, 4, N // 2], F32, name="wv8_raw%d" % h, offset=WV8_RAW_AT + 4096 * h, align_bytes=ALIGN)
+            nc.sync.dma_start(out=raw[:], in_=wv8[:, h * N // 2 : (h + 1) * N // 2].rearrange("(p t) n -> p t n", t=4))
+            return raw
+
         def load_scale_rows(scales, rows, name):
             raw = keep.tile([P, scales.shape[2]], U8, name=name, align_bytes=ALIGN)
             nc.sync.dma_start(out=raw[rows, :].bitcast(I32), in_=scales.rearrange("a q n -> q a n").bitcast(I32))
@@ -134,11 +139,11 @@ def tile_list_kvt_qf_exp_kernel(
         picked_second = gather_scales(CH, 2 * CH, "wq_sraw")
         nc.vector.tensor_copy(out=early_rows[ROWS, CH + R :].bitcast(I32), in_=picked_second[ROWS, :].bitcast(I32))
         place(early_rows[:, CH + R // 2 :], ROWS, planes_second)
-        wv8_raw = shared.tile([P, 4, N], F32, name="wv8_raw", offset=WV8_RAW_AT, align_bytes=ALIGN)
-        nc.sync.dma_start(out=wv8_raw[:], in_=wv8.rearrange("(p t) n -> p t n", t=4))
+        wv8_raw = [load_wv8_half(0)]
         wv4 = keep.tile([P, 2 * N], U8, name="wv4", align_bytes=ALIGN)
         nc.sync.dma_start(out=wv4[:].bitcast(I32), in_=wv4_words[0].bitcast(I32))
         place(late_rows[:], OTHER_ROWS, planes_late)
+        wv8_raw.append(load_wv8_half(1))
         x_raw = shared.tile([P, 2, 4, M], F32, name="x_raw", offset=X_RAW_AT, align_bytes=ALIGN)
         nc.sync.dma_start(out=x_raw[:], in_=x.rearrange("(a p t) m -> p a t m", a=2, t=4))
         wq_raw = load_weight_words(wq_words, "wq_raw")
@@ -190,7 +195,7 @@ def tile_list_kvt_qf_exp_kernel(
             quantise(woven[:], kq[:], kq_s[:])
             return kq, kq_s
 
-        def values(c, nt, copy, js=slice(0, CH)):
+        def value_sums(c, nt, js):
             ns = slice(nt * P, (nt + 1) * P)
             width = js.stop - js.start
             bank = psum.tile([P, width], F32, name="bank", tag="bank")
@@ -203,9 +208,13 @@ def tile_list_kvt_qf_exp_kernel(
                 lhsT_scale=wv4_s[:, nt // 2, (nt % 2) * P : (nt % 2 + 1) * P],
                 rhs=cols[c][:, 1, js].bitcast(FP4X4), rhs_scale=col_scales[c][1][:, js], start=False, stop=True,
             )
-            staged = outs.tile([P, width], F32, name="staged", tag="staged")
+            return bank
+
+        def values(c, nt, copy, js=slice(0, CH)):
+            bank = value_sums(c, nt, js)
+            staged = outs.tile([P, js.stop - js.start], F32, name="staged", tag="staged")
             copy(out=staged[:], in_=bank[:])
-            nc.sync.dma_start(out=out_1[ns, c * CH + js.start : c * CH + js.stop], in_=staged[:])
+            nc.sync.dma_start(out=out_1[nt * P : (nt + 1) * P, c * CH + js.start : c * CH + js.stop], in_=staged[:])
 
         def scores(first, operands, mh):
             ms = slice(mh * P, (mh + 1) * P)
@@ -245,17 +254,21 @@ def tile_list_kvt_qf_exp_kernel(
         deal_words(wk_raw[1][:], wk[1][:], on_scalar, slice(0, 4))
         picked = gather_words(CH, keep.tile([P, CH], U32, name="picked1", tag="picked", align_bytes=ALIGN))
         cols.append(part_words(picked, shifted(keep, 2, CH, U16, MOVING_AT, "parted1")))
-        wv8b = keep.tile([P, N, 4], BF16, name="wv8b", align_bytes=ALIGN)
-        nc.vector.tensor_copy(
-            out=wv8b[:].rearrange("p (c i) t -> p c t i", i=4), in_=wv8_raw[:].rearrange("p t (c i) -> p c t i", i=4)
-        )
+        wv8q = keep.tile([P, N], U32, name="wv8q", align_bytes=ALIGN)
+        wv8q_s = shifted(keep, 1, N, U8, OTHER_PLANE_AT, "wv8q_s")[:, 0]
+        wv8b = []
+        for h in range(2):
+            wv8b.append(keep.tile([P, N // 2, 4], BF16, name="wv8b%d" % h, align_bytes=ALIGN))
+            nc.vector.tensor_copy(
+                out=wv8b[h][:].rearrange("p (c i) t -> p c t i", i=4), in_=wv8_raw[h][:].rearrange("p t (c i) -> p c t i", i=4)
+            )
         planes_rest = shifted(shared, 2, 2 * CH, U8, PLANE_AT, "planes_rest", offset=WV8_RAW_AT)
         nc.vector.memset(planes_rest[:].rearrange("p a n -> p (a n)").bitcast(I32), 0)
         col_scales.extend([planes_rest[:, a, first : first + CH] for a in range(2)] for first in (0, CH))
-        wv8q = keep.tile([P, N], U32, name="wv8q", align_bytes=ALIGN)
-        wv8q_s = shifted(keep, 1, N, U8, OTHER_PLANE_AT, "wv8q_s")[:, 0]
-        quantise(wv8b[:].rearrange("p n t -> p (n t)"), wv8q[:], wv8q_s[:])
-        place(gather_scales(2 * CH, J, "wv8b")[:], ROWS, planes_rest)
+        for h in range(2):
+            ns = slice(h * N // 2, (h + 1) * N // 2)
+            quantise(wv8b[h][:].rearrange("p n t -> p (n t)"), wv8q[:, ns], wv8q_s[:, ns])
+        place(gather_scales(2 * CH, J, "wv8b0")[:], ROWS, planes_rest)
 
         pairs00 = key_sums(0, 0)
         pairs01 = key_sums(0, 1)
@@ -271,9 +284,13 @@ def tile_list_kvt_qf_exp_kernel(
         xq = shifted(keep, 2, M, U32, MOVING_AT, "xq")
         xq_s = shifted(keep, 2, M, U8, OTHER_PLANE_AT, "xq_s")
         quantise(xb[:].rearrange("p a m t -> p (a m t)"), xq[:].rearrange("p a m -> p (a m)"), xq_s[:].rearrange("p a m -> p (a m)"))
-        for c in range(2):
-            for nt in range(4):
+        for nt in range(3):
+            for c in range(2):
                 values(c, nt, on_scalar)
+        staged = outs.tile([P, 2, CH], F32, name="staged", tag="staged")
+        for c in range(2):
+            on_scalar(out=staged[:, c, :], in_=value_sums(c, 3, slice(0, CH))[:])
+        nc.sync.dma_start(out=out_1[3 * P :, : 2 * CH], in_=staged[:].rearrange("p c j -> p (c j)"))
         queries = [(xq[:, a, :].bitcast(FP8X4), xq_s[:, a, :]) for a in range(2)]
         pairs_q = paired_sums(wq, wq_s, [(b, queries) for b in range(2)])
 

from contextlib import ExitStack

import concourse.mybir as mybir

K, R, M, N, T, J = 1024, 1024, 256, 512, 4096, 2048
FLOPS = 2 * (K * R * M + K * R * J + R * M * J + K * N * J)

F32 = mybir.dt.float32
BF16 = mybir.dt.bfloat16
I32 = mybir.dt.int32
U32 = mybir.dt.uint32
U16 = mybir.dt.uint16
U8 = mybir.dt.uint8
FP8X4 = mybir.dt.float8_e4m3fn_x4
FP4X4 = mybir.dt.float4_e2m1fn_x4
EXP = mybir.ActivationFunctionType.Exp

P = 128
ROWS = slice(96, 128)
OTHER_ROWS = slice(32, 64)
CH = 512
HALF = CH // 2
SCORE_SCALE = 0.015625
ALIGN = 256
MOVING_AT = 128
PLANE_AT = 64
OTHER_PLANE_AT = 192
WARM_EARLY = 4
WARM_PASSES = WARM_EARLY + 2

WV8_RAW_AT = 0
XB_AT = 8192
X_RAW_AT = 16384
WOVEN_BYTES = 4096
OVERLAP = 64


def tile_list_kvt_qf_exp_kernel(
    tc, tab_words, tab_scales, x, wq_words, wq_scales, wk_words, wk_scales, wv8, wv4_words, wv4_scales, offs, out_0, out_1
):
    nc = tc.nc
    with ExitStack() as ctx:
        keep = ctx.enter_context(tc.tile_pool(name="keep", bufs=1))
        shared = ctx.enter_context(tc.tile_pool(name="shared", bufs=1))
        ring = ctx.enter_context(tc.tile_pool(name="ring", bufs=2))
        outs = ctx.enter_context(tc.tile_pool(name="outs", bufs=8))
        psum = ctx.enter_context(tc.psum_pool(name="psum", bufs=8))

        def shifted(pool, rows, width, dtype, shift, name, **placing):
            lead = shift // {U8: 1, U16: 2, U32: 4}[dtype]
            whole = pool.tile([P, lead + rows * width], dtype, name=name, align_bytes=ALIGN, **placing)
            return whole[:, lead:].rearrange("p (a n) -> p a n", a=rows)

        def load_weight_words(words, name):
            raw = keep.tile([P, 2, words.shape[2] // 4], I32, name=name, align_bytes=ALIGN)
            nc.sync.dma_start(out=raw[:], in_=words.rearrange("a p n -> p a n").bitcast(I32))
            return raw

        def load_wv8_half(h):
            raw = shared.tile([P, 4, N // 2], F32, name="wv8_raw%d" % h, offset=WV8_RAW_AT + 4096 * h, align_bytes=ALIGN)
            nc.sync.dma_start(out=raw[:], in_=wv8[:, h * N // 2 : (h + 1) * N // 2].rearrange("(p t) n -> p t n", t=4))
            return raw

        def load_scale_rows(scales, rows, name):
            raw = keep.tile([P, scales.shape[2]], U8, name=name, align_bytes=ALIGN)
            nc.sync.dma_start(out=raw[rows, :].bitcast(I32), in_=scales.rearrange("a q n -> q a n").bitcast(I32))
            return raw

        def deal_words(raw, dst, copy, ts):
            copy(
                out=dst.rearrange("p (t a g w) -> p t a g w", a=2, t=4, g=16)[:, ts],
                in_=raw.bitcast(U32).rearrange("p a (g t w) -> p t a g w", t=4, g=16)[:, ts],
            )

        def deal_scales(raw, dst):
            nc.vector.tensor_copy(
                out=dst.bitcast(I32).rearrange("p (b t g w) -> p b t g w", b=2, t=4, g=16),
                in_=raw.bitcast(I32).rearrange("p (b g t w) -> p b t g w", b=2, t=4, g=16),
            )

        def place(staged, rows, planes):
            for q in (0, 2, 1, 3):
                nc.sync.dma_start(
                    out=planes[32 * q : 32 * q + 4].bitcast(I32), in_=staged[rows.start + 8 * q : rows.start + 8 * q + 8].bitcast(I32)
                )

        def zeroed_planes(width, name):
            planes = shifted(keep, 2, width, U8, PLANE_AT, name)
            nc.vector.memset(planes[:].rearrange("p a n -> p (a n)").bitcast(I32), 0)
            return planes

        def gather_words(first, picked):
            nc.vector.tensor_copy(out=picked[:], in_=table[:].indirect(offsets[:, first // 16 : (first + picked.shape[1]) // 16]))
            return picked

        def by_pass(picked):
            return picked[:].bitcast(U16).rearrange("p (j a) -> p a j", a=2)

        def part_words(picked, parted):
            nc.vector.tensor_copy(out=parted[:], in_=by_pass(picked))
            return parted

        def gather_scales(j0, j1, tag):
            picked = keep.tile([P, j1 - j0], U8, name="picked_scales%d" % j0, tag=tag, align_bytes=ALIGN)
            nc.vector.tensor_copy(out=picked[:], in_=tscale[:].indirect(offsets[:, j0 // 16 : j1 // 16]))
            return picked

        def quantise(grouped, codes, scales):
            nc.vector.quantize_mx(out=codes.bitcast(FP8X4), scales=scales, in_=grouped)

        offsets = keep.tile([P, J // 16], U16, name="offsets")
        nc.sync.dma_start(offsets[:], offs)
        tscale = load_scale_rows(tab_scales, ROWS, "tscale")
        early_rows = keep.tile([P, CH + R + CH], U8, name="early_rows", align_bytes=ALIGN)
        late_rows = keep.tile([P, R + N // 2], U8, name="late_rows", align_bytes=ALIGN)
        wk_sraw = load_scale_rows(wk_scales, ROWS, "wk_sraw")
        wq_sraw = load_scale_rows(wq_scales, OTHER_ROWS, "wq_sraw")
        for others in (slice(0, OTHER_ROWS.start), slice(OTHER_ROWS.stop, P)):
            nc.vector.memset(late_rows[others, :R].bitcast(I32), 0)
        nc.sync.dma_start(
            out=late_rows[OTHER_ROWS, R:].bitcast(I32),
            in_=wv4_scales[0].rearrange("q (h n) -> (q h) n", h=2).bitcast(I32),
        )
        table = keep.tile([P, T], U32, name="table", align_bytes=ALIGN)
        nc.sync.dma_start(out=table[:].bitcast(I32), in_=tab_words[0].rearrange("p t b -> p (t b)").bitcast(I32))
        wk_raw = [load_weight_words(wk_words[:, :, :R], "wk_raw0")]

        nc.vector.memset(tscale[: ROWS.start, :].bitcast(I32), 0)
        planes_first = zeroed_planes(CH + R // 2, "planes_first")
        planes_second = zeroed_planes(R // 2 + CH, "planes_second")
        planes_late = zeroed_planes(R + N // 2, "planes_late")

        picked_first = gather_scales(0, CH, "picked_first")
        deal_scales(wk_sraw[ROWS, :], early_rows[ROWS, CH : CH + R])
        nc.vector.tensor_copy(out=early_rows[ROWS, :CH].bitcast(I32), in_=picked_first[ROWS, :].bitcast(I32))
        place(early_rows[:, : CH + R // 2], ROWS, planes_first)
        wk_raw.append(load_weight_words(wk_words[:, :, R:], "wk_raw1"))
        deal_scales(wq_sraw[OTHER_ROWS, :], late_rows[OTHER_ROWS, :R])
        picked_second = gather_scales(CH, 2 * CH, "wq_sraw")
        nc.vector.tensor_copy(out=early_rows[ROWS, CH + R :].bitcast(I32), in_=picked_second[ROWS, :].bitcast(I32))
        place(early_rows[:, CH + R // 2 :], ROWS, planes_second)
        wv8_raw = [load_wv8_half(0)]
        wv4 = keep.tile([P, 2 * N], U8, name="wv4", align_bytes=ALIGN)
        nc.sync.dma_start(out=wv4[:].bitcast(I32), in_=wv4_words[0].bitcast(I32))
        place(late_rows[:], OTHER_ROWS, planes_late)
        wv8_raw.append(load_wv8_half(1))
        x_raw = shared.tile([P, 2, 4, M], F32, name="x_raw", offset=X_RAW_AT, align_bytes=ALIGN)
        nc.sync.dma_start(out=x_raw[:], in_=x.rearrange("(a p t) m -> p a t m", a=2, t=4))
        wq_raw = load_weight_words(wq_words, "wq_raw")
        wk_s = [planes_first[:, :, CH:], planes_second[:, :, : R // 2]]
        wq_s = [planes_late[:, :, : R // 2], planes_late[:, :, R // 2 : R]]
        wv4_s = planes_late[:, :, R:]
        col_scales = [[planes[:, a, first : first + CH] for a in range(2)] for planes, first in ((planes_first, 0), (planes_second, R // 2))]
        wk = [keep.tile([P, 512], U32, name="wk0", align_bytes=ALIGN)]

        def w_tile(dealt, dealt_s, a, b, t):
            u = 2 * t + a
            return dealt[b][:, 64 * u : 64 * (u + 1)].bitcast(FP4X4), dealt_s[b][:, a, P * t : P * (t + 1)]

        def paired_sums(weights, weight_scales, halves):
            pairs = ring.tile([P, 2, 2, HALF, 2], BF16, name="pairs", bufs=6, align_bytes=ALIGN)
            for h, (b, moving) in enumerate(halves):
                for u in range(2):
                    bank = psum.tile([P, 2, HALF], F32, name="bank", tag="bank")
                    for e in range(2):
                        for a in range(2):
                            lhs, lhs_s = w_tile(weights, weight_scales, a, b, 2 * u + e)
                            nc.tensor.matmul_mx(
                                out=bank[:, e, :], lhsT=lhs, lhsT_scale=lhs_s, rhs=moving[a][0], rhs_scale=moving[a][1],
                                start=(a == 0), stop=(a == 1),
                            )
                    nc.scalar.copy(out=pairs[:, h, u], in_=bank[:].rearrange("p e j -> p j e"))
            return pairs

        def key_sums(c, b):
            spans = [slice(h * HALF, (h + 1) * HALF) for h in range(2)]
            return paired_sums(
                wk, wk_s, [(b, [(cols[c][:, a, js].bitcast(FP4X4), col_scales[c][a][:, js]) for a in range(2)]) for js in spans]
            )

        def weave(pairs, woven=None, hs=slice(0, 2)):
            count = hs.stop - hs.start
            if woven is None:
                woven = ring.tile([P, count * HALF * 4], BF16, name="woven", bufs=3, align_bytes=ALIGN)
            nc.vector.tensor_copy(
                out=woven[:].bitcast(I32).rearrange("p (h j u) -> p h j u", h=count, u=2),
                in_=pairs[:].rearrange("p h u j e -> p (h u j e)").bitcast(I32).rearrange("p (h u j) -> p h j u", h=2, u=2)[:, hs],
            )
            return woven

        def quantised_keys(woven):
            width = woven.shape[1] // 4
            kq = shifted(ring, 1, width, U32, MOVING_AT, "kq", bufs=7)[:, 0]
            kq_s = shifted(ring, 1, width, U8, PLANE_AT, "kq_s", bufs=7)[:, 0]
            quantise(woven[:], kq[:], kq_s[:])
            return kq, kq_s

        def value_sums(c, nt, js):
            ns = slice(nt * P, (nt + 1) * P)
            width = js.stop - js.start
            bank = psum.tile([P, width], F32, name="bank", tag="bank")
            nc.tensor.matmul_mx(
                out=bank[:], lhsT=wv8q[:, ns].bitcast(FP8X4), lhsT_scale=wv8q_s[:, ns],
                rhs=cols[c][:, 0, js].bitcast(FP4X4), rhs_scale=col_scales[c][0][:, js], start=True, stop=False,
            )
            nc.tensor.matmul_mx(
                out=bank[:], lhsT=wv4[:, 2 * nt * P : 2 * (nt + 1) * P].bitcast(FP4X4),
                lhsT_scale=wv4_s[:, nt // 2, (nt % 2) * P : (nt % 2 + 1) * P],
                rhs=cols[c][:, 1, js].bitcast(FP4X4), rhs_scale=col_scales[c][1][:, js], start=False, stop=True,
            )
            return bank

        def values(c, nt, copy, js=slice(0, CH)):
            bank = value_sums(c, nt, js)
            staged = outs.tile([P, js.stop - js.start], F32, name="staged", tag="staged")
            copy(out=staged[:], in_=bank[:])
            nc.sync.dma_start(out=out_1[nt * P : (nt + 1) * P, c * CH + js.start : c * CH + js.stop], in_=staged[:])

        def scores(first, operands, mh):
            ms = slice(mh * P, (mh + 1) * P)
            width = operands[0][1].shape[1]
            bank = psum.tile([P, width], F32, name="bank", tag="bank")
            for b in range(2):
                nc.tensor.matmul_mx(
                    out=bank[:], lhsT=qq[:, b, ms].bitcast(FP8X4), lhsT_scale=qq_s[:, b, ms],
                    rhs=operands[b][0].bitcast(FP8X4), rhs_scale=operands[b][1], start=(b == 0), stop=(b == 1),
                )
            staged = outs.tile([P, width], F32, name="staged", tag="staged")
            nc.scalar.activation(out=staged[:], in_=bank[:], func=EXP, scale=SCORE_SCALE)
            nc.sync.dma_start(out=out_0[ms, first : first + width], in_=staged[:])

        def chunk_scores(c):
            for mh in range(M // P):
                scores(c * CH, [(kq[:], kq_s[:]) for kq, kq_s in (keys[c, 0], keys[c, 1])], mh)

        on_scalar, on_vector = nc.scalar.copy, nc.vector.tensor_copy

        idle = psum.tile([P, CH], F32, name="bank", tag="bank")
        for i in range(WARM_PASSES):
            moving = late_rows[:, : 2 * CH] if i < WARM_EARLY else wk_raw[0][:, 0, :]
            nc.tensor.matmul_mx(
                out=idle[:], lhsT=late_rows[:, : 2 * P].bitcast(FP4X4), lhsT_scale=late_rows[:, :P],
                rhs=moving.bitcast(FP4X4), rhs_scale=late_rows[:, :CH], start=(i == 0), stop=(i == WARM_PASSES - 1),
            )

        for u in range(2):
            deal_words(wk_raw[0][:], wk[0][:], on_scalar, slice(2 * u, 2 * u + 2))
        cols = [shifted(keep, 2, CH, U16, MOVING_AT, "parted0")]
        for h in range(2):
            picked = gather_words(h * HALF, keep.tile([P, HALF], U32, name="picked0%d" % h, tag="picked", align_bytes=ALIGN))
            for a in range(2):
                nc.vector.tensor_copy(out=cols[0][:, a, h * HALF : (h + 1) * HALF], in_=by_pass(picked)[:, a, :])
        wk.append(keep.tile([P, 512], U32, name="wk1", align_bytes=ALIGN))
        deal_words(wk_raw[1][:], wk[1][:], on_scalar, slice(0, 4))
        picked = gather_words(CH, keep.tile([P, CH], U32, name="picked1", tag="picked", align_bytes=ALIGN))
        cols.append(part_words(picked, shifted(keep, 2, CH, U16, MOVING_AT, "parted1")))
        wv8q = keep.tile([P, N], U32, name="wv8q", align_bytes=ALIGN)
        wv8q_s = shifted(keep, 1, N, U8, OTHER_PLANE_AT, "wv8q_s")[:, 0]
        wv8b = []
        for h in range(2):
            wv8b.append(keep.tile([P, N // 2, 4], BF16, name="wv8b%d" % h, align_bytes=ALIGN))
            nc.vector.tensor_copy(
                out=wv8b[h][:].rearrange("p (c i) t -> p c t i", i=4), in_=wv8_raw[h][:].rearrange("p t (c i) -> p c t i", i=4)
            )
        planes_rest = shifted(shared, 2, 2 * CH, U8, PLANE_AT, "planes_rest", offset=WV8_RAW_AT)
        nc.vector.memset(planes_rest[:].rearrange("p a n -> p (a n)").bitcast(I32), 0)
        col_scales.extend([planes_rest[:, a, first : first + CH] for a in range(2)] for first in (0, CH))
        for h in range(2):
            ns = slice(h * N // 2, (h + 1) * N // 2)
            quantise(wv8b[h][:].rearrange("p n t -> p (n t)"), wv8q[:, ns], wv8q_s[:, ns])
        place(gather_scales(2 * CH, J, "wv8b0")[:], ROWS, planes_rest)

        pairs00 = key_sums(0, 0)
        pairs01 = key_sums(0, 1)
        pairs10 = key_sums(1, 0)
        pairs11 = key_sums(1, 1)
        xb = shared.tile([P, 2, M, 4], BF16, name="xb", offset=XB_AT, align_bytes=ALIGN)
        nc.vector.tensor_copy(
            out=xb[:].rearrange("p a (c i) t -> p a c t i", i=4), in_=x_raw[:].rearrange("p a t (c i) -> p a c t i", i=4)
        )
        wq = [keep.tile([P, 512], U32, name="wq%d" % b, align_bytes=ALIGN) for b in range(2)]
        for b in range(2):
            deal_words(wq_raw[:, :, 256 * b : 256 * (b + 1)], wq[b][:], on_vector, slice(0, 4))
        xq = shifted(keep, 2, M, U32, MOVING_AT, "xq")
        xq_s = shifted(keep, 2, M, U8, OTHER_PLANE_AT, "xq_s")
        quantise(xb[:].rearrange("p a m t -> p (a m t)"), xq[:].rearrange("p a m -> p (a m)"), xq_s[:].rearrange("p a m -> p (a m)"))
        for nt in range(3):
            for c in range(2):
                values(c, nt, on_scalar)
        staged = outs.tile([P, 2, CH], F32, name="staged", tag="staged")
        for c in range(2):
            on_scalar(out=staged[:, c, :], in_=value_sums(c, 3, slice(0, CH))[:])
        nc.sync.dma_start(out=out_1[3 * P :, : 2 * CH], in_=staged[:].rearrange("p c j -> p (c j)"))
        queries = [(xq[:, a, :].bitcast(FP8X4), xq_s[:, a, :]) for a in range(2)]
        pairs_q = paired_sums(wq, wq_s, [(b, queries) for b in range(2)])

        def woven_over_xb(name, offset):
            return shared.tile([P, 4 * CH], BF16, name=name, offset=offset, align_bytes=64)

        above, below = XB_AT + WOVEN_BYTES - OVERLAP, XB_AT - WOVEN_BYTES + OVERLAP
        picked = gather_words(2 * CH, shared.tile([P, CH], U32, name="picked2", offset=XB_AT, align_bytes=ALIGN))
        woven00 = weave(pairs00, woven_over_xb("woven_above", above))
        cols.append(part_words(picked, shifted(keep, 2, CH, U16, MOVING_AT, "parted2")))
        keys = {(0, 0): quantised_keys(woven00)}
        keys[0, 1] = quantised_keys(weave(pairs01, woven_over_xb("woven_below", below)))
        qq = keep.tile([P, 2, M], U32, name="qq", align_bytes=ALIGN)
        qq_s = shifted(keep, 2, M, U8, OTHER_PLANE_AT, "qq_s")
        qb = weave(pairs_q, keep.tile([P, 4 * CH], BF16, name="qb", tag="qb", align_bytes=ALIGN))
        quantise(qb[:], qq[:].rearrange("p b m -> p (b m)"), qq_s[:].rearrange("p b m -> p (b m)"))

        pairs20 = key_sums(2, 0)
        keys[1, 0] = quantised_keys(weave(pairs10, keep.tile([P, 4 * CH], BF16, name="woven10", tag="qb", align_bytes=ALIGN)))
        values(2, 0, on_vector)
        values(2, 1, on_vector)
        pairs21 = key_sums(2, 1)
        picked = gather_words(3 * CH, keep.tile([P, CH], U32, name="picked3", tag="qb", align_bytes=ALIGN))
        woven11 = weave(pairs11, woven_over_xb("woven_above", above))
        cols.append(part_words(picked, shifted(keep, 2, CH, U16, MOVING_AT, "parted3")))
        keys[1, 1] = quantised_keys(woven11)
        chunk_scores(0)
        keys[2, 0] = quantised_keys(weave(pairs20))
        values(2, 2, on_vector)
        values(2, 3, on_vector)
        chunk_scores(1)
        keys[2, 1] = quantised_keys(weave(pairs21))
        keys[3, 0] = quantised_keys(weave(key_sums(3, 0)))
        values(3, 0, on_vector)
        chunk_scores(2)
        values(3, 1, on_vector)

        pairs31 = key_sums(3, 1)
        last = [quantised_keys(weave(pairs31, hs=slice(h, h + 1))) for h in range(2)]
        spans = [slice(h * HALF, (h + 1) * HALF) for h in range(2)]
        operands = [[(keys[3, 0][0][:, js], keys[3, 0][1][:, js]), (last[h][0][:], last[h][1][:])] for h, js in enumerate(spans)]
        values(3, 2, on_vector, spans[0])
        values(3, 2, on_scalar, spans[1])
        values(3, 3, on_scalar, spans[0])
        for mh in range(M // P):
            scores(3 * CH, operands[0], mh)
        values(3, 3, on_vector, spans[1])
        banks = [psum.tile([P, HALF], F32, name="bank", tag="bank") for mh in range(M // P)]
        for b in range(2):
            for mh in range(M // P):
                ms = slice(mh * P, (mh + 1) * P)
                nc.tensor.matmul_mx(
                    out=banks[mh][:], lhsT=qq[:, b, ms].bitcast(FP8X4), lhsT_scale=qq_s[:, b, ms],
                    rhs=operands[1][b][0].bitcast(FP8X4), rhs_scale=operands[1][b][1], start=(b == 0), stop=(b == 1),
                )
        for mh in range(M // P):
            staged = outs.tile([P, HALF], F32, name="staged", tag="staged")
            nc.scalar.activation(out=staged[:], in_=banks[mh][:], func=EXP, scale=SCORE_SCALE)
            nc.sync.dma_start(out=out_0[mh * P : (mh + 1) * P, 3 * CH + HALF :], in_=staged[:])
